import numpy as np, ml_dtypes
CORES = [16,17,18,19,32,33,34,35]
N = 8
BF = ml_dtypes.bfloat16
W, A, S, CAP, RO = 4096, 256, 1, 64, 3
P, BL = A // S, W // CAP
WT = 2 * np.arange(16) + 1
def counts(rng, fat):
    return np.where(fat, rng.integers(9, 17, fat.shape), rng.integers(0, 9, fat.shape))
def cols(rng, n, top):
    on = np.argsort(rng.random((N, 8, 16, W)), axis=2) < n[:, :, None, :]
    return np.where(on, 1 + (top * rng.random((N, 8, 16, W))).astype(np.int64), 0)
def lines(rng, fat, share):
    o = np.argsort(np.where(fat, 0.0, 1.0) + 0.5 * rng.random((N, 8, W)), axis=-1); nf = np.add.reduce(fat.astype(np.int64), axis=-1)[:, :, None, None]
    v = rng.random((N, 8, 16, A))
    k = np.where(rng.random((N, 8, 16, A)) < share, (v * nf).astype(np.int64), nf + (v * (W - nf)).astype(np.int64))
    return np.take_along_axis(o, k.reshape(N, 8, 16 * A), 2).reshape(N, 8, 16, A)
def hop(e, u):
    return (((e * u) >> 5) + e) & (W - 1)
def first(X):
    u = np.add.reduce(X * WT.reshape(1, 1, 16, 1), axis=2) & (W - 1); h = hop(np.arange(W).reshape(1, 1, W), u)
    y = np.take_along_axis(X, h[:, :, None, :], 3)
    return np.add.reduce(np.sign(y - X), axis=2), np.add.reduce((X > 0).astype(np.int64), axis=2)
def top16(s):
    v = np.full(16, 255); d = (65280 - s) & (W - 1)
    for w in range(15, -1, -1):
        c = min(254, d // (2 * w + 1)); v[w] -= c; d -= c * (2 * w + 1)
    return v
def pack(X, E, M):
    return {"xt": X.reshape(N, 128, W).astype(np.float32).astype(BF), "led": E.reshape(N, 128, A).astype(np.int32), "mk": M.reshape(N, 128, A).astype(np.float32).astype(BF)}
def setup_inputs(rng):
    fat = rng.random((N, 8, W)) < rng.choice(np.array([0.3, 0.5, 0.7]), (N, 8, 1))
    X = cols(rng, counts(rng, fat), 255)
    share = rng.choice(np.array([0.01, 0.05, 0.15, 0.6]), (N, 8, 1, A)) * rng.choice(np.array([0.2, 1.0, 1.5]), (N, 8, 1, 1))
    return pack(X, lines(rng, fat, share), rng.integers(0, 2, (N, 8, 16, A)))
def setup_inputs_spread(rng):
    fat = rng.random((N, 8, W)) < rng.choice(np.array([0.2, 0.5, 0.8]), (N, 8, 1))
    top = np.minimum(np.exp2(8 * rng.random((N, 8, 1, W))).astype(np.int64), 255)
    X = cols(rng, counts(rng, fat), top)
    E = lines(rng, fat, rng.choice(np.array([0.01, 0.05, 0.2, 0.7]), (N, 8, 1, A)))
    low = (W * rng.random((N, 8, 16, A)) ** 4).astype(np.int64); E = np.where(rng.random((N, 8, 1, A)) < 0.25, low, E)
    return pack(X, E, (rng.random((N, 8, 16, A)) < rng.random((N, 8, 1, A))).astype(np.int64))
def setup_inputs_ends(rng):
    kind = rng.integers(0, 3, (N, 8, 1, W))
    X = np.where(kind == 0, 0, np.where(kind == 1, 255, 255 * rng.integers(0, 2, (N, 8, 16, W))))
    X[..., 1] = 1; X[..., hop(1, 256)] = 255
    X[..., 2] = 255; X[..., hop(2, 65280 & (W - 1))] = 0
    X[..., W - 2] = 254; X[..., hop(W - 2, 65024 & (W - 1))] = 255
    X[..., W - 1] = top16(W - 1); X[..., hop(W - 1, W - 1)] = 0
    sh = (N, 8, 16, A)
    other = np.where(rng.random(sh) < 0.5, rng.choice(np.array([1, 2, W - 2]), sh), rng.integers(0, W, sh))
    E = np.where(rng.random(sh) < 0.7, (W - 1) * rng.integers(0, 2, sh), other)
    M = (rng.random(sh) < rng.choice(np.array([0.0, 0.5, 1.0]), (N, 8, 1, A))).astype(np.int64)
    i = np.arange(P) * S; q = N - 1
    for r in (0, q):
        for g in range(8):
            k = 2 * rng.integers(0, 8, P); E[r, g, k, i] = W - 1; M[r, g, k, i] = 1
    E[1, 0, :, 0::S] = 0; M[1, 0, :, 0::S] = 0
    E[q, 0, :, 0] = 0; M[q, 0, :, 0] = 0
    a, b, c, d = int(i[CAP - 1]), int(i[P - 1]), int(i[P - 2]), int(i[3])
    E[q, 7, :, a] = W - 1; M[q, 7, :, a] = 1
    E[q, 7, :, b] = 0; M[q, 7, :, b] = 0; E[q, 7, 14:, b] = W - 1; M[q, 7, 14:, b] = 1
    E[q, 7, :, c] = 0; M[q, 7, :, c] = 0; E[q, 7, 14, c] = W - 2; M[q, 7, 14, c] = 1; E[q, 7, 15, c] = 1
    E[:, 7, 0::2, d] = 2; M[:, 7, 0::2, d] = 1; E[:, 7, 1::2, d] = W - 1; M[:, 7, 1::2, d] = 0
    return pack(X, E, M)
def setup_inputs_corners(rng):
    fat = rng.random((N, 8, W)) < 0.5; X = cols(rng, counts(rng, fat), 255)
    E = lines(rng, fat, 0.1); M = rng.integers(0, 2, (N, 8, 16, A)); g, n = first(X)
    room = (0, 1, CAP - 1, CAP, CAP + 1, P, CAP, P - 1); even = np.arange(16)[:, None] % 2 == 0
    for q in range(N):
        for b in range(8):
            gg = g[q, b]; hot = np.flatnonzero((n[q, b] >= 9) & (gg != 0)); thin = np.flatnonzero(n[q, b] <= 8)
            c = int(rng.choice(np.array(room)))
            if q == 0: c = room[b]
            if q == N - 1: c = room[(b + 4) % 8]
            o = np.concatenate([np.array([P - 1]), rng.permutation(P - 1)]); yes = o[:c]; z = np.zeros((1, P), bool); z[0, o[c:]] = True
            e = np.where(rng.random((16, P)) < 0.2, (W - 1) * rng.integers(0, 2, (16, P)), rng.integers(0, W, (16, P)))
            m = (rng.random((16, P)) < rng.choice(np.array([0.0, 0.5, 1.0]), (1, P))).astype(np.int64)
            ge = gg[e]; m = np.where(even & z & (ge != 0), (ge > 0).astype(np.int64), m)
            e = np.where(~even & z, rng.choice(thin, (16, P)), e)
            k = 2 * rng.integers(0, 8, c); hh = rng.choice(hot, c); e[k, yes] = hh; m[k, yes] = (gg[hh] < 0).astype(np.int64)
            E[q, b, :, 0::S] = e; M[q, b, :, 0::S] = m
    return pack(X, E, M)
def setup_inputs_ties(rng):
    fat = rng.random((N, 8, W)) < 0.5
    n = np.where(fat, np.where(rng.random((N, 8, W)) < 0.8, 9, 16), 8); X = cols(rng, n, rng.choice(np.array([1, 2, 3]), (N, 8, 1, W)))
    E = lines(rng, fat, rng.choice(np.array([0.02, 0.2, 0.5]), (N, 8, 1, A)))
    E = np.take_along_axis(E, rng.integers(0, 3, (N, 8, 16, A)), 2)
    return pack(X, E, (rng.random((N, 8, 16, A)) < rng.choice(np.array([0.1, 0.5, 0.9]), (N, 8, 1, A))).astype(np.int64))
def setup_inputs_deep(rng):
    fat = rng.random((N, 8, W)) < 0.5; X = cols(rng, counts(rng, fat), 255)
    X[..., 0] = 0
    X[..., 3] = 253; X[..., hop(3, 64768 & (W - 1))] = 255
    X[..., 5] = 252; X[..., hop(5, 64512 & (W - 1))] = 255
    X[..., 7] = 255; X[..., hop(7, 65280 & (W - 1))] = 255; X[..., hop(7, 62976 & (W - 1))] = 255
    X[..., 11] = W >> 8
    X[..., W - 3] = top16(W - 21); X[..., hop(W - 3, W - 21)] = 0; X[..., hop(W - 3, W - 21) + 1] = 255
    X[..., 1001] = 255; X[..., 0, 1001] = 254; X[..., hop(1001, 65279 & (W - 1))] = 0
    X[..., 13] = 0; X[..., 7:, 13] = 255; X[..., hop(13, 52785 & (W - 1))] = 0
    X[..., 17] = 0; X[..., :9, 17] = 255; X[..., hop(17, 20655 & (W - 1))] = 0
    E = lines(rng, fat, 0.1); M = rng.integers(0, 2, (N, 8, 16, A)); s, n = first(X)
    h = hop(np.arange(W).reshape(1, 1, W), np.add.reduce(X * WT.reshape(1, 1, 16, 1), axis=2) & (W - 1))
    kind = np.argsort(rng.random((N, 8, P)), axis=-1) % 7
    for q in range(N):
        for b in range(8):
            if b in (1, 6):
                far = np.arange(W) >= (W >> 2); nn = n[q, b]; hh = h[q, b]
                thin = np.flatnonzero((nn <= 8) & far); hot = np.flatnonzero((nn >= 9) & (s[q, b] < 0) & (nn[hh] <= 8) & far[hh])
                E[q, b] = rng.choice(thin, (16, A))
                c = int(rng.integers(CAP >> 3, (CAP >> 2) + 1)); i = S * rng.permutation(P)[:c]; k = 2 * rng.integers(0, 8, c)
                E[q, b, k, i] = rng.choice(hot, c); M[q, b, k, i] = 1
                continue
            for v in range(1, 7):
                i = S * np.flatnonzero(kind[q, b] == v); k = 2 * rng.integers(0, 8, len(i))
                E[q, b, :, i] = 0; M[q, b, :, i] = 0
                if v == 1:
                    for w, e, m in ((0, 3, 1), (2, 3, 1), (4, 3, 1), (6, 5, 1), (7, 7, 1), (8, 7, 0), (9, 7, 1), (10, 7, 0), (11, 7, 1), (12, 7, 0), (13, 7, 0), (14, 7, 0)):
                        E[q, b, w, i] = e; M[q, b, w, i] = m
                elif v == 2:
                    E[q, b, k, i] = W - 3; M[q, b, k, i] = 1
                elif v == 3:
                    E[q, b, k, i] = 11; M[q, b, k, i] = 1; E[q, b, k + 1, i] = 7
                else:
                    E[q, b, k, i] = (1001, 13, 17)[v - 4]; M[q, b, k, i] = 1
    return pack(X, E, M)
def check_inputs(d):
    bad = []
    for k, lo, hi in (("xt", 0, 255), ("led", 0, W - 1), ("mk", 0, 1)):
        v = np.asarray(d[k]).astype(np.float64)
        if np.min(v) < lo or np.max(v) > hi or np.any(v != np.floor(v)): bad.append("range of " + k)
    return bad
def look(X, ix):
    return np.take_along_axis(X, ix.reshape(N, 8, 1, 16 * P), 3).reshape(N, 8, 16, 16, P)
def reference(xt, led, mk):
    X = xt.astype(np.float32).astype(np.int64).reshape(N, 8, 16, W)
    E = led.astype(np.int64).reshape(N, 8, 16, A); M = mk.astype(np.float32).astype(np.int64).reshape(N, 8, 16, A)
    kappa = np.zeros((N, 1, 1, 1), np.int64); ks = np.arange(16).reshape(1, 1, 16, 1)
    for t in range(RO):
        c = t % S; e = E[:, :, :, c::S].copy(); m = M[:, :, :, c::S].copy()
        x = look(X, e); q = x.copy(); b = np.zeros((N, 8, 16, P), np.int64)
        for k in range(16):
            mm = m[:, :, k][:, :, None, :]
            if k % 2 == 0: b = b + mm * x[:, :, :, k]
            else:
                q[:, :, :, k] = np.minimum(b, x[:, :, :, k]); b = b - mm * q[:, :, :, k]
        u = np.add.reduce(WT.reshape(1, 1, 16, 1, 1) * q, axis=2) & (W - 1)
        h = (((e * u) >> 5) + e + kappa) & (W - 1)
        g = np.add.reduce(np.sign(look(X, h) - q), axis=2); over = np.add.reduce((q > 0).astype(np.int64), axis=2)
        con = (over >= 9) & (((m == 1) & (g < 0)) | ((m == 0) & (g > 0)))
        best = np.argmax(np.where(con, np.abs(g), 0), axis=2)
        flip = np.any(con, axis=2)
        win = flip[:, :, None, :] & (ks == best[:, :, None, :])
        E[:, :, :, c::S] = np.where(win, h, e); M[:, :, :, c::S] = np.where(win, 1 - m, m)
        f = flip.astype(np.int64); kappa = (np.add.reduce(f.reshape(N, 8 * P), axis=1) & 31).reshape(N, 1, 1, 1)
        place = np.add.accumulate(f, axis=2) - 1; go = flip & (place < CAP)
        qb = np.take_along_axis(q, best[:, :, None, None, :], 3)[:, :, :, 0]; ub = np.take_along_axis(u, best[:, :, None, :], 2)[:, :, 0]
        new = X.copy()
        for r in range(N):
            d = (r + 1 + t % (N - 1)) % N
            for v in range(8):
                i = np.flatnonzero(go[r, v]); col = BL * place[r, v, i] + (ub[r, v, i] & (BL - 1))
                new[d, v][:, col] = (X[d, v][:, col] + qb[r, v][:, i]) >> 1
        X = new
    return {"yx": X.reshape(N, 128, W).astype(np.float32).astype(BF), "yl": E.reshape(N, 128, A).astype(np.float32), "ym": M.reshape(N, 128, A).astype(np.float32).astype(BF)}

@@ -1,0 +1,580 @@
+import numpy as np
+from concourse.mybir import AluOpType as ALU, AxisListType, ActivationFunctionType as ACT
+
+NX, NOFF, ZC, C15, TRO, WEND = 4096, 4096, 8192, 8193, 8208, 16400
+GW = 8208
+NENG = 8
+
+SCRATCH = {
+    "XT": ("sbuf", [128, WEND], "bfloat16"),
+    "ledI": ("sbuf", [128, 256], "int32"),
+    "E": ("sbuf", [128, 256], "float32"),
+    "Ek": ("sbuf", [128, 256], "float32"),
+    "mB": ("sbuf", [128, 256], "bfloat16"),
+    "sg": ("sbuf", [128, 256], "bfloat16"),
+    "LA": ("sbuf", [128, 256], "uint16"),
+    "LB": ("sbuf", [128, 256], "uint16"),
+    "LY": ("sbuf", [128, 256], "uint16"),
+    "tE": ("sbuf", [128, 256], "float32"),
+    "tM": ("sbuf", [128, 256], "float32"),
+    "dh": ("sbuf", [128, 256], "float32"),
+    "wE": ("sbuf", [128, 256], "float32"),
+    "wM": ("sbuf", [128, 256], "bfloat16"),
+    "Ab": ("sbuf", [128, 4096], "bfloat16"),
+    "Bb": ("sbuf", [128, 4096], "bfloat16"),
+    "bb": ("sbuf", [128, 4096 + 32], "bfloat16"),
+    "Qb": ("sbuf", [128, 4096 + 16], "bfloat16"),
+    "zb": ("sbuf", [128, 4096], "bfloat16"),
+    "sb": ("sbuf", [128, 4096], "bfloat16"),
+    "pb": ("sbuf", [128, 4096], "bfloat16"),
+    "zero": ("sbuf", [128, 1024], "bfloat16"),
+    "uI": ("sbuf", [128, 256], "int32"),
+    "uA": ("sbuf", [128, 256], "int32"),
+    "eu": ("sbuf", [128, 256], "int32"),
+    "wv": ("sbuf", [128, 256], "int32"),
+    "hs": ("sbuf", [128, 256], "int32"),
+    "hI": ("sbuf", [128, 256], "int32"),
+    "ov": ("sbuf", [128, 256], "bfloat16"),
+    "gov": ("sbuf", [128, 256], "bfloat16"),
+    "comp": ("sbuf", [128, 256], "float32"),
+    "R1": ("sbuf", [128, 256], "float32"),
+    "R2": ("sbuf", [128, 256], "float32"),
+    "win": ("sbuf", [128, 256], "bfloat16"),
+    "flipX": ("sbuf", [128, 256], "bfloat16"),
+    "wsb": ("sbuf", [128, 256], "bfloat16"),
+    "D": ("sbuf", [128, 1024], "float16"),
+    "LJ": ("sbuf", [128, 4], "uint16"),
+    "kr": ("sbuf", [128, 1], "float32"),
+    "kri": ("sbuf", [128, 1], "int32"),
+    "krm": ("sbuf", [128, 1], "int32"),
+    "kap": ("sbuf", [128, 1], "float32"),
+    "qs0": ("sbuf", [128, 64], "bfloat16"),
+    "qs1": ("sbuf", [128, 64], "bfloat16"),
+    "qs2": ("sbuf", [128, 64], "bfloat16"),
+    "land0": ("sbuf", [128, 64], "bfloat16"),
+    "land1": ("sbuf", [128, 64], "bfloat16"),
+    "land2": ("sbuf", [128, 64], "bfloat16"),
+    "vi": ("sbuf", [128, 4], "int32"),
+    "vm": ("sbuf", [128, 4], "int32"),
+    "vinv": ("sbuf", [128, 4], "float32"),
+    "vbs": ("sbuf", [128, 4], "float32"),
+    "vid": ("sbuf", [128, 4], "float32"),
+    "LI": ("sbuf", [128, 8], "uint16"),
+    "tx": ("sbuf", [128, 64], "float32"),
+    "ND": ("sbuf", [128, 128], "int32"),
+    "pI": ("sbuf", [128, 1], "int32"),
+    "kI": ("sbuf", [128, 1], "int32"),
+    "parI": ("sbuf", [128, 1], "int32"),
+    "kcol": ("sbuf", [128, 1], "float32"),
+    "sgn": ("sbuf", [128, 1], "float32"),
+    "offY": ("sbuf", [128, 1], "float32"),
+    "oB": ("sbuf", [128, 1], "float32"),
+    "s2c": ("sbuf", [128, 1], "float32"),
+    "s3c": ("sbuf", [128, 1], "float32"),
+    "wcol": ("sbuf", [128, 1], "float32"),
+    "w256": ("sbuf", [128, 1], "float32"),
+    "k64": ("sbuf", [128, 1], "float32"),
+    "i8": ("sbuf", [128, 8], "int32"),
+    "i8s": ("sbuf", [128, 8], "int32"),
+    "blkO": ("sbuf", [128, 8], "bfloat16"),
+    "blkE": ("sbuf", [128, 8], "bfloat16"),
+    "wb8": ("sbuf", [128, 8], "float32"),
+    "iD": ("sbuf", [128, 128], "int32"),
+    "iG": ("sbuf", [128, 128], "int32"),
+    "iGs": ("sbuf", [128, 128], "int32"),
+    "iR": ("sbuf", [128, 128], "int32"),
+    "iB": ("sbuf", [128, 4], "int32"),
+    "iC": ("sbuf", [128, 4], "int32"),
+    "ident": ("sbuf", [128, 128], "bfloat16"),
+    "tri": ("sbuf", [128, 128], "bfloat16"),
+    "all16": ("sbuf", [128, 128], "bfloat16"),
+    "ones": ("sbuf", [128, 128], "bfloat16"),
+    "onesh": ("sbuf", [128, 128], "float16"),
+    "kmat": ("sbuf", [128, 128], "bfloat16"),
+    "Pd": ("sbuf", [128, 128], "bfloat16"),
+    "crow": ("sbuf", [128, 128], "bfloat16"),
+    "Ct": ("sbuf", [128, 128], "float32"),
+    "base": ("sbuf", [128, 4], "float32"),
+    "jc": ("sbuf", [128, 4], "float16"),
+    "ecb": ("sbuf", [128, 16], "bfloat16"),
+    "ec": ("sbuf", [128, 16], "float16"),
+    "sel": ("sbuf", [128, 2048], "bfloat16"),
+    "pU0": ("psum", [128, 512], "float32"),
+    "pU1": ("psum", [128, 512], "float32"),
+    "pOV": ("psum", [128, 512], "float32"),
+    "pS": ("psum", [128, 512], "float32"),
+    "pGK": ("psum", [128, 512], "float32"),
+    "pWN": ("psum", [128, 512], "float32"),
+    "pZ": ("psum", [128, 512], "float32"),
+    "pSM": ("psum", [128, 512], "float32"),
+}
+SEMAPHORES = (["cV", "cS", "cP", "cG", "sent"] + ["arr%d" % t for t in range(3)] + ["d%d" % i for i in range(24)])
+
+
+def rank_program(g, core, T, topo):
+    rank = T.rank_of(core)
+    if rank is None:
+        return
+    n_ranks = len(T.cores)
+    rounds = 3
+    V, S, P = g.vector, g.scalar, g.tensor
+    Q = {"V": V, "S": S, "P": P, "G": g, "Y": g.sync}
+    count = {}
+    known = {q: {} for q in Q}
+    lastw, readers, banks = {}, {}, {}
+    seq, nd = [0], [0]
+
+    def depends(q, R, W, B):
+        toks = []
+        for t in R:
+            if t in lastw:
+                toks.append(lastw[t])
+        for t in W:
+            if t in lastw:
+                toks.append(lastw[t])
+            toks += [x for x in readers.get(t, []) if x[2] != q]
+        for b in B:
+            toks += [x for qq, x in banks.get(b, {}).items() if qq != q]
+        for sem, val, _, snap, _ in sorted(toks, key=lambda x: -x[4]):
+            k = known[q]
+            if k.get(sem, 0) >= val:
+                continue
+            Q[q].wait_ge(T.sem[sem], val)
+            for s, v in snap.items():
+                if k.get(s, 0) < v:
+                    k[s] = v
+            k[sem] = max(k.get(sem, 0), val)
+
+    def note(q, sem, n, R, W, B, snap):
+        count[sem] = count.get(sem, 0) + n
+        seq[0] += 1
+        tok = (sem, count[sem], q, snap, seq[0])
+        for t in R:
+            readers.setdefault(t, []).append(tok)
+        for t in W:
+            lastw[t] = tok
+            readers[t] = []
+        for b in B:
+            banks.setdefault(b, {})[q] = tok
+
+    def op(q, f, R, W, B=()):
+        depends(q, R, W, B)
+        f().then_inc(T.sem["c" + q], 1)
+        note(q, "c" + q, 1, R, W, B, dict(known[q]))
+
+    def dma(q, out, in_, R, W):
+        depends(q, R, W, ())
+        sem = "d%d" % nd[0]
+        nd[0] += 1
+        Q[q].dma_start(out, in_).then_inc(T.sem[sem], 16)
+        note(q, sem, 16, R, W, (), dict(known[q]))
+
+    def vts(out, in0, s1, o0, s2, o1, R, W, B=()):
+        if o1 is None:
+            op("V", lambda: V.tensor_scalar(out, in0, s1, None, o0), R, W, B)
+        else:
+            op("V", lambda: V.tensor_scalar(out, in0, s1, s2, o0, o1), R, W, B)
+
+    def vtt(out, a, b, o, R, W, B=()):
+        op("V", lambda: V.tensor_tensor(out, a, b, o), R, W, B)
+
+    def vcp(out, in_, R, W, B=()):
+        op("V", lambda: V.tensor_copy(out, in_), R, W, B)
+
+    def vms(ap, c, W):
+        op("V", lambda: V.memset(ap, c), [], W)
+
+    def sact(out, in_, f, R, W, B=(), bias=0.0, scale=1.0):
+        op("S", lambda: S.activation(out, in_, f, bias=bias, scale=scale), R, W, B)
+
+    def iota(out, pat, base, cm, W, small=False):
+        if small:
+            op("G", lambda: g.iota(out, pat, base, cm, allow_small_or_imprecise_dtypes=True), [], W)
+        else:
+            op("G", lambda: g.iota(out, pat, base, cm), [], W)
+
+    def do(*lists_):
+        lists_ = [list(x) for x in lists_ if x]
+        while lists_:
+            for x in lists_:
+                x.pop(0)()
+            lists_ = [x for x in lists_ if x]
+
+    dma("S", T.ledI[:], T.led[:], [], ["ledI"])
+    for b in range(4):
+        c = slice(b * 1024, (b + 1) * 1024)
+        dma("Y", T.XT[:, c], T.xt[:, c], [], ["X%d" % b])
+        if b == 0:
+            dma("S", T.mB[:], T.mk[:], [], ["mB0", "mB1"])
+    XALL = ["X0", "X1", "X2", "X3", "N0", "N1", "N2", "N3", "N1s", "N3s", "C"]
+
+    iota(T.pI[:], [[0, 1]], 0, 1, ["pI"])
+    iota(T.i8[:], [[-16, 8]], 0, 1, ["i8"])
+    vms(T.ones[:], 1.0, ["ones"])
+    vms(T.sel[:], 0.0, ["sel"])
+    vts(T.kI[:], T.pI[:], 15, ALU.bitwise_and, None, None, ["pI"], ["kI"])
+    vts(T.i8s[:], T.i8[:], 4, ALU.arith_shift_right, None, None, ["i8"], ["i8s"])
+    vts(T.parI[:], T.kI[:], 1, ALU.bitwise_and, None, None, ["kI"], ["parI"])
+    vcp(T.kcol[:], T.kI[:], ["kI"], ["kcol"])
+    vts(T.blkO[:], T.i8s[:], 0, ALU.is_equal, None, None, ["i8s"], ["blkO"])
+    vts(T.wcol[:], T.kI[:], 2.0, ALU.mult, 1.0, ALU.add, ["kI"], ["wcol"])
+    vts(T.offY[:], T.parI[:], -float(NOFF), ALU.mult, float(NOFF), ALU.add, ["parI"], ["offY"])
+    vts(T.oB[:], T.parI[:], float(NOFF), ALU.mult, -float(ZC), ALU.add, ["parI"], ["oB"])
+    vts(T.wb8[:], T.blkO[:], T.wcol[:, 0:1], ALU.mult, None, None, ["blkO", "wcol"], ["wb8"])
+    vts(T.s2c[:], T.kcol[:], 14.5, ALU.is_lt, None, None, ["kcol"], ["s2c"])
+    vts(T.s3c[:], T.kcol[:], 14.5, ALU.is_ge, float(ZC), ALU.add, ["kcol"], ["s3c"])
+    vms(T.XT[:, ZC:ZC + 16], 0.0, ["C"])
+    vms(T.zero[:], 0.0, ["zero"])
+    vms(T.XT[:, C15:C15 + 1], -2048.0, ["C"])
+    vms(T.bb[:, 0:16], 0.0, ["bbx"])
+    for b in range(8):
+        sact(T.sel[:, 16 * b:16 * b + 129 * 15 + 1:129], T.ones[:, 0:16], ACT.Copy, ["ones", "wb8", "sel"], ["selg%d" % b],
+             scale=T.wb8[:, b:b + 1])
+    SEL = ["sel"] + ["selg%d" % b for b in range(8)]
+    iota(T.iD[:], [[1, 128]], 0, -1, ["iD"])
+    iota(T.iG[:], [[-16, 8], [0, 16]], 0, 1, ["iG"])
+    iota(T.iR[:], [[0, 8], [1, 16]], 0, 0, ["iR"])
+    iota(T.iB[:], [[1024, 4]], 0, 0, ["iB"])
+    iota(T.iC[:], [[512, 4]], 32, 0, ["iC"])
+    iota(T.Qb[:, 4096:4112], [[0, 16]], 256, 0, ["Qx"], True)
+    iota(T.XT[:, TRO:TRO + 4096], [[0, 4096]], 0, 0, ["T1"], True)
+
+    def lists(c=slice(0, 256)):
+        return [
+            lambda: vts(T.LA[:, c], T.E[:, c], T.offY[:, 0:1], ALU.add, None, None, ["E0", "E1", "offY"], ["LA"]),
+            lambda: sact(T.tE[:, c], T.E[:, c], ACT.Identity, ["E0", "E1", "oB"], ["tE"], bias=T.oB[:, 0:1]),
+            lambda: vtt(T.tM[:, c], T.tE[:, c], T.mB[:, c], ALU.mult, ["tE", "mB0", "mB1"], ["tM"]),
+            lambda: vts(T.LB[:, c], T.tM[:, c], T.s2c[:, 0:1], ALU.mult, T.s3c[:, 0:1], ALU.add, ["tM", "s2c", "s3c"], ["LB"]),
+        ]
+
+    def signs():
+        sact(T.sg[:], T.mB[:], ACT.Copy, ["mB0", "mB1"], ["sg0", "sg1"], bias=1.0, scale=-2.0)
+
+    def neg(q, b, lo=0, hi=1024):
+        c = slice(b * 1024 + lo, b * 1024 + hi)
+        cn = slice(NOFF + b * 1024 + lo, NOFF + b * 1024 + hi)
+        if q == "V":
+            vts(T.XT[:, cn], T.XT[:, c], -1.0, ALU.mult, None, None, ["X%d" % b], ["N%d" % b])
+        else:
+            sact(T.XT[:, cn], T.XT[:, c], ACT.Copy, ["X%d" % b], ["N%ds" % b], scale=-1.0)
+
+    late = [
+        lambda: vts(T.w256[:], T.kcol[:], -1.0, ALU.mult, 256.0, ALU.add, ["kcol"], ["w256"]),
+        lambda: vts(T.ident[:], T.iD[:], 0, ALU.is_equal, None, None, ["iD"], ["ident"]),
+        lambda: vts(T.blkE[:], T.blkO[:], -1.0, ALU.mult, None, None, ["blkO"], ["blkE"]),
+        lambda: vts(T.iGs[:], T.iG[:], 4, ALU.arith_shift_right, None, None, ["iG"], ["iGs"]),
+        lambda: vts(T.Pd[:], T.ident[:], T.w256[:, 0:1], ALU.mult, None, None, ["ident", "w256"], ["Pd"]),
+        lambda: vts(T.tri[:], T.iD[:], 0, ALU.is_ge, -16.0, ALU.mult, ["iD"], ["tri"]),
+        lambda: vts(T.kmat[:], T.iGs[:], 0, ALU.is_equal, T.kcol[:, 0:1], ALU.mult, ["iGs", "kcol"], ["kmat"]),
+        lambda: vts(T.crow[:], T.iR[:], 0.125, ALU.mult, None, None, ["iR"], ["crow"]),
+        lambda: vms(T.Ct[:], 16384.0, ["Ct"]),
+        lambda: vms(T.ecb[:], 0.0, ["ecb"]),
+        lambda: vts(T.k64[:], T.kcol[:], 64.0, ALU.mult, None, None, ["kcol"], ["k64"]),
+        lambda: vms(T.Ct[:, 0:128:16], 0.5, ["Ct"]),
+        lambda: vms(T.ecb[:, 0:16:5], 1.0, ["ecb"]),
+        lambda: vcp(T.jc[:], T.iC[:], ["iC"], ["jc"]),
+        lambda: vts(T.base[:], T.iB[:], T.k64[:, 0:1], ALU.add, None, None, ["iB", "k64"], ["base"]),
+        lambda: vcp(T.ec[:], T.ecb[:], ["ecb"], ["ec"]),
+        lambda: vcp(T.onesh[:], T.ones[:], ["ones"], ["onesh"]),
+        lambda: vms(T.all16[:], -16.0, ["all16"]),
+    ]
+    vts(T.sgn[:], T.parI[:], 2.0, ALU.mult, -1.0, ALU.add, ["parI"], ["sgn"])
+    vcp(T.E[:], T.ledI[:], ["ledI"], ["E0", "E1"])
+    do(lists(), late[0:3])
+    signs()
+    neg("S", 1)
+    neg("V", 0)
+    do(late[3:10])
+    neg("V", 2)
+    do(late[10:])
+    neg("S", 3, 0, 320)
+    neg("V", 3, 320, 1024)
+
+    def ce(i):
+        return slice(i * 1024, (i + 1) * 1024)
+
+    def ca(i):
+        return slice(i * 64, (i + 1) * 64)
+
+    def cb(b):
+        return slice(b * 128, (b + 1) * 128)
+
+    def gather(q, out, lst, i, R, W):
+        src = T.XT[:, 0:GW].indirect(lst[:, ca(i)])
+        if q == "V":
+            vcp(out[:, ce(i)], src, R + XALL, W)
+        else:
+            sact(out[:, ce(i)], src, ACT.Copy, R + XALL, W)
+
+    def gA(q, i):
+        gather(q, T.Ab, T.LA, i, ["LA"], ["A%d" % i])
+
+    def gB(q, i):
+        gather(q, T.Bb, T.LB, i, ["LB"], ["B%d" % i])
+
+    def scans(i):
+        o = slice(i * 1024 + 16, (i + 1) * 1024 + 16)
+        p = slice(i * 1024 + 15, (i + 1) * 1024 + 15)
+        return [
+            lambda: op("V", lambda: V.tensor_tensor_scan(T.bb[:, o], T.Bb[:, ce(i)], T.zero[:], 0.0, ALU.add, ALU.max),
+                       ["B%d" % i, "zero"], ["bb%d" % i]),
+            lambda: op("V", lambda: V.tensor_tensor_scan(T.Qb[:, ce(i)], T.bb[:, p], T.Ab[:, ce(i)], 0.0, ALU.max, ALU.min),
+                       ["bb%d" % i, "bbx" if i == 0 else "bb%d" % (i - 1), "A%d" % i], ["Q%d" % i]),
+        ]
+
+    def over(q, i):
+        if q == "V":
+            vts(T.pb[:, ce(i)], T.Qb[:, ce(i)], -1.0, ALU.max, 1.0, ALU.min, ["Q%d" % i], ["p%d" % i])
+        else:
+            sact(T.pb[:, ce(i)], T.Qb[:, ce(i)], ACT.Sign, ["Q%d" % i], ["p%d" % i])
+
+    def group(calls, R, W, B):
+        def f():
+            r = None
+            for c in calls:
+                r = P.matmul(*c)
+            return r
+        op("P", f, R, W, B)
+
+    UB = (("pU0", 0), ("pU1", 0), ("pU0", 0), ("pU0", 64))
+
+    def pU(i):
+        n, o = UB[i]
+        group([(T[n][:, o:o + 64], T.sel[:, 128 * k:128 * (k + 1)], T.Qb[:, i * 1024 + k:(i + 1) * 1024:16], k == 0, k == 15)
+               for k in range(16)], SEL + ["Q%d" % i], ["u%d" % i], [n])
+
+    def hchain(cs, t):
+        n = UB[cs[0]][0]
+        a = slice(cs[0] * 64, cs[-1] * 64 + 64)
+        p = T[n][:, 0:64 * len(cs)]
+        s = str(cs[0])
+        e = "E%d" % (cs[0] // 2)
+        ek = T.E if t == 0 else T.Ek
+        return [
+            lambda: vts(T.uI[:, a], p, T.sgn[:, 0:1], ALU.mult, None, None, ["u%d" % i for i in cs] + ["sgn"], ["uI" + s], [n]),
+            lambda: vts(T.uA[:, a], T.uI[:, a], 4095, ALU.bitwise_and, None, None, ["uI" + s], ["uA" + s]),
+            lambda: vtt(T.eu[:, a], T.E[:, a], T.uA[:, a], ALU.mult, ["uA" + s, e], ["eu" + s]),
+            lambda: vts(T.wv[:, a], T.eu[:, a], 5, ALU.arith_shift_right, 4095, ALU.bitwise_and, ["eu" + s], ["wv" + s]),
+            lambda: vtt(T.hs[:, a], T.wv[:, a], ek[:, a], ALU.add, ["wv" + s, e if t == 0 else "Ek"], ["hs" + s]),
+            lambda: vts(T.hI[:, a], T.hs[:, a], 4095, ALU.bitwise_and, None, None, ["hs" + s], ["hI%d" % i for i in cs]),
+            lambda: vts(T.LY[:, a], T.hI[:, a], T.offY[:, 0:1], ALU.add, None, None, ["hI%d" % cs[0], "offY"],
+                        ["LY%d" % i for i in cs]),
+        ]
+
+    def ysub(i, part=None):
+        lo, hi = (0, 64) if part is None else (32 * part, 32 * part + 32)
+        a = slice(i * 64 + lo, i * 64 + hi)
+        c = slice(a.start * 16, a.stop * 16)
+        vtt(T.zb[:, c], T.XT[:, 0:GW].indirect(T.LY[:, a]), T.Qb[:, c], ALU.subtract,
+            ["LY%d" % i, "Q%d" % i] + XALL, ["z%d" % i if part is None or part == 1 else "z%da" % i])
+
+    def sign(q, i):
+        if q == "V":
+            vts(T.sb[:, ce(i)], T.zb[:, ce(i)], -1.0, ALU.max, 1.0, ALU.min, ["z%d" % i, "z%da" % i], ["s%d" % i])
+        else:
+            sact(T.sb[:, ce(i)], T.zb[:, ce(i)], ACT.Sign, ["z%d" % i, "z%da" % i], ["s%d" % i])
+
+    def sums(ps, src, tag, b):
+        group([(T[ps][:, b * 128 + k:(b + 1) * 128:16], src[:, b * 2048 + k:(b + 1) * 2048:16],
+                (T.blkE if k % 2 == 0 else T.blkO)[:], True, True) for k in range(16)],
+              [tag + str(2 * b), tag + str(2 * b + 1), "blkE", "blkO"], [ps + str(b)], [ps])
+
+    def pGK():
+        group([(T.pGK[:, cb(b)], T.sg[:, cb(b)], T.Pd[:], True, True) for b in range(2)], ["sg0", "sg1", "Pd"], ["pGK"], ["pGK"])
+
+    def dec_over(b):
+        s = str(b)
+        return [
+            lambda: vts(T.ov[:, cb(b)], T.pOV[:, cb(b)], 8.5, ALU.is_ge, None, None, ["pOV" + s], ["ov" + s], ["pOV"]),
+            lambda: vtt(T.gov[:, cb(b)], T.pGK[:, cb(b)], T.ov[:, cb(b)], ALU.mult, ["pGK", "ov" + s], ["gov" + s], ["pGK"]),
+        ]
+
+    def decide(b):
+        s = str(b)
+        c = cb(b)
+
+        def places():
+            sact(T.flipX[:, c], T.R2[:, c], ACT.Sign, ["R2" + s], ["fl" + s], bias=-0.5)
+
+        def winners():
+            vtt(T.win[:, c], T.comp[:, c], T.R2[:, c], ALU.is_equal, ["comp" + s, "R2" + s], ["win" + s])
+            group([(T.pWN[:, c], T.win[:, c], T.ident[:], True, True)], ["win" + s, "ident"], ["pWN" + s], ["pWN"])
+            calls = [(T.pZ[:, c], T.ones[:], T.crow[:], True, False), (T.pZ[:, c], T.tri[:], T.flipX[:, c], False, False)]
+            R = ["tri", "fl" + s, "ones", "crow"]
+            if b == 1:
+                calls.append((T.pZ[:, c], T.all16[:], T.flipX[:, cb(0)], False, False))
+                R += ["all16", "fl0"]
+            group(calls, R, ["pZ" + s], ["pZ"])
+            sact(T.wsb[:, c], T.pWN[:, c], ACT.Copy, ["pWN" + s], ["wsb" + s], ["pWN"])
+            group([(T.pZ[:, c], T.wsb[:, c], T.kmat[:], False, True)], ["wsb" + s, "kmat"], ["pZ" + s], ["pZ"])
+
+        def scan(dst, src, w, r):
+            op("V", lambda: V.tensor_tensor_scan(dst[:, c], T.Ct[:], src[:, c], 0.5, ALU.min, ALU.max), ["Ct", r], [w])
+
+        return [
+            lambda: vtt(T.comp[:, c], T.pS[:, c], T.gov[:, c], ALU.mult, ["pS" + s, "gov" + s], ["comp" + s], ["pS"]),
+            lambda: scan(T.R1, T.comp, "R1" + s, "comp" + s),
+            lambda: vcp(T.R1[:, b * 128:(b + 1) * 128:16], T.R1[:, b * 128 + 15:(b + 1) * 128:16], ["R1" + s], ["R1" + s]),
+            lambda: (scan(T.R2, T.R1, "R2" + s, "R1" + s), places()),
+            winners,
+        ]
+
+    def clamps(b):
+        s = str(b)
+
+        def one(c):
+            lo = -(256.0 * c + 16)
+            o = slice(c * 256 + b * 128, c * 256 + (b + 1) * 128)
+            vts(T.D[:, o], T.pZ[:, cb(b)], lo, ALU.max, lo + 16, ALU.min, ["pZ" + s], ["D%d%d" % (c, b)], ["pZ"])
+        return [lambda c=c: one(c) for c in range(4)]
+
+    def pLJ(b):
+        calls = [] if b else [(T.pSM[:, 0:4], T.onesh[:], T.jc[:], True, False)]
+        for c in range(4):
+            calls.append((T.pSM[:, 0:4], T.D[:, c * 256 + b * 128:c * 256 + (b + 1) * 128], T.ec[:, 4 * c:4 * c + 4], False,
+                          b == 1 and c == 3))
+        group(calls, ["onesh", "jc", "ec"] + ["D%d%d" % (c, b) for c in range(4)], ["LJp"], ["pSM"])
+
+    def send(t):
+        vcp(T.LJ[:], T.pSM[:, 0:4], ["LJp"], ["LJ"], ["pSM"])
+        qn = "qs%d" % t
+        sact(T[qn][:], T.Qb[:].indirect(T.LJ[:, 0:4]), ACT.Abs, ["LJ", "Qx", "Q0", "Q1", "Q2", "Q3"], [qn])
+        dst = T.cores[(rank + 1 + t % (n_ranks - 1)) % n_ranks]
+        rid, pid, _ = topo.addr(dst)
+        eng = topo.engines(core, dst)[:NENG]
+        depends("G", [qn], [], ())
+        g.remote_dma(T["land%d" % t][:], T[qn][:], T.sem["arr%d" % t], T.sem.sent, pid, rid, sum(1 << e for e in eng))
+        count["sent"] = count.get("sent", 0) + len(eng)
+        src = T.cores[(rank - 1 - t % (n_ranks - 1)) % n_ranks]
+        note("R", "arr%d" % t, len(topo.engines(src, core)[:NENG]), [], ["land%d" % t], (), {})
+
+    def kappa():
+        group([(T.pU1[:, 64:72], T.ones[:], T.flipX[:, b * 128:(b + 1) * 128:16], b == 0, b == 1) for b in range(2)],
+              ["ones", "fl0", "fl1"], ["kp"], ["pU1"])
+
+    def kappa2():
+        return [
+            lambda: op("V", lambda: V.tensor_reduce(T.kr[:], T.pU1[:, 64:72], AxisListType.X, ALU.add), ["kp"], ["kr"], ["pU1"]),
+            lambda: vcp(T.kri[:], T.kr[:], ["kr"], ["kri"]),
+            lambda: vts(T.krm[:], T.kri[:], 31, ALU.bitwise_and, None, None, ["kri"], ["krm"]),
+            lambda: vcp(T.kap[:], T.krm[:], ["krm"], ["kap"]),
+        ]
+
+    def ekappa():
+        sact(T.Ek[:], T.E[:], ACT.Identity, ["E0", "E1", "kap"], ["Ek"], bias=T.kap[:, 0:1])
+
+    def update(b):
+        c = cb(b)
+        s = str(b)
+        return [
+            lambda: vtt(T.dh[:, c], T.hI[:, c], T.E[:, c], ALU.subtract, ["hI%d" % (2 * b), "hI%d" % (2 * b + 1), "E" + s], ["dh" + s]),
+            lambda: vtt(T.wM[:, c], T.pWN[:, c], T.sg[:, c], ALU.mult, ["pWN" + s, "sg" + s], ["wM" + s], ["pWN"]),
+            lambda: vtt(T.wE[:, c], T.pWN[:, c], T.dh[:, c], ALU.mult, ["pWN" + s, "dh" + s], ["wE" + s], ["pWN"]),
+            lambda: vtt(T.mB[:, c], T.mB[:, c], T.wM[:, c], ALU.add, ["mB" + s, "wM" + s], ["mB" + s]),
+            lambda: vtt(T.E[:, c], T.E[:, c], T.wE[:, c], ALU.add, ["E" + s, "wE" + s], ["E" + s]),
+        ]
+
+    def arrive(t, last):
+        ln = "land%d" % t
+        group([(T.pSM[:, 32:36], T.sel[:, 128 * r:128 * (r + 1)], T[ln][:, r:64:16], r == 0, r == 15) for r in range(16)],
+              SEL + [ln], ["pA"], ["pSM"])
+        vcp(T.vi[:], T.pSM[:, 32:36], ["pA"], ["vi"], ["pSM"])
+        vts(T.vinv[:], T.pSM[:, 32:36], 65535.5, ALU.is_ge, float(TRO), ALU.mult, ["pA"], ["vinv"], ["pSM"])
+        vts(T.vm[:], T.vi[:], 63, ALU.bitwise_and, None, None, ["vi"], ["vm"])
+        vtt(T.vbs[:], T.vinv[:], T.base[:], ALU.add, ["vinv", "base"], ["vbs"])
+        vtt(T.vid[:], T.vm[:], T.vbs[:], ALU.add, ["vm", "vbs"], ["vid"])
+        vcp(T.LI[:, 0:4], T.vid[:], ["vid"], ["LI"])
+        if not last:
+            vts(T.LI[:, 4:8], T.vid[:], float(NOFF), ALU.add, None, None, ["vid"], ["LI2"])
+        vtt(T.tx[:], T.XT[:, 0:TRO + 4096].indirect(T.LI[:, 0:4]), T[ln][:], ALU.add, ["LI", ln, "T1"] + XALL, ["tx"])
+        vts(T.ND[:, 0:64], T.tx[:], 0.5, ALU.mult, -0.25, ALU.add, ["tx"], ["ND0"])
+        xw = XALL[:10] + ["T1"]
+        if last:
+            op("V", lambda: V.tensor_copy(T.XT[:, 0:WEND].indirect(T.LI[:, 0:4]), T.ND[:, 0:64]), ["LI", "ND0"], xw)
+        else:
+            vts(T.ND[:, 64:128], T.tx[:], -0.5, ALU.mult, 0.25, ALU.add, ["tx"], ["ND1"])
+            op("V", lambda: V.tensor_copy(T.XT[:, 0:WEND].indirect(T.LI[:, 0:8]), T.ND[:]), ["LI", "LI2", "ND0", "ND1"], xw)
+
+    for t in range(rounds):
+        last = t == rounds - 1
+        gA("V", 0)
+        gB("S", 0)
+        gB("S", 1)
+        do(scans(0))
+        pU(0)
+        gA("V", 1)
+        if t == 0:
+            pGK()
+        gA("S", 2)
+        gB("S", 2)
+        gA("S", 3)
+        gB("S", 3)
+        h0 = hchain((0,), t)
+        do(h0[:3])
+        do(scans(1), h0[3:5])
+        pU(1)
+        do(h0[5:])
+        ysub(0)
+        over("S", 0)
+        over("S", 1)
+        sums("pOV", T.pb, "p", 0)
+        h1 = hchain((1,), t)
+        do(h1[:3])
+        do(scans(2), h1[3:5])
+        pU(2)
+        do(h1[5:])
+        sign("S", 0)
+        do(scans(3))
+        pU(3)
+        ysub(1)
+        sign("S", 1)
+        over("S", 2)
+        over("S", 3)
+        sums("pS", T.sb, "s", 0)
+        d0 = dec_over(0) + decide(0)
+        h23 = hchain((2, 3), t)
+        do(h23, d0[0:2])
+        ysub(2, 0)
+        d0[2]()
+        ysub(2, 1)
+        sign("S", 2)
+        d0[3]()
+        ysub(3, 0)
+        d0[4]()
+        sums("pOV", T.pb, "p", 1)
+        d1 = dec_over(1) + decide(1)
+        d1[0]()
+        d0[5]()
+        d1[1]()
+        d0[6]()
+        ysub(3, 1)
+        u0 = update(0)
+        sign("V", 3)
+        sums("pS", T.sb, "s", 1)
+        do(clamps(0))
+        pLJ(0)
+        do(u0[0:1])
+        do(d1[2:], u0[1:])
+        do(clamps(1))
+        pLJ(1)
+        u1 = update(1)
+        if not last:
+            kappa()
+        do(u1[0:3])
+        send(t)
+        do(u1[3:])
+        if last:
+            dma("Y", T.ym[:], T.mB[:], ["mB0", "mB1"], ["ym"])
+            dma("S", T.yl[:], T.E[:], ["E0", "E1"], ["yl"])
+        else:
+            do(lists(), kappa2())
+            signs()
+            ekappa()
+            pGK()
+        arrive(t, last)
+    for b in range(2):
+        c = slice(b * 2048, (b + 1) * 2048)
+        dma("YS"[b], T.yx[:, c], T.XT[:, c], ["X%d" % (2 * b), "X%d" % (2 * b + 1)], ["yx%d" % b])
+    for sem, n in count.items():
+        if known["G"].get(sem, 0) < n:
+            g.wait_ge(T.sem[sem], n)

@@ -1,114 +1,87 @@
-import numpy as np
-from concourse.mybir import AluOpType as ALU, AxisListType, ActivationFunctionType as ACT
+import math
+from concourse.mybir import AluOpType as ALU, ActivationFunctionType as ACT
 
-NX, NOFF, ZC, C15, TRO, WEND = 4096, 4096, 8192, 8193, 8208, 16400
-GW = 8208
+ZC, C15, SP, NOFF = 4096, 4097, 4112, 16384
+GW = NOFF + 4096
+AW = SP + 4096
+WEND = NOFF + AW
 NENG = 8
+LAM, LOW, PART = 0.6, -78.0, 0.4
 
-SCRATCH = {
-    "XT": ("sbuf", [128, WEND], "bfloat16"),
-    "ledI": ("sbuf", [128, 256], "int32"),
-    "E": ("sbuf", [128, 256], "float32"),
-    "Ek": ("sbuf", [128, 256], "float32"),
-    "mB": ("sbuf", [128, 256], "bfloat16"),
-    "sg": ("sbuf", [128, 256], "bfloat16"),
-    "LA": ("sbuf", [128, 256], "uint16"),
-    "LB": ("sbuf", [128, 256], "uint16"),
-    "LY": ("sbuf", [128, 256], "uint16"),
-    "tE": ("sbuf", [128, 256], "float32"),
-    "tM": ("sbuf", [128, 256], "float32"),
-    "dh": ("sbuf", [128, 256], "float32"),
-    "wE": ("sbuf", [128, 256], "float32"),
-    "wM": ("sbuf", [128, 256], "bfloat16"),
-    "Ab": ("sbuf", [128, 4096], "bfloat16"),
-    "Bb": ("sbuf", [128, 4096], "bfloat16"),
-    "bb": ("sbuf", [128, 4096 + 32], "bfloat16"),
-    "Qb": ("sbuf", [128, 4096 + 16], "bfloat16"),
-    "zb": ("sbuf", [128, 4096], "bfloat16"),
-    "sb": ("sbuf", [128, 4096], "bfloat16"),
-    "pb": ("sbuf", [128, 4096], "bfloat16"),
-    "zero": ("sbuf", [128, 1024], "bfloat16"),
-    "uI": ("sbuf", [128, 256], "int32"),
-    "uA": ("sbuf", [128, 256], "int32"),
-    "eu": ("sbuf", [128, 256], "int32"),
-    "wv": ("sbuf", [128, 256], "int32"),
-    "hs": ("sbuf", [128, 256], "int32"),
-    "hI": ("sbuf", [128, 256], "int32"),
-    "ov": ("sbuf", [128, 256], "bfloat16"),
-    "gov": ("sbuf", [128, 256], "bfloat16"),
-    "comp": ("sbuf", [128, 256], "float32"),
-    "R1": ("sbuf", [128, 256], "float32"),
-    "R2": ("sbuf", [128, 256], "float32"),
-    "win": ("sbuf", [128, 256], "bfloat16"),
-    "flipX": ("sbuf", [128, 256], "bfloat16"),
-    "wsb": ("sbuf", [128, 256], "bfloat16"),
-    "D": ("sbuf", [128, 1024], "float16"),
-    "LJ": ("sbuf", [128, 4], "uint16"),
-    "kr": ("sbuf", [128, 1], "float32"),
-    "kri": ("sbuf", [128, 1], "int32"),
-    "krm": ("sbuf", [128, 1], "int32"),
-    "kap": ("sbuf", [128, 1], "float32"),
-    "qs0": ("sbuf", [128, 64], "bfloat16"),
-    "qs1": ("sbuf", [128, 64], "bfloat16"),
-    "qs2": ("sbuf", [128, 64], "bfloat16"),
-    "land0": ("sbuf", [128, 64], "bfloat16"),
-    "land1": ("sbuf", [128, 64], "bfloat16"),
-    "land2": ("sbuf", [128, 64], "bfloat16"),
-    "vi": ("sbuf", [128, 4], "int32"),
-    "vm": ("sbuf", [128, 4], "int32"),
-    "vinv": ("sbuf", [128, 4], "float32"),
-    "vbs": ("sbuf", [128, 4], "float32"),
-    "vid": ("sbuf", [128, 4], "float32"),
-    "LI": ("sbuf", [128, 8], "uint16"),
-    "tx": ("sbuf", [128, 64], "float32"),
-    "ND": ("sbuf", [128, 128], "int32"),
-    "pI": ("sbuf", [128, 1], "int32"),
-    "kI": ("sbuf", [128, 1], "int32"),
-    "parI": ("sbuf", [128, 1], "int32"),
-    "kcol": ("sbuf", [128, 1], "float32"),
-    "sgn": ("sbuf", [128, 1], "float32"),
-    "offY": ("sbuf", [128, 1], "float32"),
-    "oB": ("sbuf", [128, 1], "float32"),
-    "s2c": ("sbuf", [128, 1], "float32"),
-    "s3c": ("sbuf", [128, 1], "float32"),
-    "wcol": ("sbuf", [128, 1], "float32"),
-    "w256": ("sbuf", [128, 1], "float32"),
-    "k64": ("sbuf", [128, 1], "float32"),
-    "i8": ("sbuf", [128, 8], "int32"),
-    "i8s": ("sbuf", [128, 8], "int32"),
-    "blkO": ("sbuf", [128, 8], "bfloat16"),
-    "blkE": ("sbuf", [128, 8], "bfloat16"),
-    "wb8": ("sbuf", [128, 8], "float32"),
-    "iD": ("sbuf", [128, 128], "int32"),
-    "iG": ("sbuf", [128, 128], "int32"),
-    "iGs": ("sbuf", [128, 128], "int32"),
-    "iR": ("sbuf", [128, 128], "int32"),
-    "iB": ("sbuf", [128, 4], "int32"),
-    "iC": ("sbuf", [128, 4], "int32"),
-    "ident": ("sbuf", [128, 128], "bfloat16"),
-    "tri": ("sbuf", [128, 128], "bfloat16"),
-    "all16": ("sbuf", [128, 128], "bfloat16"),
-    "ones": ("sbuf", [128, 128], "bfloat16"),
-    "onesh": ("sbuf", [128, 128], "float16"),
-    "kmat": ("sbuf", [128, 128], "bfloat16"),
-    "Pd": ("sbuf", [128, 128], "bfloat16"),
-    "crow": ("sbuf", [128, 128], "bfloat16"),
-    "Ct": ("sbuf", [128, 128], "float32"),
-    "base": ("sbuf", [128, 4], "float32"),
-    "jc": ("sbuf", [128, 4], "float16"),
-    "ecb": ("sbuf", [128, 16], "bfloat16"),
-    "ec": ("sbuf", [128, 16], "float16"),
-    "sel": ("sbuf", [128, 2048], "bfloat16"),
-    "pU0": ("psum", [128, 512], "float32"),
-    "pU1": ("psum", [128, 512], "float32"),
-    "pOV": ("psum", [128, 512], "float32"),
-    "pS": ("psum", [128, 512], "float32"),
-    "pGK": ("psum", [128, 512], "float32"),
-    "pWN": ("psum", [128, 512], "float32"),
-    "pZ": ("psum", [128, 512], "float32"),
-    "pSM": ("psum", [128, 512], "float32"),
-}
+OPT = dict(cc="VVVV", gE="VSSS", gB="SSSS", relu="VSSS", over="SSSS", y="SVSVVVVV", sign="SSSSSSVV")
+GATHER, SCATTER, MATMUL, WAKE, LOAD, FLIGHT, SLACK = 1.5, 3.8, 0.5, 150, 2400, 3000, 100
+SWEEPS = 4
+
+
+def _sb(cols, dt):
+    return ("sbuf", [128, cols], dt)
+
+
+SCRATCH = {"XT": _sb(WEND, "bfloat16"), "Qb": _sb(4096 + 16, "bfloat16"), "D": _sb(1024, "float16"), "LL": _sb(384, "uint16"),
+           "ND": _sb(128, "int32"), "tx": _sb(64, "float32"), "LI": _sb(4, "uint16"), "LJ": _sb(4, "uint16"),
+           "zero": _sb(1024, "bfloat16"), "iS": _sb(144, "int32"), "ec": _sb(16, "float16"), "LY": _sb(256, "uint16"),
+           "prm": _sb(512, "float16")}
+SCRATCH.update({n: _sb(4096, "bfloat16") for n in ("Bb", "bb", "zb", "sb")})
+SCRATCH.update({n: _sb(2048, "bfloat16") for n in ("pe", "po")})
+SCRATCH.update({n: _sb(256, "int32") for n in ("ledI", "eu", "wv", "hs", "hm")})
+SCRATCH.update({n: _sb(256, "float32") for n in ("E", "wE")})
+SCRATCH.update({n: _sb(256, "float16") for n in ("E16", "mA", "mE")})
+SCRATCH.update({n: _sb(256, "bfloat16") for n in ("mB", "sg", "cc", "ts", "comp", "val", "win", "cum")})
+SCRATCH.update({n: _sb(64, "bfloat16") for n in ("qs0", "qs1", "qs2", "land0", "land1", "land2")})
+SCRATCH.update({n: _sb(144, "bfloat16") for n in ("Wp", "Wn", "W2", "On")})
+SCRATCH.update({n: _sb(128, "bfloat16") for n in ("ones", "I4k", "cU", "cCap", "cPh", "blkT", "blk16", "kmat", "crow")})
+SCRATCH.update({n: _sb(128, "float16") for n in ("onesh", "identH")})
+SCRATCH.update({n: _sb(128, "int32") for n in ("iD", "iG", "iR", "iP")})
+SCRATCH.update({n: _sb(4, "int32") for n in ("vi", "vm", "iB", "iC")})
+SCRATCH.update({n: _sb(4, "float32") for n in ("vinv", "vbs", "vid", "base")})
+SCRATCH.update({n: _sb(1, "int32") for n in ("pI", "kI", "parI", "i7", "kri", "krm")})
+SCRATCH.update({n: _sb(1, "float32") for n in ("kcol", "negk", "wcol", "wneg", "w2", "k64", "kap", "sa", "sc0", "ma", "mc", "lo7",
+                                                "hi7", "bk")})
+SCRATCH["jc"] = _sb(4, "float16")
+SCRATCH.update({n: ("psum", [128, 512], "float32") for n in ("pU0", "pU1", "pE", "pA", "pB", "pZ", "pSM", "pY")})
 SEMAPHORES = (["cV", "cS", "cP", "cG", "sent"] + ["arr%d" % t for t in range(3)] + ["d%d" % i for i in range(24)])
+
+
+def in_order(calls):
+    n = len(calls)
+    lastw, readers, pre, post = {}, {}, [], [[] for _ in calls]
+    for i, (q, _, _, R, W, _, _) in enumerate(calls):
+        p = {lastw[t] for t in list(R) + list(W) if t in lastw} | {j for t in W for j in readers.get(t, [])}
+        pre.append(sorted(p))
+        for j in p:
+            post[j].append(i)
+        for t in R:
+            readers.setdefault(t, []).append(i)
+        for t in W:
+            lastw[t], readers[t] = i, []
+
+    def sweep(pre, post, rank):
+        left = [len(p) for p in pre]
+        ready = {i: 0 for i in range(n) if not left[i]}
+        done, free, bank, order = [0] * n, {}, {}, []
+        while ready:
+            st = {i: max([r, free.get(calls[i][0], 0)] + [bank[b][1] + WAKE for b in calls[i][5] if b in bank and bank[b][0] != calls[i][0]])
+                  for i, r in ready.items()}
+            first = min(ready, key=lambda i: (st[i], -rank[i]))
+            i = max((i for i in ready if calls[i][0] == calls[first][0] and st[i] <= st[first] + SLACK), key=lambda i: rank[i])
+            free[calls[i][0]], done[i] = st[i] + calls[i][1], st[i] + calls[i][2]
+            for b in calls[i][5]:
+                bank[b] = (calls[i][0], done[i])
+            del ready[i]
+            order.append(i)
+            for j in post[i]:
+                left[j] -= 1
+                if not left[j]:
+                    ready[j] = max(done[x] for x in pre[j]) + WAKE
+        return done, order
+
+    rank, best = [-i for i in range(n)], None
+    for _ in range(SWEEPS):
+        done, order = sweep(pre, post, rank)
+        if best is None or max(done) < best[0]:
+            best = (max(done), order)
+        rank, _ = sweep(post, pre, done)
+    return best[1]
 
 
 def rank_program(g, core, T, topo):
@@ -119,462 +92,350 @@ def rank_program(g, core, T, topo):
     rounds = 3
     V, S, P = g.vector, g.scalar, g.tensor
     Q = {"V": V, "S": S, "P": P, "G": g, "Y": g.sync}
-    count = {}
-    known = {q: {} for q in Q}
-    lastw, readers, banks = {}, {}, {}
-    seq, nd = [0], [0]
+    calls = []
 
-    def depends(q, R, W, B):
-        toks = []
-        for t in R:
-            if t in lastw:
-                toks.append(lastw[t])
-        for t in W:
-            if t in lastw:
-                toks.append(lastw[t])
-            toks += [x for x in readers.get(t, []) if x[2] != q]
-        for b in B:
-            toks += [x for qq, x in banks.get(b, {}).items() if qq != q]
-        for sem, val, _, snap, _ in sorted(toks, key=lambda x: -x[4]):
-            k = known[q]
-            if k.get(sem, 0) >= val:
-                continue
-            Q[q].wait_ge(T.sem[sem], val)
-            for s, v in snap.items():
-                if k.get(s, 0) < v:
-                    k[s] = v
-            k[sem] = max(k.get(sem, 0), val)
+    def op(q, c, f, R, W, B=()):
+        calls.append((q, c, c, R, W, B, f))
 
-    def note(q, sem, n, R, W, B, snap):
-        count[sem] = count.get(sem, 0) + n
-        seq[0] += 1
-        tok = (sem, count[sem], q, snap, seq[0])
-        for t in R:
-            readers.setdefault(t, []).append(tok)
-        for t in W:
-            lastw[t] = tok
-            readers[t] = []
-        for b in B:
-            banks.setdefault(b, {})[q] = tok
+    def dma(q, out, in_, R, W, c):
+        calls.append((q, 100, c, R, W, (), ("dma", out, in_)))
 
-    def op(q, f, R, W, B=()):
-        depends(q, R, W, B)
-        f().then_inc(T.sem["c" + q], 1)
-        note(q, "c" + q, 1, R, W, B, dict(known[q]))
-
-    def dma(q, out, in_, R, W):
-        depends(q, R, W, ())
-        sem = "d%d" % nd[0]
-        nd[0] += 1
-        Q[q].dma_start(out, in_).then_inc(T.sem[sem], 16)
-        note(q, sem, 16, R, W, (), dict(known[q]))
-
-    def vts(out, in0, s1, o0, s2, o1, R, W, B=()):
+    def vts(out, in0, s1, o0, s2, o1, R, W, B=(), c=64):
         if o1 is None:
-            op("V", lambda: V.tensor_scalar(out, in0, s1, None, o0), R, W, B)
+            op("V", c, lambda: V.tensor_scalar(out, in0, s1, None, o0), R, W, B)
         else:
-            op("V", lambda: V.tensor_scalar(out, in0, s1, s2, o0, o1), R, W, B)
+            op("V", c, lambda: V.tensor_scalar(out, in0, s1, s2, o0, o1), R, W, B)
 
-    def vtt(out, a, b, o, R, W, B=()):
-        op("V", lambda: V.tensor_tensor(out, a, b, o), R, W, B)
+    def vtt(out, a, b, o, R, W, B=(), c=64):
+        op("V", c, lambda: V.tensor_tensor(out, a, b, o), R, W, B)
 
-    def vcp(out, in_, R, W, B=()):
-        op("V", lambda: V.tensor_copy(out, in_), R, W, B)
+    def vcp(out, in_, R, W, B=(), c=64):
+        op("V", c, lambda: V.tensor_copy(out, in_), R, W, B)
 
-    def vms(ap, c, W):
-        op("V", lambda: V.memset(ap, c), [], W)
+    def vms(ap, x, W, c=64):
+        op("V", c, lambda: V.memset(ap, x), [], W)
 
-    def sact(out, in_, f, R, W, B=(), bias=0.0, scale=1.0):
-        op("S", lambda: S.activation(out, in_, f, bias=bias, scale=scale), R, W, B)
+    def vscan(out, a, b, init, o0, o1, R, W, c=64):
+        op("V", c, lambda: V.tensor_tensor_scan(out, a, b, init, o0, o1), R, W)
+
+    def sact(out, in_, f, R, W, B=(), bias=0.0, scale=1.0, c=64):
+        op("S", c, lambda: S.activation(out, in_, f, bias=bias, scale=scale), R, W, B)
 
     def iota(out, pat, base, cm, W, small=False):
+        c = 160 + 2 * math.prod(n for _, n in pat)
         if small:
-            op("G", lambda: g.iota(out, pat, base, cm, allow_small_or_imprecise_dtypes=True), [], W)
+            op("G", c, lambda: g.iota(out, pat, base, cm, allow_small_or_imprecise_dtypes=True), [], W)
         else:
-            op("G", lambda: g.iota(out, pat, base, cm), [], W)
+            op("G", c, lambda: g.iota(out, pat, base, cm), [], W)
 
-    def do(*lists_):
-        lists_ = [list(x) for x in lists_ if x]
-        while lists_:
-            for x in lists_:
-                x.pop(0)()
-            lists_ = [x for x in lists_ if x]
+    def group(mms, R, W, B, n=64):
+        def f():
+            r = None
+            for m in mms:
+                r = P.matmul(*m)
+            return r
+        op("P", len(mms) * n * MATMUL, f, R, W, B)
 
-    dma("S", T.ledI[:], T.led[:], [], ["ledI"])
+    def col(name):
+        return T[name][:, 0:1]
+
+    def gat(n):
+        return 70 + GATHER * n
+
+    EE, MM = ["E0", "E1"], ["mB0", "mB1"]
+    dma("S", T.ledI[:], T.led[:], [], ["ledI"], LOAD)
+    dma("S", T.mB[:], T.mk[:], [], MM, LOAD + 300)
     for b in range(4):
         c = slice(b * 1024, (b + 1) * 1024)
-        dma("Y", T.XT[:, c], T.xt[:, c], [], ["X%d" % b])
-        if b == 0:
-            dma("S", T.mB[:], T.mk[:], [], ["mB0", "mB1"])
-    XALL = ["X0", "X1", "X2", "X3", "N0", "N1", "N2", "N3", "N1s", "N3s", "C"]
+        dma("Y", T.XT[:, c], T.xt[:, c], [], ["X%d" % b], LOAD + 1100 * (b + 1))
+    XP = ["X0", "X1", "X2", "X3", "C", "T1"]
+    NP = ["N0", "N1", "N2", "N3"]
+    XALL = XP + NP
 
     iota(T.pI[:], [[0, 1]], 0, 1, ["pI"])
-    iota(T.i8[:], [[-16, 8]], 0, 1, ["i8"])
-    vms(T.ones[:], 1.0, ["ones"])
-    vms(T.sel[:], 0.0, ["sel"])
-    vts(T.kI[:], T.pI[:], 15, ALU.bitwise_and, None, None, ["pI"], ["kI"])
-    vts(T.i8s[:], T.i8[:], 4, ALU.arith_shift_right, None, None, ["i8"], ["i8s"])
-    vts(T.parI[:], T.kI[:], 1, ALU.bitwise_and, None, None, ["kI"], ["parI"])
-    vcp(T.kcol[:], T.kI[:], ["kI"], ["kcol"])
-    vts(T.blkO[:], T.i8s[:], 0, ALU.is_equal, None, None, ["i8s"], ["blkO"])
-    vts(T.wcol[:], T.kI[:], 2.0, ALU.mult, 1.0, ALU.add, ["kI"], ["wcol"])
-    vts(T.offY[:], T.parI[:], -float(NOFF), ALU.mult, float(NOFF), ALU.add, ["parI"], ["offY"])
-    vts(T.oB[:], T.parI[:], float(NOFF), ALU.mult, -float(ZC), ALU.add, ["parI"], ["oB"])
-    vts(T.wb8[:], T.blkO[:], T.wcol[:, 0:1], ALU.mult, None, None, ["blkO", "wcol"], ["wb8"])
-    vts(T.s2c[:], T.kcol[:], 14.5, ALU.is_lt, None, None, ["kcol"], ["s2c"])
-    vts(T.s3c[:], T.kcol[:], 14.5, ALU.is_ge, float(ZC), ALU.add, ["kcol"], ["s3c"])
-    vms(T.XT[:, ZC:ZC + 16], 0.0, ["C"])
-    vms(T.zero[:], 0.0, ["zero"])
-    vms(T.XT[:, C15:C15 + 1], -2048.0, ["C"])
-    vms(T.bb[:, 0:16], 0.0, ["bbx"])
-    for b in range(8):
-        sact(T.sel[:, 16 * b:16 * b + 129 * 15 + 1:129], T.ones[:, 0:16], ACT.Copy, ["ones", "wb8", "sel"], ["selg%d" % b],
-             scale=T.wb8[:, b:b + 1])
-    SEL = ["sel"] + ["selg%d" % b for b in range(8)]
+    iota(T.iP[:], [[16, 8], [1000, 2], [2, 8]], 0, -1, ["iP"])
     iota(T.iD[:], [[1, 128]], 0, -1, ["iD"])
+    iota(T.iS[:], [[1, 144]], -15, -1, ["iS"])
     iota(T.iG[:], [[-16, 8], [0, 16]], 0, 1, ["iG"])
     iota(T.iR[:], [[0, 8], [1, 16]], 0, 0, ["iR"])
     iota(T.iB[:], [[1024, 4]], 0, 0, ["iB"])
     iota(T.iC[:], [[512, 4]], 32, 0, ["iC"])
     iota(T.Qb[:, 4096:4112], [[0, 16]], 256, 0, ["Qx"], True)
-    iota(T.XT[:, TRO:TRO + 4096], [[0, 4096]], 0, 0, ["T1"], True)
+    vms(T.XT[:, ZC:ZC + 16], 0.0, ["C"])
+    vms(T.XT[:, C15:C15 + 1], 2048.0, ["C"])
+    vms(T.XT[:, SP:AW:64], 0.0, ["T1"])
+    vms(T.zero[:], 0.0, ["zero"], 512)
+    vms(T.ones[:], 1.0, ["ones"])
+    vms(T.onesh[:], 1.0, ["onesh"])
+    vms(T.cU[:], 6144.0, ["cU"])
+    vms(T.cCap[:], -0.0625, ["cCap"])
+    vms(T.cPh[:], PART * math.exp(LAM + LOW) / 128, ["cPh"])
+    vms(T.ec[:], 0.0, ["ec"])
+    vms(T.ec[:, 0:16:5], 1.0, ["ec"])
+    for name, bits in (("kI", 15), ("parI", 1), ("i7", 7)):
+        vts(T[name][:], T.pI[:], bits, ALU.bitwise_and, None, None, ["pI"], [name])
+    for name, src, a, b in (("ma", "parI", NOFF, -NOFF), ("mc", "parI", -NOFF, NOFF + 2048), ("sa", "parI", -0.125, 0),
+                            ("sc0", "parI", 0.125, -0.0625), ("negk", "kI", -1, 0), ("kcol", "kI", 1, 0), ("wcol", "kI", 2, 1),
+                            ("wneg", "kI", -2, -1), ("w2", "kI", 4, 2), ("k64", "kI", 64, 0), ("bk", "kI", -LAM, LOW)):
+        vts(T[name][:], T[src][:], float(a), ALU.mult, float(b), ALU.add, [src], [name])
+    vts(T.lo7[:], T.i7[:], 7, ALU.is_equal, float(C15), ALU.mult, ["i7"], ["lo7"])
+    vts(T.hi7[:], T.i7[:], 7, ALU.is_equal, float(ZC), ALU.add, ["i7"], ["hi7"])
+    for par in range(2):
+        for b in range(2):
+            j = 2 * par + b
+            vts(T.prm[:, 128 * j:128 * j + 128], T.iP[:], 1000 * b - par, ALU.is_equal, None, None, ["iP"], ["perm%d" % j], c=128)
+    vts(T.identH[:], T.iD[:], 0, ALU.is_equal, None, None, ["iD"], ["identH"], c=128)
+    vts(T.I4k[:], T.iD[:], 0, ALU.is_equal, -4096.0, ALU.mult, ["iD"], ["I4k"], c=128)
+    for name, w in (("Wn", "wneg"), ("W2", "w2"), ("Wp", "wcol"), ("On", None)):
+        vts(T[name][:], T.iS[:], col("negk"), ALU.is_equal, col(w) if w else 1.0, ALU.mult, ["iS", "negk", w], [name], c=144)
+    for name, w in (("blkT", PART), ("blk16", -16.0), ("kmat", col("kcol"))):
+        vts(T[name][:], T.iG[:], col("kcol"), ALU.is_equal, w, ALU.mult, ["iG", "kcol"], [name], c=128)
+    vts(T.crow[:], T.iR[:], 0.125, ALU.mult, None, None, ["iR"], ["crow"], c=128)
+    vcp(T.jc[:], T.iC[:], ["iC"], ["jc"])
+    vts(T.base[:], T.iB[:], col("k64"), ALU.add, None, None, ["iB", "k64"], ["base"])
 
-    def lists(c=slice(0, 256)):
-        return [
-            lambda: vts(T.LA[:, c], T.E[:, c], T.offY[:, 0:1], ALU.add, None, None, ["E0", "E1", "offY"], ["LA"]),
-            lambda: sact(T.tE[:, c], T.E[:, c], ACT.Identity, ["E0", "E1", "oB"], ["tE"], bias=T.oB[:, 0:1]),
-            lambda: vtt(T.tM[:, c], T.tE[:, c], T.mB[:, c], ALU.mult, ["tE", "mB0", "mB1"], ["tM"]),
-            lambda: vts(T.LB[:, c], T.tM[:, c], T.s2c[:, 0:1], ALU.mult, T.s3c[:, 0:1], ALU.add, ["tM", "s2c", "s3c"], ["LB"]),
-        ]
+    def sel(name, k):
+        return T[name][:, 15 - k:143 - k]
 
-    def signs():
-        sact(T.sg[:], T.mB[:], ACT.Copy, ["mB0", "mB1"], ["sg0", "sg1"], bias=1.0, scale=-2.0)
+    E8 = ["E8_%d" % i for i in range(4)]
 
-    def neg(q, b, lo=0, hi=1024):
-        c = slice(b * 1024 + lo, b * 1024 + hi)
-        cn = slice(NOFF + b * 1024 + lo, NOFF + b * 1024 + hi)
-        if q == "V":
-            vts(T.XT[:, cn], T.XT[:, c], -1.0, ALU.mult, None, None, ["X%d" % b], ["N%d" % b])
-        else:
-            sact(T.XT[:, cn], T.XT[:, c], ACT.Copy, ["X%d" % b], ["N%ds" % b], scale=-1.0)
+    def lists():
+        vts(T.E16[:], T.E[:], -2048.0, ALU.add, None, None, EE, ["E16"], c=256)
+        vts(T.mA[:], T.mB[:], -float(NOFF), ALU.mult, NOFF + 2048.0, ALU.add, MM, ["mA"], c=128)
+        vts(T.mE[:], T.mB[:], col("ma"), ALU.mult, col("mc"), ALU.add, MM + ["ma", "mc"], ["mE"], c=128)
+        for bank, par, srcs in (("pU0", 0, ("E16", "mA")), ("pU1", 1, ("E16", "mA")), ("pY", 1, ("E16",))):
+            terms = [(s, b) for s in srcs for b in range(2)]
+            group([(T[bank][:, 0:128], T.prm[:, 128 * (2 * par + b):128 * (2 * par + b + 1)], T[s][:, b:256:2], i == 0,
+                    i == len(terms) - 1) for i, (s, b) in enumerate(terms)],
+                  list(srcs) + ["perm%d" % (2 * par), "perm%d" % (2 * par + 1)], [bank], [bank], 128)
+        group([(T.pE[:, 0:256], T.identH[:], T[s][:], s == "E16", s == "mE") for s in ("E16", "mE")], ["identH", "E16", "mE"],
+              E8, ["pE"], 256)
+        vts(T.LL[:, 256:384], T.pU1[:, 0:128], col("lo7"), ALU.max, col("hi7"), ALU.min, ["pU1", "lo7", "hi7"], ["LB"], ["pU1"], 128)
+        vcp(T.LL[:, 0:128], T.pU0[:, 0:128], ["pU0"], ["LE"], ["pU0"], 128)
+        vts(T.LL[:, 128:256], T.pY[:, 0:128], 2048.0, ALU.add, None, None, ["pY"], ["LX"], ["pY"], 128)
+        sact(T.sg[:], T.mB[:], ACT.Identity, MM + ["sa", "sc0"], ["sg"], bias=col("sc0"), scale=col("sa"), c=256)
 
-    late = [
-        lambda: vts(T.w256[:], T.kcol[:], -1.0, ALU.mult, 256.0, ALU.add, ["kcol"], ["w256"]),
-        lambda: vts(T.ident[:], T.iD[:], 0, ALU.is_equal, None, None, ["iD"], ["ident"]),
-        lambda: vts(T.blkE[:], T.blkO[:], -1.0, ALU.mult, None, None, ["blkO"], ["blkE"]),
-        lambda: vts(T.iGs[:], T.iG[:], 4, ALU.arith_shift_right, None, None, ["iG"], ["iGs"]),
-        lambda: vts(T.Pd[:], T.ident[:], T.w256[:, 0:1], ALU.mult, None, None, ["ident", "w256"], ["Pd"]),
-        lambda: vts(T.tri[:], T.iD[:], 0, ALU.is_ge, -16.0, ALU.mult, ["iD"], ["tri"]),
-        lambda: vts(T.kmat[:], T.iGs[:], 0, ALU.is_equal, T.kcol[:, 0:1], ALU.mult, ["iGs", "kcol"], ["kmat"]),
-        lambda: vts(T.crow[:], T.iR[:], 0.125, ALU.mult, None, None, ["iR"], ["crow"]),
-        lambda: vms(T.Ct[:], 16384.0, ["Ct"]),
-        lambda: vms(T.ecb[:], 0.0, ["ecb"]),
-        lambda: vts(T.k64[:], T.kcol[:], 64.0, ALU.mult, None, None, ["kcol"], ["k64"]),
-        lambda: vms(T.Ct[:, 0:128:16], 0.5, ["Ct"]),
-        lambda: vms(T.ecb[:, 0:16:5], 1.0, ["ecb"]),
-        lambda: vcp(T.jc[:], T.iC[:], ["iC"], ["jc"]),
-        lambda: vts(T.base[:], T.iB[:], T.k64[:, 0:1], ALU.add, None, None, ["iB", "k64"], ["base"]),
-        lambda: vcp(T.ec[:], T.ecb[:], ["ecb"], ["ec"]),
-        lambda: vcp(T.onesh[:], T.ones[:], ["ones"], ["onesh"]),
-        lambda: vms(T.all16[:], -16.0, ["all16"]),
-    ]
-    vts(T.sgn[:], T.parI[:], 2.0, ALU.mult, -1.0, ALU.add, ["parI"], ["sgn"])
-    vcp(T.E[:], T.ledI[:], ["ledI"], ["E0", "E1"])
-    do(lists(), late[0:3])
-    signs()
-    neg("S", 1)
-    neg("V", 0)
-    do(late[3:10])
-    neg("V", 2)
-    do(late[10:])
-    neg("S", 3, 0, 320)
-    neg("V", 3, 320, 1024)
-
-    def ce(i):
-        return slice(i * 1024, (i + 1) * 1024)
+    vcp(T.E[:], T.ledI[:], ["ledI"], EE, c=256)
+    lists()
+    for b in range(4):
+        vts(T.XT[:, NOFF + b * 1024:NOFF + (b + 1) * 1024], T.XT[:, b * 1024:(b + 1) * 1024], -1.0, ALU.mult, None, None,
+            ["X%d" % b], ["N%d" % b], c=512)
 
     def ca(i):
         return slice(i * 64, (i + 1) * 64)
 
+    def ce(i, par=None):
+        return slice(i * 1024, (i + 1) * 1024) if par is None else slice(i * 1024 + par, (i + 1) * 1024, 2)
+
+    def ch(i):
+        return slice(i * 512, (i + 1) * 512)
+
     def cb(b):
         return slice(b * 128, (b + 1) * 128)
 
-    def gather(q, out, lst, i, R, W):
-        src = T.XT[:, 0:GW].indirect(lst[:, ca(i)])
-        if q == "V":
-            vcp(out[:, ce(i)], src, R + XALL, W)
+    def lst(n, i):
+        return T.LL[:, 128 * n + 32 * i:128 * n + 32 * i + 32]
+
+    def line(buf, i, k):
+        return buf[:, i * 1024 + k:(i + 1) * 1024:16]
+
+    def amounts(i):
+        s = str(i)
+        src = T.XT[:, 0:GW].indirect(lst(0, i))
+        if OPT["gE"][i] == "V":
+            vcp(T.Qb[:, ce(i, 0)], src, ["LE"] + XALL, ["Qe" + s], c=gat(512))
         else:
-            sact(out[:, ce(i)], src, ACT.Copy, R + XALL, W)
-
-    def gA(q, i):
-        gather(q, T.Ab, T.LA, i, ["LA"], ["A%d" % i])
-
-    def gB(q, i):
-        gather(q, T.Bb, T.LB, i, ["LB"], ["B%d" % i])
-
-    def scans(i):
-        o = slice(i * 1024 + 16, (i + 1) * 1024 + 16)
-        p = slice(i * 1024 + 15, (i + 1) * 1024 + 15)
-        return [
-            lambda: op("V", lambda: V.tensor_tensor_scan(T.bb[:, o], T.Bb[:, ce(i)], T.zero[:], 0.0, ALU.add, ALU.max),
-                       ["B%d" % i, "zero"], ["bb%d" % i]),
-            lambda: op("V", lambda: V.tensor_tensor_scan(T.Qb[:, ce(i)], T.bb[:, p], T.Ab[:, ce(i)], 0.0, ALU.max, ALU.min),
-                       ["bb%d" % i, "bbx" if i == 0 else "bb%d" % (i - 1), "A%d" % i], ["Q%d" % i]),
-        ]
-
-    def over(q, i):
-        if q == "V":
-            vts(T.pb[:, ce(i)], T.Qb[:, ce(i)], -1.0, ALU.max, 1.0, ALU.min, ["Q%d" % i], ["p%d" % i])
+            sact(T.Qb[:, ce(i, 0)], src, ACT.Copy, ["LE"] + XALL, ["Qe" + s], c=gat(512))
+        src = T.XT[:, 0:SP].indirect(lst(2, i))
+        if OPT["gB"][i] == "V":
+            vts(T.Bb[:, ce(i, 1)], src, -1.0, ALU.mult, None, None, ["LB"] + XP, ["Bo" + s], c=gat(512))
         else:
-            sact(T.pb[:, ce(i)], T.Qb[:, ce(i)], ACT.Sign, ["Q%d" % i], ["p%d" % i])
-
-    def group(calls, R, W, B):
-        def f():
-            r = None
-            for c in calls:
-                r = P.matmul(*c)
-            return r
-        op("P", f, R, W, B)
-
-    UB = (("pU0", 0), ("pU1", 0), ("pU0", 0), ("pU0", 64))
-
-    def pU(i):
-        n, o = UB[i]
-        group([(T[n][:, o:o + 64], T.sel[:, 128 * k:128 * (k + 1)], T.Qb[:, i * 1024 + k:(i + 1) * 1024:16], k == 0, k == 15)
-               for k in range(16)], SEL + ["Q%d" % i], ["u%d" % i], [n])
-
-    def hchain(cs, t):
-        n = UB[cs[0]][0]
-        a = slice(cs[0] * 64, cs[-1] * 64 + 64)
-        p = T[n][:, 0:64 * len(cs)]
-        s = str(cs[0])
-        e = "E%d" % (cs[0] // 2)
-        ek = T.E if t == 0 else T.Ek
-        return [
-            lambda: vts(T.uI[:, a], p, T.sgn[:, 0:1], ALU.mult, None, None, ["u%d" % i for i in cs] + ["sgn"], ["uI" + s], [n]),
-            lambda: vts(T.uA[:, a], T.uI[:, a], 4095, ALU.bitwise_and, None, None, ["uI" + s], ["uA" + s]),
-            lambda: vtt(T.eu[:, a], T.E[:, a], T.uA[:, a], ALU.mult, ["uA" + s, e], ["eu" + s]),
-            lambda: vts(T.wv[:, a], T.eu[:, a], 5, ALU.arith_shift_right, 4095, ALU.bitwise_and, ["eu" + s], ["wv" + s]),
-            lambda: vtt(T.hs[:, a], T.wv[:, a], ek[:, a], ALU.add, ["wv" + s, e if t == 0 else "Ek"], ["hs" + s]),
-            lambda: vts(T.hI[:, a], T.hs[:, a], 4095, ALU.bitwise_and, None, None, ["hs" + s], ["hI%d" % i for i in cs]),
-            lambda: vts(T.LY[:, a], T.hI[:, a], T.offY[:, 0:1], ALU.add, None, None, ["hI%d" % cs[0], "offY"],
-                        ["LY%d" % i for i in cs]),
-        ]
-
-    def ysub(i, part=None):
-        lo, hi = (0, 64) if part is None else (32 * part, 32 * part + 32)
-        a = slice(i * 64 + lo, i * 64 + hi)
-        c = slice(a.start * 16, a.stop * 16)
-        vtt(T.zb[:, c], T.XT[:, 0:GW].indirect(T.LY[:, a]), T.Qb[:, c], ALU.subtract,
-            ["LY%d" % i, "Q%d" % i] + XALL, ["z%d" % i if part is None or part == 1 else "z%da" % i])
-
-    def sign(q, i):
-        if q == "V":
-            vts(T.sb[:, ce(i)], T.zb[:, ce(i)], -1.0, ALU.max, 1.0, ALU.min, ["z%d" % i, "z%da" % i], ["s%d" % i])
+            sact(T.Bb[:, ce(i, 1)], src, ACT.Copy, ["LB"] + XP, ["Bo" + s], scale=-1.0, c=gat(512))
+        if OPT["relu"][i] == "V":
+            vts(T.Bb[:, ce(i, 0)], T.Qb[:, ce(i, 0)], 0.0, ALU.max, None, None, ["Qe" + s], ["Be" + s], c=256)
         else:
-            sact(T.sb[:, ce(i)], T.zb[:, ce(i)], ACT.Sign, ["z%d" % i, "z%da" % i], ["s%d" % i])
+            sact(T.Bb[:, ce(i, 0)], T.Qb[:, ce(i, 0)], ACT.Relu, ["Qe" + s], ["Be" + s], c=512)
+        vscan(T.bb[:, ce(i)], T.Bb[:, ce(i)], T.zero[:], 0.0, ALU.add, ALU.max, ["Be" + s, "Bo" + s, "zero"], ["bb" + s], 512)
+        vtt(T.Qb[:, ce(i, 1)], T.XT[:, 0:4096].indirect(lst(1, i)), T.bb[:, ce(i, 0)], ALU.min, ["LX", "bb" + s] + XP, ["Qo" + s],
+            c=gat(512))
+        vts(T.pe[:, ch(i)], T.Qb[:, ce(i, 0)], 0.0, ALU.not_equal, None, None, ["Qe" + s], ["pe" + s], c=256)
+        if OPT["over"][i] == "V":
+            vts(T.po[:, ch(i)], T.Qb[:, ce(i, 1)], 1.0, ALU.min, None, None, ["Qo" + s], ["po" + s], c=256)
+        else:
+            sact(T.po[:, ch(i)], T.Qb[:, ce(i, 1)], ACT.Sign, ["Qo" + s], ["po" + s], c=512)
 
-    def sums(ps, src, tag, b):
-        group([(T[ps][:, b * 128 + k:(b + 1) * 128:16], src[:, b * 2048 + k:(b + 1) * 2048:16],
-                (T.blkE if k % 2 == 0 else T.blkO)[:], True, True) for k in range(16)],
-              [tag + str(2 * b), tag + str(2 * b + 1), "blkE", "blkO"], [ps + str(b)], [ps])
+    def hashes(i, t):
+        n = "pU%d" % (i % 2)
+        o, a, s = T[n][:, 0:64], ca(i), str(i)
+        mms = [(o, T.cU[:], T.ones[:, 0:64], True, False)]
+        for k in range(0, 16, 2):
+            mms += [(o, sel("Wn", k), line(T.Qb, i, k), False, False), (o, sel("W2", k), line(T.Bb, i, k), False, False)]
+        group(mms, ["cU", "ones", "Wn", "W2", "Qe" + s, "Be" + s], [n], [n])
+        group([(o, sel("Wp", k), line(T.Qb, i, k), False, k == 15) for k in range(1, 16, 2)], ["Wp", "Qo" + s], [n], [n])
+        if OPT["cc"][i] == "V":
+            vts(T.cc[:, a], o, -2047.5, ALU.add, None, None, [n], ["cc" + s], [n])
+        else:
+            sact(T.cc[:, a], o, ACT.Copy, [n], ["cc" + s], [n], bias=-2047.5)
+        vtt(o, o, T.cc[:, a], ALU.subtract, [n, "cc" + s], [n], [n])
+        ek = T.pE[:, a] if t == 0 else T.pE[:, 256 + 64 * i:256 + 64 * i + 64]
+        vtt(T.eu[:, a], o, T.E[:, a], ALU.mult, [n, "E%d" % (i // 2)], ["eu" + s], [n])
+        vts(T.wv[:, a], T.eu[:, a], 5, ALU.arith_shift_right, 4095, ALU.bitwise_and, ["eu" + s], ["wv" + s])
+        vtt(T.hs[:, a], ek, T.wv[:, a], ALU.add, ["wv" + s, "E8_" + s, "Ek"], ["hs" + s], ["pE"])
+        vts(T.hm[:, a], T.hs[:, a], 4095 + NOFF, ALU.bitwise_and, None, None, ["hs" + s], ["hm" + s])
+        vcp(T.LY[:, a], T.hm[:, a], ["hm" + s], ["LY" + s])
 
-    def pGK():
-        group([(T.pGK[:, cb(b)], T.sg[:, cb(b)], T.Pd[:], True, True) for b in range(2)], ["sg0", "sg1", "Pd"], ["pGK"], ["pGK"])
+    def bank(b):
+        return "pA" if b == 0 else "pB"
 
-    def dec_over(b):
-        s = str(b)
-        return [
-            lambda: vts(T.ov[:, cb(b)], T.pOV[:, cb(b)], 8.5, ALU.is_ge, None, None, ["pOV" + s], ["ov" + s], ["pOV"]),
-            lambda: vtt(T.gov[:, cb(b)], T.pGK[:, cb(b)], T.ov[:, cb(b)], ALU.mult, ["pGK", "ov" + s], ["gov" + s], ["pGK"]),
-        ]
+    def scores(i):
+        s = str(i)
+        for j in (2 * i, 2 * i + 1):
+            c, z = ch(j), "z%d" % j
+            src = T.XT[:, 0:GW].indirect(T.LY[:, 32 * j:32 * j + 32])
+            if OPT["y"][j] == "V":
+                vtt(T.zb[:, c], src, T.Qb[:, c], ALU.subtract, ["LY" + s, "Qe" + s, "Qo" + s] + XALL, [z], c=gat(512))
+                if OPT["sign"][j] == "V":
+                    vts(T.sb[:, c], T.zb[:, c], -1.0, ALU.max, 1.0, ALU.min, [z], ["s%d" % j], c=256)
+                else:
+                    sact(T.sb[:, c], T.zb[:, c], ACT.Sign, [z], ["s%d" % j], c=512)
+            else:
+                sact(T.zb[:, c], src, ACT.Copy, ["LY" + s] + XALL, [z], scale=-1.0, c=gat(512))
+                group([(T.pY[:], T.I4k[:], T.Qb[:, c], True, False), (T.pY[:], T.I4k[:], T.zb[:, c], False, True)],
+                      ["I4k", z, "Qe" + s, "Qo" + s], ["pY"], ["pY"], 512)
+                sact(T.sb[:, c], T.pY[:], ACT.Sign, ["pY"], ["s%d" % j], ["pY"], c=512)
+        n = bank(i // 2)
+        o = T[n][:, 64 * (i % 2):64 * (i % 2) + 64]
+        group([(o, sel("On", k), line(T.sb, i, k), k == 0, k == 15) for k in range(16)], ["On", "s%d" % (2 * i), "s%d" % (2 * i + 1)],
+              ["pS" + s], [n])
 
     def decide(b):
-        s = str(b)
-        c = cb(b)
-
-        def places():
-            sact(T.flipX[:, c], T.R2[:, c], ACT.Sign, ["R2" + s], ["fl" + s], bias=-0.5)
-
-        def winners():
-            vtt(T.win[:, c], T.comp[:, c], T.R2[:, c], ALU.is_equal, ["comp" + s, "R2" + s], ["win" + s])
-            group([(T.pWN[:, c], T.win[:, c], T.ident[:], True, True)], ["win" + s, "ident"], ["pWN" + s], ["pWN"])
-            calls = [(T.pZ[:, c], T.ones[:], T.crow[:], True, False), (T.pZ[:, c], T.tri[:], T.flipX[:, c], False, False)]
-            R = ["tri", "fl" + s, "ones", "crow"]
-            if b == 1:
-                calls.append((T.pZ[:, c], T.all16[:], T.flipX[:, cb(0)], False, False))
-                R += ["all16", "fl0"]
-            group(calls, R, ["pZ" + s], ["pZ"])
-            sact(T.wsb[:, c], T.pWN[:, c], ACT.Copy, ["pWN" + s], ["wsb" + s], ["pWN"])
-            group([(T.pZ[:, c], T.wsb[:, c], T.kmat[:], False, True)], ["wsb" + s, "kmat"], ["pZ" + s], ["pZ"])
-
-        def scan(dst, src, w, r):
-            op("V", lambda: V.tensor_tensor_scan(dst[:, c], T.Ct[:], src[:, c], 0.5, ALU.min, ALU.max), ["Ct", r], [w])
-
-        return [
-            lambda: vtt(T.comp[:, c], T.pS[:, c], T.gov[:, c], ALU.mult, ["pS" + s, "gov" + s], ["comp" + s], ["pS"]),
-            lambda: scan(T.R1, T.comp, "R1" + s, "comp" + s),
-            lambda: vcp(T.R1[:, b * 128:(b + 1) * 128:16], T.R1[:, b * 128 + 15:(b + 1) * 128:16], ["R1" + s], ["R1" + s]),
-            lambda: (scan(T.R2, T.R1, "R2" + s, "R1" + s), places()),
-            winners,
-        ]
-
-    def clamps(b):
-        s = str(b)
-
-        def one(c):
-            lo = -(256.0 * c + 16)
-            o = slice(c * 256 + b * 128, c * 256 + (b + 1) * 128)
-            vts(T.D[:, o], T.pZ[:, cb(b)], lo, ALU.max, lo + 16, ALU.min, ["pZ" + s], ["D%d%d" % (c, b)], ["pZ"])
-        return [lambda c=c: one(c) for c in range(4)]
-
-    def pLJ(b):
-        calls = [] if b else [(T.pSM[:, 0:4], T.onesh[:], T.jc[:], True, False)]
-        for c in range(4):
-            calls.append((T.pSM[:, 0:4], T.D[:, c * 256 + b * 128:c * 256 + (b + 1) * 128], T.ec[:, 4 * c:4 * c + 4], False,
-                          b == 1 and c == 3))
-        group(calls, ["onesh", "jc", "ec"] + ["D%d%d" % (c, b) for c in range(4)], ["LJp"], ["pSM"])
+        n, c, s = bank(b), cb(b), str(b)
+        for i in (2 * b, 2 * b + 1):
+            o = T[n][:, 128 + 64 * (i % 2):192 + 64 * (i % 2)]
+            mms = [(o, T.cCap[:], T.ones[:, 0:64], True, False)]
+            mms += [(o, sel("On", k), (T.po if k % 2 else T.pe)[:, i * 512 + k // 2:(i + 1) * 512:8], False, k == 15) for k in range(16)]
+            group(mms, ["cCap", "ones", "On", "pe%d" % i, "po%d" % i], ["cap%d" % i], [n])
+        two = ["%d" % (2 * b), "%d" % (2 * b + 1)]
+        vtt(T.ts[:, c], T[n][:, 0:128], T.sg[:, c], ALU.mult, ["pS" + x for x in two] + ["sg"], ["ts" + s], [n], 128)
+        vtt(T.comp[:, c], T[n][:, 128:256], T.ts[:, c], ALU.min, ["cap" + x for x in two] + ["ts" + s], ["comp" + s], [n], 128)
+        sact(T.val[:, c], T.comp[:, c], ACT.Exp, ["comp" + s, "bk"], ["val" + s], bias=col("bk"), scale=16 * 17 * LAM, c=128)
+        o = T[n][:, 256:384]
+        group([(o, T.cPh[:], T.ones[:], True, False), (o, T.blkT[:], T.val[:, c], False, True)],
+              ["cPh", "ones", "blkT", "val" + s], ["sum" + s], [n], 128)
+        vtt(T.win[:, c], o, T.val[:, c], ALU.is_lt, ["sum" + s, "val" + s], ["win" + s], [n], 128)
+        vscan(T.cum[:, c], T.win[:, c], T.zero[:, 0:128], 0.0 if b == 0 else T.cum[:, 127:128], ALU.add, ALU.add,
+              ["win" + s, "zero"] + ["cum0"] * b, ["cum" + s])
+        o = T.pZ[:, c]
+        group([(o, T.ones[:], T.crow[:], True, False), (o, T.win[:, c], T.kmat[:], False, False),
+               (o, T.cum[:, c], T.blk16[:], False, True)], ["ones", "crow", "kmat", "blk16", "win" + s, "cum" + s],
+              ["pZ" + s], ["pZ"], 128)
+        mms = [] if b else [(T.pSM[:, 0:4], T.onesh[:], T.jc[:], True, False)]
+        for j in range(4):
+            lo = -(256.0 * j + 16)
+            d = T.D[:, j * 256 + b * 128:j * 256 + (b + 1) * 128]
+            vts(d, o, lo, ALU.max, lo + 16, ALU.min, ["pZ" + s], ["D%d%d" % (j, b)], ["pZ"], 128)
+            mms.append((T.pSM[:, 0:4], d, T.ec[:, 4 * j:4 * j + 4], False, b == 1 and j == 3))
+        group(mms, ["onesh", "jc", "ec"] + ["D%d%d" % (j, b) for j in range(4)], ["pSM"], ["pSM"])
 
     def send(t):
-        vcp(T.LJ[:], T.pSM[:, 0:4], ["LJp"], ["LJ"], ["pSM"])
+        vcp(T.LJ[:], T.pSM[:, 0:4], ["pSM"], ["LJ"], ["pSM"])
         qn = "qs%d" % t
-        sact(T[qn][:], T.Qb[:].indirect(T.LJ[:, 0:4]), ACT.Abs, ["LJ", "Qx", "Q0", "Q1", "Q2", "Q3"], [qn])
-        dst = T.cores[(rank + 1 + t % (n_ranks - 1)) % n_ranks]
-        rid, pid, _ = topo.addr(dst)
-        eng = topo.engines(core, dst)[:NENG]
-        depends("G", [qn], [], ())
-        g.remote_dma(T["land%d" % t][:], T[qn][:], T.sem["arr%d" % t], T.sem.sent, pid, rid, sum(1 << e for e in eng))
-        count["sent"] = count.get("sent", 0) + len(eng)
-        src = T.cores[(rank - 1 - t % (n_ranks - 1)) % n_ranks]
-        note("R", "arr%d" % t, len(topo.engines(src, core)[:NENG]), [], ["land%d" % t], (), {})
-
-    def kappa():
-        group([(T.pU1[:, 64:72], T.ones[:], T.flipX[:, b * 128:(b + 1) * 128:16], b == 0, b == 1) for b in range(2)],
-              ["ones", "fl0", "fl1"], ["kp"], ["pU1"])
-
-    def kappa2():
-        return [
-            lambda: op("V", lambda: V.tensor_reduce(T.kr[:], T.pU1[:, 64:72], AxisListType.X, ALU.add), ["kp"], ["kr"], ["pU1"]),
-            lambda: vcp(T.kri[:], T.kr[:], ["kr"], ["kri"]),
-            lambda: vts(T.krm[:], T.kri[:], 31, ALU.bitwise_and, None, None, ["kri"], ["krm"]),
-            lambda: vcp(T.kap[:], T.krm[:], ["krm"], ["kap"]),
-        ]
-
-    def ekappa():
-        sact(T.Ek[:], T.E[:], ACT.Identity, ["E0", "E1", "kap"], ["Ek"], bias=T.kap[:, 0:1])
+        sact(T[qn][:], T.Qb[:].indirect(T.LJ[:, 0:4]), ACT.Abs, ["LJ", "Qx"] + ["Q%s%d" % (x, i) for x in "eo" for i in range(4)], [qn],
+             c=gat(64))
+        calls.append(("G", 300, FLIGHT, [qn], ["land%d" % t], (), ("send", t)))
 
     def update(b):
-        c = cb(b)
-        s = str(b)
-        return [
-            lambda: vtt(T.dh[:, c], T.hI[:, c], T.E[:, c], ALU.subtract, ["hI%d" % (2 * b), "hI%d" % (2 * b + 1), "E" + s], ["dh" + s]),
-            lambda: vtt(T.wM[:, c], T.pWN[:, c], T.sg[:, c], ALU.mult, ["pWN" + s, "sg" + s], ["wM" + s], ["pWN"]),
-            lambda: vtt(T.wE[:, c], T.pWN[:, c], T.dh[:, c], ALU.mult, ["pWN" + s, "dh" + s], ["wE" + s], ["pWN"]),
-            lambda: vtt(T.mB[:, c], T.mB[:, c], T.wM[:, c], ALU.add, ["mB" + s, "wM" + s], ["mB" + s]),
-            lambda: vtt(T.E[:, c], T.E[:, c], T.wE[:, c], ALU.add, ["E" + s, "wE" + s], ["E" + s]),
-        ]
+        c, s = cb(b), str(b)
+        e8 = E8[2 * b:2 * b + 2]
+        vtt(T.pE[:, c], T.hm[:, c], T.pE[:, c], ALU.subtract, e8 + ["hm%d" % i for i in (2 * b, 2 * b + 1)], e8, ["pE"], 128)
+        vtt(T.wE[:, c], T.pE[:, c], T.win[:, c], ALU.mult, e8 + ["win" + s], ["wE" + s], ["pE"], 128)
+        vtt(T.mB[:, c], T.mB[:, c], T.win[:, c], ALU.not_equal, ["mB" + s, "win" + s], ["mB" + s], c=256)
+        vtt(T.E[:, c], T.E[:, c], T.wE[:, c], ALU.add, ["E" + s, "wE" + s], ["E" + s], c=256)
+
+    def kappa():
+        group([(T.pZ[:, 256:257], T.ones[:], T.cum[:, 255:256], True, True)], ["ones", "cum1"], ["kp"], ["pZ"])
+        vcp(T.kri[:], T.pZ[:, 256:257], ["kp"], ["kri"], ["pZ"])
+        vts(T.krm[:], T.kri[:], 31, ALU.bitwise_and, None, None, ["kri"], ["krm"])
+        vcp(T.kap[:], T.krm[:], ["krm"], ["kap"])
+        sact(T.pE[:, 256:512], T.pE[:, 0:256], ACT.Identity, ["kap"] + E8, ["Ek"], ["pE"], bias=col("kap"), c=256)
 
     def arrive(t, last):
         ln = "land%d" % t
-        group([(T.pSM[:, 32:36], T.sel[:, 128 * r:128 * (r + 1)], T[ln][:, r:64:16], r == 0, r == 15) for r in range(16)],
-              SEL + [ln], ["pA"], ["pSM"])
-        vcp(T.vi[:], T.pSM[:, 32:36], ["pA"], ["vi"], ["pSM"])
-        vts(T.vinv[:], T.pSM[:, 32:36], 65535.5, ALU.is_ge, float(TRO), ALU.mult, ["pA"], ["vinv"], ["pSM"])
+        group([(T.pSM[:, 32:36], sel("Wp", r), T[ln][:, r:64:16], r == 0, r == 15) for r in range(16)], ["Wp", ln], ["pSM"], ["pSM"])
+        vcp(T.vi[:], T.pSM[:, 32:36], ["pSM"], ["vi"], ["pSM"])
+        vts(T.vinv[:], T.pSM[:, 32:36], 65535.5, ALU.is_ge, float(SP), ALU.mult, ["pSM"], ["vinv"], ["pSM"])
         vts(T.vm[:], T.vi[:], 63, ALU.bitwise_and, None, None, ["vi"], ["vm"])
         vtt(T.vbs[:], T.vinv[:], T.base[:], ALU.add, ["vinv", "base"], ["vbs"])
         vtt(T.vid[:], T.vm[:], T.vbs[:], ALU.add, ["vm", "vbs"], ["vid"])
-        vcp(T.LI[:, 0:4], T.vid[:], ["vid"], ["LI"])
-        if not last:
-            vts(T.LI[:, 4:8], T.vid[:], float(NOFF), ALU.add, None, None, ["vid"], ["LI2"])
-        vtt(T.tx[:], T.XT[:, 0:TRO + 4096].indirect(T.LI[:, 0:4]), T[ln][:], ALU.add, ["LI", ln, "T1"] + XALL, ["tx"])
+        vcp(T.LI[:], T.vid[:], ["vid"], ["LI"])
+        vtt(T.tx[:], T.XT[:, 0:AW].indirect(T.LI[:, 0:4]), T[ln][:], ALU.add, ["LI", ln] + XP, ["tx"], c=gat(64))
         vts(T.ND[:, 0:64], T.tx[:], 0.5, ALU.mult, -0.25, ALU.add, ["tx"], ["ND0"])
-        xw = XALL[:10] + ["T1"]
-        if last:
-            op("V", lambda: V.tensor_copy(T.XT[:, 0:WEND].indirect(T.LI[:, 0:4]), T.ND[:, 0:64]), ["LI", "ND0"], xw)
-        else:
+        vcp(T.XT[:, 0:AW].indirect(T.LI[:, 0:4]), T.ND[:, 0:64], ["LI", "ND0"], XP, c=60 + 64 * SCATTER)
+        if not last:
             vts(T.ND[:, 64:128], T.tx[:], -0.5, ALU.mult, 0.25, ALU.add, ["tx"], ["ND1"])
-            op("V", lambda: V.tensor_copy(T.XT[:, 0:WEND].indirect(T.LI[:, 0:8]), T.ND[:]), ["LI", "LI2", "ND0", "ND1"], xw)
+            vcp(T.XT[:, NOFF:WEND].indirect(T.LI[:, 0:4]), T.ND[:, 64:128], ["LI", "ND1"], NP, c=60 + 64 * SCATTER)
 
     for t in range(rounds):
         last = t == rounds - 1
-        gA("V", 0)
-        gB("S", 0)
-        gB("S", 1)
-        do(scans(0))
-        pU(0)
-        gA("V", 1)
-        if t == 0:
-            pGK()
-        gA("S", 2)
-        gB("S", 2)
-        gA("S", 3)
-        gB("S", 3)
-        h0 = hchain((0,), t)
-        do(h0[:3])
-        do(scans(1), h0[3:5])
-        pU(1)
-        do(h0[5:])
-        ysub(0)
-        over("S", 0)
-        over("S", 1)
-        sums("pOV", T.pb, "p", 0)
-        h1 = hchain((1,), t)
-        do(h1[:3])
-        do(scans(2), h1[3:5])
-        pU(2)
-        do(h1[5:])
-        sign("S", 0)
-        do(scans(3))
-        pU(3)
-        ysub(1)
-        sign("S", 1)
-        over("S", 2)
-        over("S", 3)
-        sums("pS", T.sb, "s", 0)
-        d0 = dec_over(0) + decide(0)
-        h23 = hchain((2, 3), t)
-        do(h23, d0[0:2])
-        ysub(2, 0)
-        d0[2]()
-        ysub(2, 1)
-        sign("S", 2)
-        d0[3]()
-        ysub(3, 0)
-        d0[4]()
-        sums("pOV", T.pb, "p", 1)
-        d1 = dec_over(1) + decide(1)
-        d1[0]()
-        d0[5]()
-        d1[1]()
-        d0[6]()
-        ysub(3, 1)
-        u0 = update(0)
-        sign("V", 3)
-        sums("pS", T.sb, "s", 1)
-        do(clamps(0))
-        pLJ(0)
-        do(u0[0:1])
-        do(d1[2:], u0[1:])
-        do(clamps(1))
-        pLJ(1)
-        u1 = update(1)
-        if not last:
-            kappa()
-        do(u1[0:3])
+        for i in range(4):
+            amounts(i)
+            hashes(i, t)
+            scores(i)
+        for b in range(2):
+            decide(b)
+            update(b)
         send(t)
-        do(u1[3:])
         if last:
-            dma("Y", T.ym[:], T.mB[:], ["mB0", "mB1"], ["ym"])
-            dma("S", T.yl[:], T.E[:], ["E0", "E1"], ["yl"])
+            dma("Y", T.ym[:], T.mB[:], MM, ["ym"], LOAD)
+            dma("S", T.yl[:], T.E[:], EE, ["yl"], LOAD)
         else:
-            do(lists(), kappa2())
-            signs()
-            ekappa()
-            pGK()
+            lists()
+            kappa()
         arrive(t, last)
     for b in range(2):
         c = slice(b * 2048, (b + 1) * 2048)
-        dma("YS"[b], T.yx[:, c], T.XT[:, c], ["X%d" % (2 * b), "X%d" % (2 * b + 1)], ["yx%d" % b])
+        dma("YS"[b], T.yx[:, c], T.XT[:, c], ["X%d" % (2 * b), "X%d" % (2 * b + 1)], ["yx%d" % b], LOAD + 2000)
+
+    count = {}
+    known = {q: {} for q in Q}
+    lastw, readers, banks = {}, {}, {}
+    n_dma = 0
+    for seq, i in enumerate(in_order(calls)):
+        q, _, _, R, W, B, f = calls[i]
+        toks = [lastw[x] for x in list(R) + list(W) if x in lastw]
+        toks += [y for x in W for y in readers.get(x, [])]
+        toks += [y for b in B for qq, y in banks.get(b, {}).items() if qq != q]
+        k = known[q]
+        for sem, val, _, snap, _ in sorted(toks, key=lambda y: -y[4]):
+            if k.get(sem, 0) < val:
+                Q[q].wait_ge(T.sem[sem], val)
+                for s, v in list(snap.items()) + [(sem, val)]:
+                    k[s] = max(k.get(s, 0), v)
+        snap = dict(k)
+        if isinstance(f, tuple) and f[0] == "send":
+            t = f[1]
+            step = 1 + t % (n_ranks - 1)
+            dst, src = T.cores[(rank + step) % n_ranks], T.cores[(rank - step) % n_ranks]
+            rid, pid, _ = topo.addr(dst)
+            eng = topo.engines(core, dst)[:NENG]
+            g.remote_dma(T["land%d" % t][:], T["qs%d" % t][:], T.sem["arr%d" % t], T.sem.sent, pid, rid, sum(1 << e for e in eng))
+            count["sent"] = count.get("sent", 0) + len(eng)
+            q, sem, n, R, snap = "R", "arr%d" % t, len(topo.engines(src, core)[:NENG]), [], {}
+        elif isinstance(f, tuple):
+            sem, n = "d%d" % n_dma, 16
+            n_dma += 1
+            Q[q].dma_start(f[1], f[2]).then_inc(T.sem[sem], n)
+        else:
+            sem, n = "c" + q, 1
+            f().then_inc(T.sem[sem], n)
+        count[sem] = count.get(sem, 0) + n
+        tok = (sem, count[sem], q, snap, seq)
+        for x in R:
+            readers.setdefault(x, []).append(tok)
+        for x in W:
+            lastw[x], readers[x] = tok, []
+        for b in B:
+            banks.setdefault(b, {})[q] = tok
     for sem, n in count.items():
         if known["G"].get(sem, 0) < n:
             g.wait_ge(T.sem[sem], n)

@@ -1,44 +1,48 @@
 import math
 from concourse.mybir import AluOpType as ALU, ActivationFunctionType as ACT
 
-ZC, C15, SP, NOFF = 4096, 4097, 4112, 16384
+ZC, C15, SP, NOFF = 4096, 4097, 4160, 16384
 GW = NOFF + 4096
 AW = SP + 4096
 WEND = NOFF + AW
 NENG = 8
 LAM, LOW, PART = 0.6, -78.0, 0.4
+BIG = float(2 ** 24)
 
-OPT = dict(cc="VVVV", gE="VSSS", gB="SSSS", relu="VSSS", over="SSSS", y="SVSVVVVV", sign="SSSSSSVV")
-GATHER, SCATTER, MATMUL, WAKE, LOAD, FLIGHT, SLACK = 1.5, 3.8, 0.5, 150, 2400, 3000, 100
-SWEEPS = 4
+OPT = dict(cc="SSSS", gE="VSSS", gB="SSSS", relu="VVVV", over="SSSS")
+PIECES = [[(32, "S", "S"), (32, "V", "V")]] * 2 + [[(32, "S", "S"), (32, "V", "S")], [(24, "S", "S"), (40, "V", "V")]]
+BLOCKS = [(0,), (1,), (2,), (3,)]
+SPLIT = 1
+GATHER, SCATTER, MATMUL, WAKE, LOAD, FLIGHT, SLACK = 1.56, 3.8, 0.55, 180, 2400, 3000, 50
+SWEEPS, JITTER = 60, 600
+ORDER = []
 
 
 def _sb(cols, dt):
     return ("sbuf", [128, cols], dt)
 
 
-SCRATCH = {"XT": _sb(WEND, "bfloat16"), "Qb": _sb(4096 + 16, "bfloat16"), "D": _sb(1024, "float16"), "LL": _sb(384, "uint16"),
+SCRATCH = {"XT": _sb(WEND, "bfloat16"), "Qb": _sb(4096 + 16, "bfloat16"), "F": _sb(1024, "float32"), "LL": _sb(384, "uint16"),
            "ND": _sb(128, "int32"), "tx": _sb(64, "float32"), "LI": _sb(4, "uint16"), "LJ": _sb(4, "uint16"),
-           "zero": _sb(1024, "bfloat16"), "iS": _sb(144, "int32"), "ec": _sb(16, "float16"), "LY": _sb(256, "uint16"),
-           "prm": _sb(512, "float16")}
+           "zero": _sb(1024, "bfloat16"), "iS": _sb(144, "int32"), "LY": _sb(256, "uint16"),
+           "prm": _sb(512, "float16"), "fJ": _sb(512, "bfloat16"), "jneg": _sb(512, "bfloat16")}
 SCRATCH.update({n: _sb(4096, "bfloat16") for n in ("Bb", "bb", "zb", "sb")})
 SCRATCH.update({n: _sb(2048, "bfloat16") for n in ("pe", "po")})
 SCRATCH.update({n: _sb(256, "int32") for n in ("ledI", "eu", "wv", "hs", "hm")})
-SCRATCH.update({n: _sb(256, "float32") for n in ("E", "wE")})
+SCRATCH.update({n: _sb(256, "float32") for n in ("E", "wE", "Ls", "wu")})
 SCRATCH.update({n: _sb(256, "float16") for n in ("E16", "mA", "mE")})
-SCRATCH.update({n: _sb(256, "bfloat16") for n in ("mB", "sg", "cc", "ts", "comp", "val", "win", "cum")})
-SCRATCH.update({n: _sb(64, "bfloat16") for n in ("qs0", "qs1", "qs2", "land0", "land1", "land2")})
+SCRATCH.update({n: _sb(256, "bfloat16") for n in ("mB", "sg", "cc", "ts", "comp", "val", "win", "cum", "fA", "arow", "ovT")})
+SCRATCH.update({n: _sb(72, "bfloat16") for n in ("qs0", "qs1", "qs2", "land0", "land1", "land2")})
 SCRATCH.update({n: _sb(144, "bfloat16") for n in ("Wp", "Wn", "W2", "On")})
-SCRATCH.update({n: _sb(128, "bfloat16") for n in ("ones", "I4k", "cU", "cCap", "cPh", "blkT", "blk16", "kmat", "crow")})
-SCRATCH.update({n: _sb(128, "float16") for n in ("onesh", "identH")})
-SCRATCH.update({n: _sb(128, "int32") for n in ("iD", "iG", "iR", "iP")})
-SCRATCH.update({n: _sb(4, "int32") for n in ("vi", "vm", "iB", "iC")})
-SCRATCH.update({n: _sb(4, "float32") for n in ("vinv", "vbs", "vid", "base")})
+SCRATCH.update({n: _sb(128, "bfloat16") for n in ("ones", "identB", "IB", "cU", "cPh", "blkT", "blkB", "kmat")})
+SCRATCH.update({"identH": _sb(128, "float16"), "blkF": _sb(128, "float32")})
+SCRATCH.update({n: _sb(128, "int32") for n in ("iD", "iG", "iP")})
+SCRATCH.update({n: _sb(4, "int32") for n in ("Fi", "Li", "um")})
+SCRATCH.update({n: _sb(4, "float32") for n in ("c64", "inv", "cb")})
 SCRATCH.update({n: _sb(1, "int32") for n in ("pI", "kI", "parI", "i7", "kri", "krm")})
-SCRATCH.update({n: _sb(1, "float32") for n in ("kcol", "negk", "wcol", "wneg", "w2", "k64", "kap", "sa", "sc0", "ma", "mc", "lo7",
-                                                "hi7", "bk")})
-SCRATCH["jc"] = _sb(4, "float16")
-SCRATCH.update({n: ("psum", [128, 512], "float32") for n in ("pU0", "pU1", "pE", "pA", "pB", "pZ", "pSM", "pY")})
+SCRATCH.update({n: _sb(1, "float32") for n in ("kcol", "negk", "wcol", "wneg", "w2", "k256", "k4k", "neg4k", "kap", "sa", "sc0", "ma",
+                                                "mc", "lo7", "hi7", "bk")})
+SCRATCH.update({n: ("psum", [128, 512], "float32") for n in ("pU0", "pU1", "pE", "pA", "pB", "pZ", "pY0", "pY1")})
 SEMAPHORES = (["cV", "cS", "cP", "cG", "sent"] + ["arr%d" % t for t in range(3)] + ["d%d" % i for i in range(24)])
 
 
@@ -75,13 +79,35 @@ def in_order(calls):
                     ready[j] = max(done[x] for x in pre[j]) + WAKE
         return done, order
 
-    rank, best = [-i for i in range(n)], None
+    def pack(pre, order):
+        start, done, busy = [0] * n, [0] * n, {}
+        for i in order:
+            q, hold, length, _, _, banks, _ = calls[i]
+            s = max([done[j] + WAKE for j in pre[i]], default=0)
+            for a, b in sorted(busy.get(q, []) + [(a - WAKE, b + WAKE) for x in banks for a, b, o in busy.get(x, []) if o != q]):
+                if b > s:
+                    if s + hold <= a:
+                        break
+                    s = b
+            start[i], done[i] = s, s + length
+            busy.setdefault(q, []).append((s, s + hold))
+            for x in banks:
+                busy.setdefault(x, []).append((s, s + hold, q))
+        return start, done
+
+    rank, best, seed = [-i for i in range(n)], None, 1
     for _ in range(SWEEPS):
-        done, order = sweep(pre, post, rank)
-        if best is None or max(done) < best[0]:
-            best = (max(done), order)
-        rank, _ = sweep(post, pre, done)
-    return best[1]
+        _, order = sweep(pre, post, rank)
+        for _ in range(3):
+            start, done = pack(pre, order)
+            if best is None or max(done) < max(best[1]):
+                best = (start, done)
+            _, back = pack(post, sorted(range(n), key=lambda i: (-done[i], -i)))
+            order = sorted(range(n), key=lambda i: (-back[i], i))
+        seed = (seed * 1103515245 + 12345) % 2 ** 31
+        rank, _ = sweep(post, pre, [d + JITTER * ((seed * (i + 1) * 2654435761 >> 16) % 1024) / 1024 for i, d in enumerate(best[1])])
+    loads = [i for i in range(n) if not calls[i][3] and calls[i][1] < calls[i][2]]
+    return loads + sorted(set(range(n)) - set(loads), key=lambda i: (best[0][i], i))
 
 
 def rank_program(g, core, T, topo):
@@ -92,7 +118,7 @@ def rank_program(g, core, T, topo):
     rounds = 3
     V, S, P = g.vector, g.scalar, g.tensor
     Q = {"V": V, "S": S, "P": P, "G": g, "Y": g.sync}
-    calls = []
+    calls, turn, ends = [], [0], []
 
     def op(q, c, f, R, W, B=()):
         calls.append((q, c, c, R, W, B, f))
@@ -115,8 +141,8 @@ def rank_program(g, core, T, topo):
     def vms(ap, x, W, c=64):
         op("V", c, lambda: V.memset(ap, x), [], W)
 
-    def vscan(out, a, b, init, o0, o1, R, W, c=64):
-        op("V", c, lambda: V.tensor_tensor_scan(out, a, b, init, o0, o1), R, W)
+    def vscan(out, a, b, init, o0, o1, R, W, c=64, B=()):
+        op("V", c, lambda: V.tensor_tensor_scan(out, a, b, init, o0, o1), R, W, B)
 
     def sact(out, in_, f, R, W, B=(), bias=0.0, scale=1.0, c=64):
         op("S", c, lambda: S.activation(out, in_, f, bias=bias, scale=scale), R, W, B)
@@ -128,13 +154,13 @@ def rank_program(g, core, T, topo):
         else:
             op("G", c, lambda: g.iota(out, pat, base, cm), [], W)
 
-    def group(mms, R, W, B, n=64):
+    def group(mms, R, W, B, n=64, wide=0):
         def f():
             r = None
             for m in mms:
                 r = P.matmul(*m)
             return r
-        op("P", len(mms) * n * MATMUL, f, R, W, B)
+        op("P", (len(mms) + 3 * wide) * max(n, 64) * MATMUL, f, R, W, B)
 
     def col(name):
         return T[name][:, 0:1]
@@ -145,38 +171,36 @@ def rank_program(g, core, T, topo):
     EE, MM = ["E0", "E1"], ["mB0", "mB1"]
     dma("S", T.ledI[:], T.led[:], [], ["ledI"], LOAD)
     dma("S", T.mB[:], T.mk[:], [], MM, LOAD + 300)
-    for b in range(4):
-        c = slice(b * 1024, (b + 1) * 1024)
-        dma("Y", T.XT[:, c], T.xt[:, c], [], ["X%d" % b], LOAD + 1100 * (b + 1))
+    dma("Y", T.XT[:, 0:3072], T.xt[:, 0:3072], [], ["X0", "X1", "X2"], LOAD + 3300)
+    dma("Y", T.XT[:, 3072:4096], T.xt[:, 3072:4096], [], ["X3"], LOAD + 4200)
     XP = ["X0", "X1", "X2", "X3", "C", "T1"]
     NP = ["N0", "N1", "N2", "N3"]
     XALL = XP + NP
 
+    wide = 64 * max(len(b) for b in BLOCKS)
     iota(T.pI[:], [[0, 1]], 0, 1, ["pI"])
     iota(T.iP[:], [[16, 8], [1000, 2], [2, 8]], 0, -1, ["iP"])
     iota(T.iD[:], [[1, 128]], 0, -1, ["iD"])
     iota(T.iS[:], [[1, 144]], -15, -1, ["iS"])
     iota(T.iG[:], [[-16, 8], [0, 16]], 0, 1, ["iG"])
-    iota(T.iR[:], [[0, 8], [1, 16]], 0, 0, ["iR"])
-    iota(T.iB[:], [[1024, 4]], 0, 0, ["iB"])
-    iota(T.iC[:], [[512, 4]], 32, 0, ["iC"])
-    iota(T.Qb[:, 4096:4112], [[0, 16]], 256, 0, ["Qx"], True)
+    iota(T.fA[:], [[1, 256]], 0, 0, ["fA"], True)
+    iota(T.fJ[:, 0:4 * wide], [[-1, 4], [0, wide]], -1, 0, ["fJ"], True)
+    iota(T.c64[:], [[64, 4]], 0, 0, ["c64"], True)
+    iota(T.Qb[:, 4096:4112], [[0, 16]], 0, 0, ["Qx"], True)
+    for t in range(rounds):
+        iota(T["qs%d" % t][:, 64:72], [[0, 8]], 0, 0, ["qi%d" % t], True)
     vms(T.XT[:, ZC:ZC + 16], 0.0, ["C"])
     vms(T.XT[:, C15:C15 + 1], 2048.0, ["C"])
     vms(T.XT[:, SP:AW:64], 0.0, ["T1"])
     vms(T.zero[:], 0.0, ["zero"], 512)
     vms(T.ones[:], 1.0, ["ones"])
-    vms(T.onesh[:], 1.0, ["onesh"])
     vms(T.cU[:], 6144.0, ["cU"])
-    vms(T.cCap[:], -0.0625, ["cCap"])
-    vms(T.cPh[:], PART * math.exp(LAM + LOW) / 128, ["cPh"])
-    vms(T.ec[:], 0.0, ["ec"])
-    vms(T.ec[:, 0:16:5], 1.0, ["ec"])
     for name, bits in (("kI", 15), ("parI", 1), ("i7", 7)):
         vts(T[name][:], T.pI[:], bits, ALU.bitwise_and, None, None, ["pI"], [name])
-    for name, src, a, b in (("ma", "parI", NOFF, -NOFF), ("mc", "parI", -NOFF, NOFF + 2048), ("sa", "parI", -0.125, 0),
-                            ("sc0", "parI", 0.125, -0.0625), ("negk", "kI", -1, 0), ("kcol", "kI", 1, 0), ("wcol", "kI", 2, 1),
-                            ("wneg", "kI", -2, -1), ("w2", "kI", 4, 2), ("k64", "kI", 64, 0), ("bk", "kI", -LAM, LOW)):
+    for name, src, a, b in (("ma", "parI", NOFF, -NOFF), ("mc", "parI", -NOFF, NOFF + 2048), ("sa", "parI", -0.0625, 0),
+                            ("sc0", "parI", 0.0625, -0.03125), ("negk", "kI", -1, 0), ("kcol", "kI", 1, 0), ("wcol", "kI", 2, 1),
+                            ("wneg", "kI", -2, -1), ("w2", "kI", 4, 2), ("k256", "kI", 256, 0), ("k4k", "kI", 4096, 0),
+                            ("neg4k", "kI", -4, 0), ("bk", "kI", -LAM, LOW)):
         vts(T[name][:], T[src][:], float(a), ALU.mult, float(b), ALU.add, [src], [name])
     vts(T.lo7[:], T.i7[:], 7, ALU.is_equal, float(C15), ALU.mult, ["i7"], ["lo7"])
     vts(T.hi7[:], T.i7[:], 7, ALU.is_equal, float(ZC), ALU.add, ["i7"], ["hi7"])
@@ -184,15 +208,15 @@ def rank_program(g, core, T, topo):
         for b in range(2):
             j = 2 * par + b
             vts(T.prm[:, 128 * j:128 * j + 128], T.iP[:], 1000 * b - par, ALU.is_equal, None, None, ["iP"], ["perm%d" % j], c=128)
-    vts(T.identH[:], T.iD[:], 0, ALU.is_equal, None, None, ["iD"], ["identH"], c=128)
-    vts(T.I4k[:], T.iD[:], 0, ALU.is_equal, -4096.0, ALU.mult, ["iD"], ["I4k"], c=128)
+    for name, w in (("identH", 1.0), ("identB", 1.0), ("IB", -BIG)):
+        vts(T[name][:], T.iD[:], 0, ALU.is_equal, w, ALU.mult, ["iD"], [name], c=128)
     for name, w in (("Wn", "wneg"), ("W2", "w2"), ("Wp", "wcol"), ("On", None)):
         vts(T[name][:], T.iS[:], col("negk"), ALU.is_equal, col(w) if w else 1.0, ALU.mult, ["iS", "negk", w], [name], c=144)
-    for name, w in (("blkT", PART), ("blk16", -16.0), ("kmat", col("kcol"))):
-        vts(T[name][:], T.iG[:], col("kcol"), ALU.is_equal, w, ALU.mult, ["iG", "kcol"], [name], c=128)
-    vts(T.crow[:], T.iR[:], 0.125, ALU.mult, None, None, ["iR"], ["crow"], c=128)
-    vcp(T.jc[:], T.iC[:], ["iC"], ["jc"])
-    vts(T.base[:], T.iB[:], col("k64"), ALU.add, None, None, ["iB", "k64"], ["base"])
+    for name, w in (("blkT", PART), ("blkB", -BIG), ("blkF", 1.0), ("kmat", col("k4k"))):
+        vts(T[name][:], T.iG[:], col("kcol"), ALU.is_equal, w, ALU.mult, ["iG", "kcol", "k4k"], [name], c=128)
+    sact(T.arow[:], T.fA[:], ACT.Copy, ["fA"], ["arow"], scale=512.0, c=256)
+    sact(T.jneg[:, 0:4 * wide], T.fJ[:, 0:4 * wide], ACT.Identity, ["fJ", "neg4k"], ["jneg"], bias=col("neg4k"), c=4 * wide)
+    sact(T.cPh[:], T.ones[:], ACT.Exp, ["ones"], ["cPh"], scale=LAM + LOW + math.log(PART / 128), c=1700)
 
     def sel(name, k):
         return T[name][:, 15 - k:143 - k]
@@ -203,35 +227,32 @@ def rank_program(g, core, T, topo):
         vts(T.E16[:], T.E[:], -2048.0, ALU.add, None, None, EE, ["E16"], c=256)
         vts(T.mA[:], T.mB[:], -float(NOFF), ALU.mult, NOFF + 2048.0, ALU.add, MM, ["mA"], c=128)
         vts(T.mE[:], T.mB[:], col("ma"), ALU.mult, col("mc"), ALU.add, MM + ["ma", "mc"], ["mE"], c=128)
-        for bank, par, srcs in (("pU0", 0, ("E16", "mA")), ("pU1", 1, ("E16", "mA")), ("pY", 1, ("E16",))):
+        for bank, par, srcs in (("pY0", 0, ("E16", "mA")), ("pY1", 1, ("E16", "mA")), ("pB", 1, ("E16",))):
             terms = [(s, b) for s in srcs for b in range(2)]
             group([(T[bank][:, 0:128], T.prm[:, 128 * (2 * par + b):128 * (2 * par + b + 1)], T[s][:, b:256:2], i == 0,
                     i == len(terms) - 1) for i, (s, b) in enumerate(terms)],
-                  list(srcs) + ["perm%d" % (2 * par), "perm%d" % (2 * par + 1)], [bank], [bank], 128)
+                  list(srcs) + ["perm%d" % (2 * par), "perm%d" % (2 * par + 1)], [bank + x for x in ("", "_0", "_1")], [bank], 128)
         group([(T.pE[:, 0:256], T.identH[:], T[s][:], s == "E16", s == "mE") for s in ("E16", "mE")], ["identH", "E16", "mE"],
               E8, ["pE"], 256)
-        vts(T.LL[:, 256:384], T.pU1[:, 0:128], col("lo7"), ALU.max, col("hi7"), ALU.min, ["pU1", "lo7", "hi7"], ["LB"], ["pU1"], 128)
-        vcp(T.LL[:, 0:128], T.pU0[:, 0:128], ["pU0"], ["LE"], ["pU0"], 128)
-        vts(T.LL[:, 128:256], T.pY[:, 0:128], 2048.0, ALU.add, None, None, ["pY"], ["LX"], ["pY"], 128)
+        vts(T.LL[:, 256:384], T.pY1[:, 0:128], col("lo7"), ALU.max, col("hi7"), ALU.min, ["pY1", "lo7", "hi7"], ["LB"], ["pY1"], 128)
+        vcp(T.LL[:, 0:128], T.pY0[:, 0:128], ["pY0"], ["LE"], ["pY0"], 128)
+        vts(T.LL[:, 128:256], T.pB[:, 0:128], 2048.0, ALU.add, None, None, ["pB_0", "pB_1"], ["LX"], ["pB"], 128)
         sact(T.sg[:], T.mB[:], ACT.Identity, MM + ["sa", "sc0"], ["sg"], bias=col("sc0"), scale=col("sa"), c=256)
 
     vcp(T.E[:], T.ledI[:], ["ledI"], EE, c=256)
     lists()
     for b in range(4):
-        vts(T.XT[:, NOFF + b * 1024:NOFF + (b + 1) * 1024], T.XT[:, b * 1024:(b + 1) * 1024], -1.0, ALU.mult, None, None,
-            ["X%d" % b], ["N%d" % b], c=512)
+        x, neg = T.XT[:, b * 1024:(b + 1) * 1024], T.XT[:, NOFF + b * 1024:NOFF + (b + 1) * 1024]
+        if b == 1:
+            sact(neg, x, ACT.Copy, ["X1"], ["N1"], scale=-1.0, c=1024)
+        else:
+            vts(neg, x, -1.0, ALU.mult, None, None, ["X%d" % b], ["N%d" % b], c=512)
 
     def ca(i):
         return slice(i * 64, (i + 1) * 64)
 
-    def ce(i, par=None):
-        return slice(i * 1024, (i + 1) * 1024) if par is None else slice(i * 1024 + par, (i + 1) * 1024, 2)
-
-    def ch(i):
-        return slice(i * 512, (i + 1) * 512)
-
-    def cb(b):
-        return slice(b * 128, (b + 1) * 128)
+    def ce(i, par):
+        return slice(i * 1024 + par, (i + 1) * 1024, 2)
 
     def lst(n, i):
         return T.LL[:, 128 * n + 32 * i:128 * n + 32 * i + 32]
@@ -239,139 +260,166 @@ def rank_program(g, core, T, topo):
     def line(buf, i, k):
         return buf[:, i * 1024 + k:(i + 1) * 1024:16]
 
+    def parts(name, i):
+        return ["%s%d_%d" % (name, i, h) for h in range(SPLIT)]
+
     def amounts(i):
-        s = str(i)
+        s, m = str(i), 1024 // SPLIT
         src = T.XT[:, 0:GW].indirect(lst(0, i))
         if OPT["gE"][i] == "V":
             vcp(T.Qb[:, ce(i, 0)], src, ["LE"] + XALL, ["Qe" + s], c=gat(512))
         else:
             sact(T.Qb[:, ce(i, 0)], src, ACT.Copy, ["LE"] + XALL, ["Qe" + s], c=gat(512))
-        src = T.XT[:, 0:SP].indirect(lst(2, i))
+        src = T.XT[:, 0:ZC + 16].indirect(lst(2, i))
         if OPT["gB"][i] == "V":
             vts(T.Bb[:, ce(i, 1)], src, -1.0, ALU.mult, None, None, ["LB"] + XP, ["Bo" + s], c=gat(512))
         else:
             sact(T.Bb[:, ce(i, 1)], src, ACT.Copy, ["LB"] + XP, ["Bo" + s], scale=-1.0, c=gat(512))
-        if OPT["relu"][i] == "V":
-            vts(T.Bb[:, ce(i, 0)], T.Qb[:, ce(i, 0)], 0.0, ALU.max, None, None, ["Qe" + s], ["Be" + s], c=256)
-        else:
-            sact(T.Bb[:, ce(i, 0)], T.Qb[:, ce(i, 0)], ACT.Relu, ["Qe" + s], ["Be" + s], c=512)
-        vscan(T.bb[:, ce(i)], T.Bb[:, ce(i)], T.zero[:], 0.0, ALU.add, ALU.max, ["Be" + s, "Bo" + s, "zero"], ["bb" + s], 512)
-        vtt(T.Qb[:, ce(i, 1)], T.XT[:, 0:4096].indirect(lst(1, i)), T.bb[:, ce(i, 0)], ALU.min, ["LX", "bb" + s] + XP, ["Qo" + s],
-            c=gat(512))
-        vts(T.pe[:, ch(i)], T.Qb[:, ce(i, 0)], 0.0, ALU.not_equal, None, None, ["Qe" + s], ["pe" + s], c=256)
-        if OPT["over"][i] == "V":
-            vts(T.po[:, ch(i)], T.Qb[:, ce(i, 1)], 1.0, ALU.min, None, None, ["Qo" + s], ["po" + s], c=256)
-        else:
-            sact(T.po[:, ch(i)], T.Qb[:, ce(i, 1)], ACT.Sign, ["Qo" + s], ["po" + s], c=512)
+        cuts = [(h, i * 1024 + h * m) for h in range(SPLIT)]
+        for h, lo in cuts:
+            j, ev = "%d_%d" % (i, h), slice(lo, lo + m, 2)
+            if OPT["relu"][i] == "V":
+                vts(T.Bb[:, ev], T.Qb[:, ev], 0.0, ALU.max, None, None, ["Qe" + s], ["Be" + j], c=m // 4)
+            else:
+                sact(T.Bb[:, ev], T.Qb[:, ev], ACT.Relu, ["Qe" + s], ["Be" + j], c=m // 2)
+            vscan(T.bb[:, lo:lo + m], T.Bb[:, lo:lo + m], T.zero[:, 0:m], 0.0, ALU.add, ALU.max, ["Be" + j, "Bo" + s, "zero"],
+                  ["bb" + j], m // 2)
+            vts(T.pe[:, lo // 2:(lo + m) // 2], T.Qb[:, ev], 0.0, ALU.not_equal, None, None, ["Qe" + s], ["pe" + j], c=m // 4)
+        vtt(T.Qb[:, ce(i, 1)], T.XT[:, 0:4096].indirect(lst(1, i)), T.bb[:, ce(i, 0)], ALU.min, ["LX"] + parts("bb", i) + XP,
+            ["Qo" + s], c=gat(512))
+        for h, lo in cuts:
+            out, od = T.po[:, lo // 2:(lo + m) // 2], T.Qb[:, lo + 1:lo + m:2]
+            if OPT["over"][i] == "V":
+                vts(out, od, 1.0, ALU.min, None, None, ["Qo" + s], ["po%d_%d" % (i, h)], c=m // 4)
+            else:
+                sact(out, od, ACT.Sign, ["Qo" + s], ["po%d_%d" % (i, h)], c=m // 2)
+
+    def upl(i):
+        n = "pU%d" % (i % 2)
+        return n, T[n][:, ca(i // 2)]
 
     def hashes(i, t):
-        n = "pU%d" % (i % 2)
-        o, a, s = T[n][:, 0:64], ca(i), str(i)
+        (n, o), a, s = upl(i), ca(i), str(i)
         mms = [(o, T.cU[:], T.ones[:, 0:64], True, False)]
         for k in range(0, 16, 2):
             mms += [(o, sel("Wn", k), line(T.Qb, i, k), False, False), (o, sel("W2", k), line(T.Bb, i, k), False, False)]
-        group(mms, ["cU", "ones", "Wn", "W2", "Qe" + s, "Be" + s], [n], [n])
-        group([(o, sel("Wp", k), line(T.Qb, i, k), False, k == 15) for k in range(1, 16, 2)], ["Wp", "Qo" + s], [n], [n])
+        group(mms, ["cU", "ones", "Wn", "W2", "Qe" + s] + parts("Be", i), [n, "u" + s], [n])
+        group([(o, sel("Wp", k), line(T.Qb, i, k), False, k == 15) for k in range(1, 16, 2)], ["Wp", "Qo" + s], [n, "u" + s], [n])
         if OPT["cc"][i] == "V":
-            vts(T.cc[:, a], o, -2047.5, ALU.add, None, None, [n], ["cc" + s], [n])
+            vts(T.cc[:, a], o, -2047.5, ALU.add, None, None, ["u" + s], ["cc" + s], [n])
         else:
-            sact(T.cc[:, a], o, ACT.Copy, [n], ["cc" + s], [n], bias=-2047.5)
-        vtt(o, o, T.cc[:, a], ALU.subtract, [n, "cc" + s], [n], [n])
+            sact(T.cc[:, a], o, ACT.Copy, ["u" + s], ["cc" + s], [n], bias=-2047.5)
+        vtt(o, o, T.cc[:, a], ALU.subtract, ["u" + s, "cc" + s], ["u" + s], [n])
         ek = T.pE[:, a] if t == 0 else T.pE[:, 256 + 64 * i:256 + 64 * i + 64]
-        vtt(T.eu[:, a], o, T.E[:, a], ALU.mult, [n, "E%d" % (i // 2)], ["eu" + s], [n])
+        vtt(T.eu[:, a], o, T.E[:, a], ALU.mult, ["u" + s, "E%d" % (i // 2)], ["eu" + s], [n])
         vts(T.wv[:, a], T.eu[:, a], 5, ALU.arith_shift_right, 4095, ALU.bitwise_and, ["eu" + s], ["wv" + s])
         vtt(T.hs[:, a], ek, T.wv[:, a], ALU.add, ["wv" + s, "E8_" + s, "Ek"], ["hs" + s], ["pE"])
         vts(T.hm[:, a], T.hs[:, a], 4095 + NOFF, ALU.bitwise_and, None, None, ["hs" + s], ["hm" + s])
         vcp(T.LY[:, a], T.hm[:, a], ["hm" + s], ["LY" + s])
 
-    def bank(b):
-        return "pA" if b == 0 else "pB"
+    def region(i, j, whole=False):
+        b = [i in x for x in BLOCKS].index(True)
+        n, w = "pA" if b % 2 == 0 else "pB", len(BLOCKS[b])
+        lo = j * w + (0 if whole else i - BLOCKS[b][0]) + (4 if w == 1 and b >= 2 and len(BLOCKS[b - 2]) == 1 else 0)
+        hi = lo + (w if whole else 1)
+        return n, T[n][:, 64 * lo:64 * hi], ["%s_%d" % (n, x) for x in range(lo, hi)]
 
     def scores(i):
-        s = str(i)
-        for j in (2 * i, 2 * i + 1):
-            c, z = ch(j), "z%d" % j
-            src = T.XT[:, 0:GW].indirect(T.LY[:, 32 * j:32 * j + 32])
-            if OPT["y"][j] == "V":
-                vtt(T.zb[:, c], src, T.Qb[:, c], ALU.subtract, ["LY" + s, "Qe" + s, "Qo" + s] + XALL, [z], c=gat(512))
-                if OPT["sign"][j] == "V":
-                    vts(T.sb[:, c], T.zb[:, c], -1.0, ALU.max, 1.0, ALU.min, [z], ["s%d" % j], c=256)
+        s, lo, names = str(i), 64 * i, []
+        for n_acc, who, sign in PIECES[i]:
+            c, m = slice(16 * lo, 16 * (lo + n_acc)), 16 * n_acc
+            z, sg = "z%d" % lo, "s%d" % lo
+            names.append(sg)
+            src = T.XT[:, 0:GW].indirect(T.LY[:, lo:lo + n_acc])
+            if who == "V":
+                vtt(T.zb[:, c], src, T.Qb[:, c], ALU.subtract, ["LY" + s, "Qe" + s, "Qo" + s] + XALL, [z], c=gat(m))
+                if sign == "V":
+                    vts(T.sb[:, c], T.zb[:, c], -1.0, ALU.max, 1.0, ALU.min, [z], [sg], c=m // 2)
                 else:
-                    sact(T.sb[:, c], T.zb[:, c], ACT.Sign, [z], ["s%d" % j], c=512)
+                    sact(T.sb[:, c], T.zb[:, c], ACT.Sign, [z], [sg], c=m)
             else:
-                sact(T.zb[:, c], src, ACT.Copy, ["LY" + s] + XALL, [z], scale=-1.0, c=gat(512))
-                group([(T.pY[:], T.I4k[:], T.Qb[:, c], True, False), (T.pY[:], T.I4k[:], T.zb[:, c], False, True)],
-                      ["I4k", z, "Qe" + s, "Qo" + s], ["pY"], ["pY"], 512)
-                sact(T.sb[:, c], T.pY[:], ACT.Sign, ["pY"], ["s%d" % j], ["pY"], c=512)
-        n = bank(i // 2)
-        o = T[n][:, 64 * (i % 2):64 * (i % 2) + 64]
-        group([(o, sel("On", k), line(T.sb, i, k), k == 0, k == 15) for k in range(16)], ["On", "s%d" % (2 * i), "s%d" % (2 * i + 1)],
-              ["pS" + s], [n])
+                sact(T.zb[:, c], src, ACT.Copy, ["LY" + s] + XALL, [z], scale=-1.0, c=gat(m))
+                n = "pY%d" % (turn[0] % 2)
+                turn[0] += 1
+                o = T[n][:, 0:m]
+                group([(o, T.IB[:], T.Qb[:, c], True, False)], ["IB", "Qe" + s, "Qo" + s], [n], [n], m)
+                group([(o, T.IB[:], T.zb[:, c], False, True)], ["IB", z], [n], [n], m)
+                sact(T.sb[:, c], o, ACT.Sign, [n], [sg], [n], c=m)
+            lo += n_acc
+        n, o, w = region(i, 0)
+        group([(o, sel("On", k), line(T.sb, i, k), k == 0, k == 15) for k in range(16)], ["On"] + names, w, [n])
+
+    def counts(b):
+        n, s, c = "pU%d" % b, str(b), slice(128 * b, 128 * b + 128)
+        group([(T[n][:, 256 + k:384:16], (T.po if k % 2 else T.pe)[:, b * 1024 + k // 2:(b + 1) * 1024:8], T.On[:, 15:143:16], True, True)
+               for k in range(16)], ["On"] + [x for i in (2 * b, 2 * b + 1) for x in parts("pe", i) + parts("po", i)], [n, "cnt" + s], [n])
+        sact(T.ovT[:, c], T[n][:, 256:384], ACT.Sign, ["cnt" + s], ["ovT" + s], [n], bias=-8.5, c=128)
+        group([(T[n][:, 384:512], T.ones[:], T.identB[:], True, False), (T[n][:, 384:512], T.ovT[:, c], T.identB[:], False, True)],
+              ["ones", "identB", "ovT" + s], [n, "ov" + s], [n], 128)
+        vtt(T.ts[:, c], T[n][:, 384:512], T.sg[:, c], ALU.mult, ["ov" + s, "sg"], ["gov" + s], [n], 128)
 
     def decide(b):
-        n, c, s = bank(b), cb(b), str(b)
-        for i in (2 * b, 2 * b + 1):
-            o = T[n][:, 128 + 64 * (i % 2):192 + 64 * (i % 2)]
-            mms = [(o, T.cCap[:], T.ones[:, 0:64], True, False)]
-            mms += [(o, sel("On", k), (T.po if k % 2 else T.pe)[:, i * 512 + k // 2:(i + 1) * 512:8], False, k == 15) for k in range(16)]
-            group(mms, ["cCap", "ones", "On", "pe%d" % i, "po%d" % i], ["cap%d" % i], [n])
-        two = ["%d" % (2 * b), "%d" % (2 * b + 1)]
-        vtt(T.ts[:, c], T[n][:, 0:128], T.sg[:, c], ALU.mult, ["pS" + x for x in two] + ["sg"], ["ts" + s], [n], 128)
-        vtt(T.comp[:, c], T[n][:, 128:256], T.ts[:, c], ALU.min, ["cap" + x for x in two] + ["ts" + s], ["comp" + s], [n], 128)
-        sact(T.val[:, c], T.comp[:, c], ACT.Exp, ["comp" + s, "bk"], ["val" + s], bias=col("bk"), scale=16 * 17 * LAM, c=128)
-        o = T[n][:, 256:384]
-        group([(o, T.cPh[:], T.ones[:], True, False), (o, T.blkT[:], T.val[:, c], False, True)],
-              ["cPh", "ones", "blkT", "val" + s], ["sum" + s], [n], 128)
-        vtt(T.win[:, c], o, T.val[:, c], ALU.is_lt, ["sum" + s, "val" + s], ["win" + s], [n], 128)
-        vscan(T.cum[:, c], T.win[:, c], T.zero[:, 0:128], 0.0 if b == 0 else T.cum[:, 127:128], ALU.add, ALU.add,
-              ["win" + s, "zero"] + ["cum0"] * b, ["cum" + s])
-        o = T.pZ[:, c]
-        group([(o, T.ones[:], T.crow[:], True, False), (o, T.win[:, c], T.kmat[:], False, False),
-               (o, T.cum[:, c], T.blk16[:], False, True)], ["ones", "crow", "kmat", "blk16", "win" + s, "cum" + s],
-              ["pZ" + s], ["pZ"], 128)
-        mms = [] if b else [(T.pSM[:, 0:4], T.onesh[:], T.jc[:], True, False)]
+        i, w = BLOCKS[b][0], 64 * len(BLOCKS[b])
+        a, s, ones = slice(64 * i, 64 * i + w), str(b), T.ones[:, 0:w]
+        (n, score, nS), (_, cap, nC), (_, total, nT), (_, ln, nL) = [region(i, j, True) for j in range(4)]
+        won = ["win%d" % x for x in BLOCKS[b]]
+        vtt(T.comp[:, a], score, T.ts[:, a], ALU.mult, nS + ["gov%d" % (i // 2)], ["comp" + s], [n], w)
+        sact(T.val[:, a], T.comp[:, a], ACT.Exp, ["comp" + s, "bk"], ["val" + s], bias=col("bk"), scale=16 * 17 * LAM, c=w)
+        group([(total, T.cPh[:], ones, True, False), (total, T.blkT[:], T.val[:, a], False, True)],
+              ["cPh", "ones", "blkT", "val" + s], nT, [n], w)
+        vtt(T.win[:, a], total, T.val[:, a], ALU.is_lt, nT + ["val" + s], won, [n], w)
+        for x in BLOCKS[b]:
+            vtt(T.wu[:, ca(x)], upl(x)[1], T.win[:, ca(x)], ALU.mult, ["u%d" % x, "win%d" % x], ["wu%d" % x], [upl(x)[0]])
+        vscan(T.cum[:, a], T.win[:, a], T.zero[:, 0:w], T.cum[:, 64 * i - 1:64 * i] if b else 0.0, ALU.add, ALU.add,
+              won + ["zero"] + (["cum%d" % (b - 1)] if b else []), ["cum" + s])
+        group([(ln, T.ones[:], T.arow[:, a], True, False), (ln, T.kmat[:], T.win[:, a], False, False),
+               (ln, T.blkF[:], T.wu[:, a], False, True)], ["ones", "arow", "kmat", "blkF"] + won + ["wu%d" % x for x in BLOCKS[b]],
+              nL, [n], w, 1)
+        sact(T.Ls[:, a], ln, ACT.Copy, nL, ["Ls" + s], [n], c=w)
+        group([(T.pZ[:, 0:4 * wide], T.IB[:], T.jneg[:, 0:4 * wide], True, False)], ["IB", "jneg"], ["pZ"], ["pZ"], 4 * wide)
+        group([(T.pZ[:, wide * j:wide * j + w], T.blkB[:], T.cum[:, a], False, j == 3) for j in range(4)], ["blkB", "cum" + s],
+              ["pZ"], ["pZ"], w)
         for j in range(4):
-            lo = -(256.0 * j + 16)
-            d = T.D[:, j * 256 + b * 128:j * 256 + (b + 1) * 128]
-            vts(d, o, lo, ALU.max, lo + 16, ALU.min, ["pZ" + s], ["D%d%d" % (j, b)], ["pZ"], 128)
-            mms.append((T.pSM[:, 0:4], d, T.ec[:, 4 * j:4 * j + 4], False, b == 1 and j == 3))
-        group(mms, ["onesh", "jc", "ec"] + ["D%d%d" % (j, b) for j in range(4)], ["pSM"], ["pSM"])
+            o = 256 * j + 64 * i
+            vscan(T.F[:, o:o + w], T.Ls[:, a], T.pZ[:, wide * j:wide * j + w], T.F[:, o - 1:o] if b else BIG, ALU.min, ALU.max,
+                  ["Ls" + s, "pZ", "F%d" % j], ["F%d" % j], w, ["pZ"])
 
     def send(t):
-        vcp(T.LJ[:], T.pSM[:, 0:4], ["pSM"], ["LJ"], ["pSM"])
-        qn = "qs%d" % t
-        sact(T[qn][:], T.Qb[:].indirect(T.LJ[:, 0:4]), ACT.Abs, ["LJ", "Qx"] + ["Q%s%d" % (x, i) for x in "eo" for i in range(4)], [qn],
-             c=gat(64))
-        calls.append(("G", 300, FLIGHT, [qn], ["land%d" % t], (), ("send", t)))
+        FF, qs, found = ["F%d" % j for j in range(4)], T["qs%d" % t], T.F[:, 255:1024:256]
+        vts(T.Fi[:], found, BIG, ALU.min, None, None, FF, ["Fi"])
+        vts(T.Li[:], T.Fi[:], 12, ALU.arith_shift_right, None, None, ["Fi"], ["Li"])
+        vcp(T.LJ[:], T.Li[:], ["Li"], ["LJ"])
+        sact(qs[:, 0:64], T.Qb[:].indirect(T.LJ[:, 0:4]), ACT.Abs, ["LJ", "Qx"] + ["Q%s%d" % (x, i) for x in "eo" for i in range(4)],
+             ["qs%d" % t], c=gat(64))
+        vts(T.inv[:], found, BIG, ALU.is_ge, float(SP), ALU.mult, FF, ["inv"])
+        vts(T.um[:], T.Fi[:], 63, ALU.bitwise_and, None, None, ["Fi"], ["um"])
+        vtt(T.cb[:], T.inv[:], T.c64[:], ALU.add, ["inv", "c64"], ["cb"])
+        vtt(qs[:, 64:68], T.um[:], T.cb[:], ALU.add, ["um", "cb"], ["qi%d" % t])
+        calls.append(("G", 300, FLIGHT, ["qs%d" % t, "qi%d" % t], ["land%d" % t], (), ("send", t)))
 
     def update(b):
-        c, s = cb(b), str(b)
-        e8 = E8[2 * b:2 * b + 2]
+        c, s = slice(128 * b, 128 * b + 128), str(b)
+        e8, won = E8[2 * b:2 * b + 2], ["win%d" % i for i in (2 * b, 2 * b + 1)]
         vtt(T.pE[:, c], T.hm[:, c], T.pE[:, c], ALU.subtract, e8 + ["hm%d" % i for i in (2 * b, 2 * b + 1)], e8, ["pE"], 128)
-        vtt(T.wE[:, c], T.pE[:, c], T.win[:, c], ALU.mult, e8 + ["win" + s], ["wE" + s], ["pE"], 128)
-        vtt(T.mB[:, c], T.mB[:, c], T.win[:, c], ALU.not_equal, ["mB" + s, "win" + s], ["mB" + s], c=256)
+        vtt(T.wE[:, c], T.pE[:, c], T.win[:, c], ALU.mult, e8 + won, ["wE" + s], ["pE"], 128)
+        vtt(T.mB[:, c], T.mB[:, c], T.win[:, c], ALU.not_equal, ["mB" + s] + won, ["mB" + s], c=256)
         vtt(T.E[:, c], T.E[:, c], T.wE[:, c], ALU.add, ["E" + s, "wE" + s], ["E" + s], c=256)
 
     def kappa():
-        group([(T.pZ[:, 256:257], T.ones[:], T.cum[:, 255:256], True, True)], ["ones", "cum1"], ["kp"], ["pZ"])
-        vcp(T.kri[:], T.pZ[:, 256:257], ["kp"], ["kri"], ["pZ"])
+        group([(T.pU0[:, 256:257], T.ones[:], T.cum[:, 255:256], True, True)], ["ones", "cum%d" % (len(BLOCKS) - 1)], ["pU0", "kp"], ["pU0"])
+        vcp(T.kri[:], T.pU0[:, 256:257], ["kp"], ["kri"], ["pU0"])
         vts(T.krm[:], T.kri[:], 31, ALU.bitwise_and, None, None, ["kri"], ["krm"])
         vcp(T.kap[:], T.krm[:], ["krm"], ["kap"])
         sact(T.pE[:, 256:512], T.pE[:, 0:256], ACT.Identity, ["kap"] + E8, ["Ek"], ["pE"], bias=col("kap"), c=256)
 
     def arrive(t, last):
         ln = "land%d" % t
-        group([(T.pSM[:, 32:36], sel("Wp", r), T[ln][:, r:64:16], r == 0, r == 15) for r in range(16)], ["Wp", ln], ["pSM"], ["pSM"])
-        vcp(T.vi[:], T.pSM[:, 32:36], ["pSM"], ["vi"], ["pSM"])
-        vts(T.vinv[:], T.pSM[:, 32:36], 65535.5, ALU.is_ge, float(SP), ALU.mult, ["pSM"], ["vinv"], ["pSM"])
-        vts(T.vm[:], T.vi[:], 63, ALU.bitwise_and, None, None, ["vi"], ["vm"])
-        vtt(T.vbs[:], T.vinv[:], T.base[:], ALU.add, ["vinv", "base"], ["vbs"])
-        vtt(T.vid[:], T.vm[:], T.vbs[:], ALU.add, ["vm", "vbs"], ["vid"])
-        vcp(T.LI[:], T.vid[:], ["vid"], ["LI"])
-        vtt(T.tx[:], T.XT[:, 0:AW].indirect(T.LI[:, 0:4]), T[ln][:], ALU.add, ["LI", ln] + XP, ["tx"], c=gat(64))
+        vts(T.LI[:], T[ln][:, 64:68], col("k256"), ALU.add, None, None, [ln, "k256"], ["LI"])
+        vtt(T.tx[:], T.XT[:, 0:AW].indirect(T.LI[:, 0:4]), T[ln][:, 0:64], ALU.add, ["LI", ln] + XP, ["tx"], c=gat(64))
         vts(T.ND[:, 0:64], T.tx[:], 0.5, ALU.mult, -0.25, ALU.add, ["tx"], ["ND0"])
         vcp(T.XT[:, 0:AW].indirect(T.LI[:, 0:4]), T.ND[:, 0:64], ["LI", "ND0"], XP, c=60 + 64 * SCATTER)
         if not last:
+            calls[-1] = calls[-1][:2] + (calls[-1][2] + WAKE,) + calls[-1][3:]
             vts(T.ND[:, 64:128], T.tx[:], -0.5, ALU.mult, 0.25, ALU.add, ["tx"], ["ND1"])
             vcp(T.XT[:, NOFF:WEND].indirect(T.LI[:, 0:4]), T.ND[:, 64:128], ["LI", "ND1"], NP, c=60 + 64 * SCATTER)
 
@@ -381,8 +429,11 @@ def rank_program(g, core, T, topo):
             amounts(i)
             hashes(i, t)
             scores(i)
-        for b in range(2):
+            if i % 2:
+                counts(i // 2)
+        for b in range(len(BLOCKS)):
             decide(b)
+        for b in range(2):
             update(b)
         send(t)
         if last:
@@ -392,15 +443,18 @@ def rank_program(g, core, T, topo):
             lists()
             kappa()
         arrive(t, last)
-    for b in range(2):
-        c = slice(b * 2048, (b + 1) * 2048)
-        dma("YS"[b], T.yx[:, c], T.XT[:, c], ["X%d" % (2 * b), "X%d" % (2 * b + 1)], ["yx%d" % b], LOAD + 2000)
+        if not last:
+            ends.append(len(calls))
+    dma("Y", T.yx[:], T.XT[:, 0:4096], XP, ["yx"], LOAD + 4000)
 
     count = {}
     known = {q: {} for q in Q}
     lastw, readers, banks = {}, {}, {}
     n_dma = 0
-    for seq, i in enumerate(in_order(calls)):
+    if not ORDER:
+        for lo, hi in zip([0] + ends, ends + [len(calls)]):
+            ORDER.extend(lo + i for i in in_order(calls[lo:hi]))
+    for seq, i in enumerate(ORDER):
         q, _, _, R, W, B, f = calls[i]
         toks = [lastw[x] for x in list(R) + list(W) if x in lastw]
         toks += [y for x in W for y in readers.get(x, [])]

@@ -9,12 +9,16 @@ NENG = 8
 LAM, LOW, PART = 0.6, -78.0, 0.4
 BIG = float(2 ** 24)
 
-OPT = dict(cc="SSSS", gE="VSSS", gB="SSSS", relu="VVVV", over="SSSS")
-PIECES = [[(32, "S", "S"), (32, "V", "V")]] * 2 + [[(32, "S", "S"), (32, "V", "S")], [(24, "S", "S"), (40, "V", "V")]]
-BLOCKS = [(0,), (1,), (2,), (3,)]
+OPT = dict(cc="SSVV", gE="VSSS", gB="SSSS", relu="VVVV", over="SSSV")
+PIECES = [[(32, "S", "S")] * 2, [(32, "S", "S"), (32, "V", "V")], [(32, "S", "S"), (32, "V", "S")], [(32, "V", "S"), (32, "V", "V")]]
+HASHED = [(0,), (1,), (2,), (3,)]
+BLOCKS = [(0, 1), (2, 3)]
+SHORT = (1,)
+PLACES = ["SSSS", "VVSS"]
 SPLIT = 1
-GATHER, SCATTER, MATMUL, WAKE, LOAD, FLIGHT, SLACK = 1.56, 3.8, 0.55, 180, 2400, 3000, 50
-SWEEPS, JITTER = 60, 600
+GATHER, SCATTER, MATMUL, WAKE, LOAD, FLIGHT, SLACK = 1.4, 3.8, 0.6, 195, 1800, 3000, 50
+START = {"V": 25, "S": 65}
+SWEEPS, JITTER = 120, 600
 ORDER = []
 
 
@@ -25,22 +29,24 @@ def _sb(cols, dt):
 SCRATCH = {"XT": _sb(WEND, "bfloat16"), "Qb": _sb(4096 + 16, "bfloat16"), "F": _sb(1024, "float32"), "LL": _sb(384, "uint16"),
            "ND": _sb(128, "int32"), "tx": _sb(64, "float32"), "LI": _sb(4, "uint16"), "LJ": _sb(4, "uint16"),
            "zero": _sb(1024, "bfloat16"), "iS": _sb(144, "int32"), "LY": _sb(256, "uint16"),
-           "prm": _sb(512, "float16"), "fJ": _sb(512, "bfloat16"), "jneg": _sb(512, "bfloat16")}
+           "prm": _sb(512, "float16"), "Pn": _sb(1024, "float32")}
 SCRATCH.update({n: _sb(4096, "bfloat16") for n in ("Bb", "bb", "zb", "sb")})
 SCRATCH.update({n: _sb(2048, "bfloat16") for n in ("pe", "po")})
 SCRATCH.update({n: _sb(256, "int32") for n in ("ledI", "eu", "wv", "hs", "hm")})
 SCRATCH.update({n: _sb(256, "float32") for n in ("E", "wE", "Ls", "wu")})
 SCRATCH.update({n: _sb(256, "float16") for n in ("E16", "mA", "mE")})
-SCRATCH.update({n: _sb(256, "bfloat16") for n in ("mB", "sg", "cc", "ts", "comp", "val", "win", "cum", "fA", "arow", "ovT")})
-SCRATCH.update({n: _sb(72, "bfloat16") for n in ("qs0", "qs1", "qs2", "land0", "land1", "land2")})
+SCRATCH.update({n: _sb(256, "bfloat16") for n in ("mB", "sg", "cc", "ts", "comp", "val", "win", "cum", "fA", "arow", "ovT", "sT", "su")})
+SCRATCH.update({n: _sb(68, "bfloat16") for n in ("qs0", "qs1", "qs2", "land0", "land1", "land2")})
 SCRATCH.update({n: _sb(144, "bfloat16") for n in ("Wp", "Wn", "W2", "On")})
-SCRATCH.update({n: _sb(128, "bfloat16") for n in ("ones", "identB", "IB", "cU", "cPh", "blkT", "blkB", "kmat")})
+SCRATCH.update({n: _sb(128, "bfloat16") for n in ("identB", "I4k", "cU", "cPh", "blkT", "blkB", "kmat")})
+SCRATCH.update({"ones": _sb(192, "bfloat16"), "kmat2": _sb(128, "bfloat16"), "blkH": _sb(128, "float16"), "wh": _sb(256, "float16"),
+                "k4h": _sb(1, "float32"), "jn": _sb(512, "bfloat16"), "IB": _sb(128, "bfloat16")})
 SCRATCH.update({"identH": _sb(128, "float16"), "blkF": _sb(128, "float32")})
 SCRATCH.update({n: _sb(128, "int32") for n in ("iD", "iG", "iP")})
 SCRATCH.update({n: _sb(4, "int32") for n in ("Fi", "Li", "um")})
-SCRATCH.update({n: _sb(4, "float32") for n in ("c64", "inv", "cb")})
+SCRATCH.update({n: _sb(4, "float32") for n in ("c64", "inv", "cb", "fJ", "jB")})
 SCRATCH.update({n: _sb(1, "int32") for n in ("pI", "kI", "parI", "i7", "kri", "krm")})
-SCRATCH.update({n: _sb(1, "float32") for n in ("kcol", "negk", "wcol", "wneg", "w2", "k256", "k4k", "neg4k", "kap", "sa", "sc0", "ma",
+SCRATCH.update({n: _sb(1, "float32") for n in ("kcol", "negk", "wcol", "par", "k256", "k4k", "k4", "ua", "uc", "kap", "sa", "sc0", "ma",
                                                 "mc", "lo7", "hi7", "bk")})
 SCRATCH.update({n: ("psum", [128, 512], "float32") for n in ("pU0", "pU1", "pE", "pA", "pB", "pZ", "pY0", "pY1")})
 SEMAPHORES = (["cV", "cS", "cP", "cG", "sent"] + ["arr%d" % t for t in range(3)] + ["d%d" % i for i in range(24)])
@@ -118,9 +124,10 @@ def rank_program(g, core, T, topo):
     rounds = 3
     V, S, P = g.vector, g.scalar, g.tensor
     Q = {"V": V, "S": S, "P": P, "G": g, "Y": g.sync}
-    calls, turn, ends = [], [0], []
+    calls, turn, ends, signs = [], [0], [], {}
 
     def op(q, c, f, R, W, B=()):
+        c += START.get(q, 0)
         calls.append((q, c, c, R, W, B, f))
 
     def dma(q, out, in_, R, W, c):
@@ -171,8 +178,8 @@ def rank_program(g, core, T, topo):
     EE, MM = ["E0", "E1"], ["mB0", "mB1"]
     dma("S", T.ledI[:], T.led[:], [], ["ledI"], LOAD)
     dma("S", T.mB[:], T.mk[:], [], MM, LOAD + 300)
-    dma("Y", T.XT[:, 0:3072], T.xt[:, 0:3072], [], ["X0", "X1", "X2"], LOAD + 3300)
-    dma("Y", T.XT[:, 3072:4096], T.xt[:, 3072:4096], [], ["X3"], LOAD + 4200)
+    dma("Y", T.XT[:, 0:3072], T.xt[:, 0:3072], [], ["X0", "X1", "X2"], LOAD + 2900)
+    dma("Y", T.XT[:, 3072:4096], T.xt[:, 3072:4096], [], ["X3"], LOAD + 3700)
     XP = ["X0", "X1", "X2", "X3", "C", "T1"]
     NP = ["N0", "N1", "N2", "N3"]
     XALL = XP + NP
@@ -183,48 +190,49 @@ def rank_program(g, core, T, topo):
     iota(T.iD[:], [[1, 128]], 0, -1, ["iD"])
     iota(T.iS[:], [[1, 144]], -15, -1, ["iS"])
     iota(T.iG[:], [[-16, 8], [0, 16]], 0, 1, ["iG"])
-    iota(T.fA[:], [[1, 256]], 0, 0, ["fA"], True)
-    iota(T.fJ[:, 0:4 * wide], [[-1, 4], [0, wide]], -1, 0, ["fJ"], True)
+    iota(T.arow[:], [[512, 256]], -128 * 512, 0, ["arow"], True)
+    iota(T.fJ[:], [[1, 4]], 0, 0, ["fJ"], True)
     iota(T.c64[:], [[64, 4]], 0, 0, ["c64"], True)
     iota(T.Qb[:, 4096:4112], [[0, 16]], 0, 0, ["Qx"], True)
-    for t in range(rounds):
-        iota(T["qs%d" % t][:, 64:72], [[0, 8]], 0, 0, ["qi%d" % t], True)
     vms(T.XT[:, ZC:ZC + 16], 0.0, ["C"])
     vms(T.XT[:, C15:C15 + 1], 2048.0, ["C"])
     vms(T.XT[:, SP:AW:64], 0.0, ["T1"])
     vms(T.zero[:], 0.0, ["zero"], 512)
-    vms(T.ones[:], 1.0, ["ones"])
+    vms(T.ones[:], 1.0, ["ones"], 96)
     vms(T.cU[:], 6144.0, ["cU"])
     for name, bits in (("kI", 15), ("parI", 1), ("i7", 7)):
         vts(T[name][:], T.pI[:], bits, ALU.bitwise_and, None, None, ["pI"], [name])
-    for name, src, a, b in (("ma", "parI", NOFF, -NOFF), ("mc", "parI", -NOFF, NOFF + 2048), ("sa", "parI", -0.0625, 0),
-                            ("sc0", "parI", 0.0625, -0.03125), ("negk", "kI", -1, 0), ("kcol", "kI", 1, 0), ("wcol", "kI", 2, 1),
-                            ("wneg", "kI", -2, -1), ("w2", "kI", 4, 2), ("k256", "kI", 256, 0), ("k4k", "kI", 4096, 0),
-                            ("neg4k", "kI", -4, 0), ("bk", "kI", -LAM, LOW)):
+    for name, src, a, b in (("ma", "parI", NOFF, -NOFF), ("mc", "parI", -NOFF, NOFF + 2048), ("negk", "kI", -1, 0), ("kcol", "kI", 1, 0),
+                            ("par", "parI", 1, 0)):
         vts(T[name][:], T[src][:], float(a), ALU.mult, float(b), ALU.add, [src], [name])
+    for name, src, a, b in (("wcol", "kcol", 2, 1), ("sa", "par", -0.0625, 0),
+                            ("sc0", "par", 0.0625, -0.03125), ("k256", "kcol", 256, 0), ("k4k", "kcol", 4096, 0), ("k4h", "kcol", 4096, 2048), ("k4", "kcol", 4, 0.5),
+                            ("bk", "kcol", -LAM, LOW)):
+        sact(T[name][:], T[src][:], ACT.Copy, [src], [name], bias=float(b), scale=float(a))
     vts(T.lo7[:], T.i7[:], 7, ALU.is_equal, float(C15), ALU.mult, ["i7"], ["lo7"])
     vts(T.hi7[:], T.i7[:], 7, ALU.is_equal, float(ZC), ALU.add, ["i7"], ["hi7"])
     for par in range(2):
         for b in range(2):
             j = 2 * par + b
             vts(T.prm[:, 128 * j:128 * j + 128], T.iP[:], 1000 * b - par, ALU.is_equal, None, None, ["iP"], ["perm%d" % j], c=128)
-    for name, w in (("identH", 1.0), ("identB", 1.0), ("IB", -BIG)):
-        vts(T[name][:], T.iD[:], 0, ALU.is_equal, w, ALU.mult, ["iD"], [name], c=128)
-    for name, w in (("Wn", "wneg"), ("W2", "w2"), ("Wp", "wcol"), ("On", None)):
-        vts(T[name][:], T.iS[:], col("negk"), ALU.is_equal, col(w) if w else 1.0, ALU.mult, ["iS", "negk", w], [name], c=144)
-    for name, w in (("blkT", PART), ("blkB", -BIG), ("blkF", 1.0), ("kmat", col("k4k"))):
-        vts(T[name][:], T.iG[:], col("kcol"), ALU.is_equal, w, ALU.mult, ["iG", "kcol", "k4k"], [name], c=128)
-    sact(T.arow[:], T.fA[:], ACT.Copy, ["fA"], ["arow"], scale=512.0, c=256)
-    sact(T.jneg[:, 0:4 * wide], T.fJ[:, 0:4 * wide], ACT.Identity, ["fJ", "neg4k"], ["jneg"], bias=col("neg4k"), c=4 * wide)
-    sact(T.cPh[:], T.ones[:], ACT.Exp, ["ones"], ["cPh"], scale=LAM + LOW + math.log(PART / 128), c=1700)
+    for name in ("identH", "identB"):
+        vts(T[name][:], T.iD[:], 0, ALU.is_equal, None, None, ["iD"], [name], c=128)
+    vts(T.On[:], T.iS[:], col("negk"), ALU.is_equal, None, None, ["iS", "negk"], ["On"], c=144)
+    for name in ("blkF", "blkH"):
+        vts(T[name][:], T.iG[:], col("kcol"), ALU.is_equal, None, None, ["iG", "kcol"], [name], c=128)
+    for name, src, w in (("Wp", "On", "wcol"), ("Wn", "Wp", -1.0), ("W2", "Wp", 2.0), ("blkT", "blkF", PART), ("blkB", "blkF", -BIG),
+                         ("kmat", "blkF", "k4k"), ("kmat2", "blkF", "k4h")):
+        sact(T[name][:], T[src][:], ACT.Copy, [src, w], [name], scale=col(w) if w in SCRATCH else w, c=144)
+    vts(T.jB[:], T.fJ[:], col("k4"), ALU.add, BIG, ALU.mult, ["fJ", "k4"], ["jB"])
+    sact(T.cPh[:], T.ones[:, 0:128], ACT.Exp, ["ones"], ["cPh"], scale=LAM + LOW + math.log(PART / 128), c=1700)
 
     def sel(name, k):
         return T[name][:, 15 - k:143 - k]
 
     E8 = ["E8_%d" % i for i in range(4)]
 
-    def lists():
-        vts(T.E16[:], T.E[:], -2048.0, ALU.add, None, None, EE, ["E16"], c=256)
+    def lists(src="E"):
+        vts(T.E16[:], T[src][:], -2048.0, ALU.add, None, None, EE if src == "E" else [src], ["E16"], c=256)
         vts(T.mA[:], T.mB[:], -float(NOFF), ALU.mult, NOFF + 2048.0, ALU.add, MM, ["mA"], c=128)
         vts(T.mE[:], T.mB[:], col("ma"), ALU.mult, col("mc"), ALU.add, MM + ["ma", "mc"], ["mE"], c=128)
         for bank, par, srcs in (("pY0", 0, ("E16", "mA")), ("pY1", 1, ("E16", "mA")), ("pB", 1, ("E16",))):
@@ -239,14 +247,16 @@ def rank_program(g, core, T, topo):
         vts(T.LL[:, 128:256], T.pB[:, 0:128], 2048.0, ALU.add, None, None, ["pB_0", "pB_1"], ["LX"], ["pB"], 128)
         sact(T.sg[:], T.mB[:], ACT.Identity, MM + ["sa", "sc0"], ["sg"], bias=col("sc0"), scale=col("sa"), c=256)
 
+    lists("ledI")
     vcp(T.E[:], T.ledI[:], ["ledI"], EE, c=256)
-    lists()
     for b in range(4):
         x, neg = T.XT[:, b * 1024:(b + 1) * 1024], T.XT[:, NOFF + b * 1024:NOFF + (b + 1) * 1024]
+        q = "S" if b == 1 else "V"
+        made = [w for c in calls if c[0] == q and c[1] == c[2] for w in c[4]] if b < 2 else []
         if b == 1:
-            sact(neg, x, ACT.Copy, ["X1"], ["N1"], scale=-1.0, c=1024)
+            sact(neg, x, ACT.Copy, ["X1"] + made, ["N1"], scale=-1.0, c=1024)
         else:
-            vts(neg, x, -1.0, ALU.mult, None, None, ["X%d" % b], ["N%d" % b], c=512)
+            vts(neg, x, -1.0, ALU.mult, None, None, ["X%d" % b] + made, ["N%d" % b], c=512)
 
     def ca(i):
         return slice(i * 64, (i + 1) * 64)
@@ -294,33 +304,41 @@ def rank_program(g, core, T, topo):
             else:
                 sact(out, od, ACT.Sign, ["Qo" + s], ["po%d_%d" % (i, h)], c=m // 2)
 
-    def upl(i):
-        n = "pU%d" % (i % 2)
-        return n, T[n][:, ca(i // 2)]
+    def upl(b):
+        n, lo, w = "pU%d" % (b % 2), 64 * sum(len(x) for x in HASHED[b % 2:b:2]), 64 * len(HASHED[b])
+        return n, T[n][:, lo:lo + w], slice(64 * HASHED[b][0], 64 * HASHED[b][0] + w)
 
-    def hashes(i, t):
-        (n, o), a, s = upl(i), ca(i), str(i)
-        mms = [(o, T.cU[:], T.ones[:, 0:64], True, False)]
+    def hashes(b, t):
+        (n, o, a), s, cs = upl(b), str(b), HASHED[b]
+        w = 64 * len(cs)
+
+        def rows(buf, k):
+            return buf[:, 16 * a.start + k:16 * a.stop:16]
+
+        def of(name):
+            return ["%s%d" % (name, i) for i in cs]
+
+        mms = [(o, T.cU[:], T.ones[:, 0:w], True, False)]
         for k in range(0, 16, 2):
-            mms += [(o, sel("Wn", k), line(T.Qb, i, k), False, False), (o, sel("W2", k), line(T.Bb, i, k), False, False)]
-        group(mms, ["cU", "ones", "Wn", "W2", "Qe" + s] + parts("Be", i), [n, "u" + s], [n])
-        group([(o, sel("Wp", k), line(T.Qb, i, k), False, k == 15) for k in range(1, 16, 2)], ["Wp", "Qo" + s], [n, "u" + s], [n])
-        if OPT["cc"][i] == "V":
-            vts(T.cc[:, a], o, -2047.5, ALU.add, None, None, ["u" + s], ["cc" + s], [n])
+            mms += [(o, sel("Wn", k), rows(T.Qb, k), False, False), (o, sel("W2", k), rows(T.Bb, k), False, False)]
+        group(mms, ["cU", "ones", "Wn", "W2"] + of("Qe") + [x for i in cs for x in parts("Be", i)], [n, "u" + s], [n], w)
+        group([(o, sel("Wp", k), rows(T.Qb, k), False, k == 15) for k in range(1, 16, 2)], ["Wp"] + of("Qo"), [n, "u" + s], [n], w)
+        if OPT["cc"][cs[0]] == "V":
+            vts(T.cc[:, a], o, -2047.5, ALU.add, None, None, ["u" + s], ["cc" + s], [n], w)
         else:
-            sact(T.cc[:, a], o, ACT.Copy, ["u" + s], ["cc" + s], [n], bias=-2047.5)
-        vtt(o, o, T.cc[:, a], ALU.subtract, ["u" + s, "cc" + s], ["u" + s], [n])
-        ek = T.pE[:, a] if t == 0 else T.pE[:, 256 + 64 * i:256 + 64 * i + 64]
-        vtt(T.eu[:, a], o, T.E[:, a], ALU.mult, ["u" + s, "E%d" % (i // 2)], ["eu" + s], [n])
-        vts(T.wv[:, a], T.eu[:, a], 5, ALU.arith_shift_right, 4095, ALU.bitwise_and, ["eu" + s], ["wv" + s])
-        vtt(T.hs[:, a], ek, T.wv[:, a], ALU.add, ["wv" + s, "E8_" + s, "Ek"], ["hs" + s], ["pE"])
-        vts(T.hm[:, a], T.hs[:, a], 4095 + NOFF, ALU.bitwise_and, None, None, ["hs" + s], ["hm" + s])
-        vcp(T.LY[:, a], T.hm[:, a], ["hm" + s], ["LY" + s])
+            sact(T.cc[:, a], o, ACT.Copy, ["u" + s], ["cc" + s], [n], bias=-2047.5, c=w)
+        vtt(o, o, T.cc[:, a], ALU.subtract, ["u" + s, "cc" + s], ["u" + s], [n], w)
+        ek = T.pE[:, a] if t == 0 else T.pE[:, 256 + a.start:256 + a.stop]
+        vtt(T.eu[:, a], o, T.E[:, a], ALU.mult, ["u" + s, "E%d" % (cs[0] // 2)], ["eu" + s], [n], w)
+        vts(T.wv[:, a], T.eu[:, a], 5, ALU.arith_shift_right, 4095, ALU.bitwise_and, ["eu" + s], ["wv" + s], c=w)
+        vtt(T.hs[:, a], ek, T.wv[:, a], ALU.add, ["wv" + s, "Ek"] + of("E8_"), ["hs" + s], ["pE"], w)
+        vts(T.hm[:, a], T.hs[:, a], 4095 + NOFF, ALU.bitwise_and, None, None, ["hs" + s], of("hm"), c=w)
+        vcp(T.LY[:, a], T.hm[:, a], of("hm"), of("LY"), c=w)
 
     def region(i, j, whole=False):
         b = [i in x for x in BLOCKS].index(True)
         n, w = "pA" if b % 2 == 0 else "pB", len(BLOCKS[b])
-        lo = j * w + (0 if whole else i - BLOCKS[b][0]) + (4 if w == 1 and b >= 2 and len(BLOCKS[b - 2]) == 1 else 0)
+        lo = j * w + (0 if whole else i - BLOCKS[b][0]) + (4 if b >= 2 else 0)
         hi = lo + (w if whole else 1)
         return n, T[n][:, 64 * lo:64 * hi], ["%s_%d" % (n, x) for x in range(lo, hi)]
 
@@ -342,56 +360,67 @@ def rank_program(g, core, T, topo):
                 n = "pY%d" % (turn[0] % 2)
                 turn[0] += 1
                 o = T[n][:, 0:m]
-                group([(o, T.IB[:], T.Qb[:, c], True, False)], ["IB", "Qe" + s, "Qo" + s], [n], [n], m)
-                group([(o, T.IB[:], T.zb[:, c], False, True)], ["IB", z], [n], [n], m)
-                sact(T.sb[:, c], o, ACT.Sign, [n], [sg], [n], c=m)
+                group([(o, T.identB[:], T.Qb[:, c], True, False)], ["identB", "Qe" + s, "Qo" + s], [n], [n], m)
+                group([(o, T.identB[:], T.zb[:, c], False, True)], ["identB", z], [n], [n], m)
+                sact(T.sb[:, c], o, ACT.Sign, [n], [sg], [n], scale=-1.0, c=m)
             lo += n_acc
         n, o, w = region(i, 0)
         group([(o, sel("On", k), line(T.sb, i, k), k == 0, k == 15) for k in range(16)], ["On"] + names, w, [n])
 
     def counts(b):
-        n, s, c = "pU%d" % b, str(b), slice(128 * b, 128 * b + 128)
+        n, s, c = "pZ", str(b), slice(128 * b, 128 * b + 128)
         group([(T[n][:, 256 + k:384:16], (T.po if k % 2 else T.pe)[:, b * 1024 + k // 2:(b + 1) * 1024:8], T.On[:, 15:143:16], True, True)
-               for k in range(16)], ["On"] + [x for i in (2 * b, 2 * b + 1) for x in parts("pe", i) + parts("po", i)], [n, "cnt" + s], [n])
-        sact(T.ovT[:, c], T[n][:, 256:384], ACT.Sign, ["cnt" + s], ["ovT" + s], [n], bias=-8.5, c=128)
-        group([(T[n][:, 384:512], T.ones[:], T.identB[:], True, False), (T[n][:, 384:512], T.ovT[:, c], T.identB[:], False, True)],
-              ["ones", "identB", "ovT" + s], [n, "ov" + s], [n], 128)
-        vtt(T.ts[:, c], T[n][:, 384:512], T.sg[:, c], ALU.mult, ["ov" + s, "sg"], ["gov" + s], [n], 128)
+               for k in range(16)], ["On"] + [x for i in (2 * b, 2 * b + 1) for x in parts("pe", i) + parts("po", i)], ["cnt"], [n])
+        sact(T.ovT[:, c], T[n][:, 256:384], ACT.Sign, ["cnt"], ["ovT" + s], [n], bias=-8.5, c=128)
+        group([(T[n][:, 384:512], T.ones[:, 0:128], T.identB[:], True, False), (T[n][:, 384:512], T.ovT[:, c], T.identB[:], False, True)],
+              ["ones", "identB", "ovT" + s], ["ov"], [n], 128)
+        vtt(T.ts[:, c], T[n][:, 384:512], T.sg[:, c], ALU.mult, ["ov", "sg"], ["gov" + s], [n], 128)
 
     def decide(b):
         i, w = BLOCKS[b][0], 64 * len(BLOCKS[b])
         a, s, ones = slice(64 * i, 64 * i + w), str(b), T.ones[:, 0:w]
-        (n, score, nS), (_, cap, nC), (_, total, nT), (_, ln, nL) = [region(i, j, True) for j in range(4)]
-        won = ["win%d" % x for x in BLOCKS[b]]
-        vtt(T.comp[:, a], score, T.ts[:, a], ALU.mult, nS + ["gov%d" % (i // 2)], ["comp" + s], [n], w)
+        (n, score, nS), (_, total, nT), (_, ln, nL) = [region(i, j, True) for j in (0, 0, 1)]
+        won, short = ["win%d" % x for x in BLOCKS[b]], b in SHORT
+        vtt(T.comp[:, a], score, T.ts[:, a], ALU.mult, nS + ["gov%d" % (x // 2) for x in BLOCKS[b]], ["comp" + s], [n], w)
         sact(T.val[:, a], T.comp[:, a], ACT.Exp, ["comp" + s, "bk"], ["val" + s], bias=col("bk"), scale=16 * 17 * LAM, c=w)
-        group([(total, T.cPh[:], ones, True, False), (total, T.blkT[:], T.val[:, a], False, True)],
-              ["cPh", "ones", "blkT", "val" + s], nT, [n], w)
+        group([(total, T.cPh[:], ones, True, False)], ["cPh", "ones"], nT, [n], w)
+        group([(total, T.blkT[:], T.val[:, a], False, True)], ["blkT", "val" + s], nT, [n], w)
         vtt(T.win[:, a], total, T.val[:, a], ALU.is_lt, nT + ["val" + s], won, [n], w)
-        for x in BLOCKS[b]:
-            vtt(T.wu[:, ca(x)], upl(x)[1], T.win[:, ca(x)], ALU.mult, ["u%d" % x, "win%d" % x], ["wu%d" % x], [upl(x)[0]])
+        for x, cs in enumerate(HASHED):
+            if cs[0] in BLOCKS[b]:
+                m, u, c = upl(x)
+                if short:
+                    sact(u, u, ACT.Copy, ["u%d" % x], ["u%d" % x], [m], bias=-2048.0, c=64 * len(cs))
+                vtt((T.wh if short else T.wu)[:, c], u, T.win[:, c], ALU.mult, ["u%d" % x] + won, ["wu%d" % y for y in cs], [m],
+                    64 * len(cs))
         vscan(T.cum[:, a], T.win[:, a], T.zero[:, 0:w], T.cum[:, 64 * i - 1:64 * i] if b else 0.0, ALU.add, ALU.add,
               won + ["zero"] + (["cum%d" % (b - 1)] if b else []), ["cum" + s])
-        group([(ln, T.ones[:], T.arow[:, a], True, False), (ln, T.kmat[:], T.win[:, a], False, False),
-               (ln, T.blkF[:], T.wu[:, a], False, True)], ["ones", "arow", "kmat", "blkF"] + won + ["wu%d" % x for x in BLOCKS[b]],
-              nL, [n], w, 1)
-        sact(T.Ls[:, a], ln, ACT.Copy, nL, ["Ls" + s], [n], c=w)
-        group([(T.pZ[:, 0:4 * wide], T.IB[:], T.jneg[:, 0:4 * wide], True, False)], ["IB", "jneg"], ["pZ"], ["pZ"], 4 * wide)
-        group([(T.pZ[:, wide * j:wide * j + w], T.blkB[:], T.cum[:, a], False, j == 3) for j in range(4)], ["blkB", "cum" + s],
-              ["pZ"], ["pZ"], w)
+        group([(ln, T.ones[:, 0:128], T.arow[:, a], True, False), (ln, (T.kmat2 if short else T.kmat)[:], T.win[:, a], False, False)],
+              ["ones", "arow", "kmat", "kmat2"] + won, nL, [n], w)
+        group([(ln, T.blkH[:], T.wh[:, a], False, True) if short else (ln, T.blkF[:], T.wu[:, a], False, True)],
+              ["blkF", "blkH"] + ["wu%d" % x for x in BLOCKS[b]], nL, [n], w, 0 if short else 1)
+        who = PLACES[b]
+        if "V" in who:
+            group([(T.pY0[:, a], T.blkB[:], T.cum[:, a], True, True)], ["blkB", "cum" + s], ["pY0"], ["pY0"], w)
+        if "S" in who:
+            group([(T.pZ[:, a], T.blkB[:], T.cum[:, a], True, True)], ["blkB", "cum" + s], ["pZ" + s], ["pZ"], w)
         for j in range(4):
             o = 256 * j + 64 * i
-            vscan(T.F[:, o:o + w], T.Ls[:, a], T.pZ[:, wide * j:wide * j + w], T.F[:, o - 1:o] if b else BIG, ALU.min, ALU.max,
-                  ["Ls" + s, "pZ", "F%d" % j], ["F%d" % j], w, ["pZ"])
+            if who[j] == "V":
+                vts(T.Pn[:, o:o + w], T.pY0[:, a], T.jB[:, j:j + 1], ALU.add, None, None, ["pY0", "jB"], ["Pn%d%s" % (j, s)], ["pY0"], w)
+            else:
+                sact(T.Pn[:, o:o + w], T.pZ[:, a], ACT.Identity, ["pZ" + s, "jB"], ["Pn%d%s" % (j, s)], ["pZ"], bias=T.jB[:, j:j + 1], c=w)
+            vscan(T.F[:, o:o + w], ln, T.Pn[:, o:o + w], T.F[:, o - 1:o] if b else BIG, ALU.min, ALU.max,
+                  nL + ["Pn%d%s" % (j, s), "F%d" % j], ["F%d" % j], w, [n])
 
     def send(t):
         FF, qs, found = ["F%d" % j for j in range(4)], T["qs%d" % t], T.F[:, 255:1024:256]
-        vts(T.Fi[:], found, BIG, ALU.min, None, None, FF, ["Fi"])
-        vts(T.Li[:], T.Fi[:], 12, ALU.arith_shift_right, None, None, ["Fi"], ["Li"])
-        vcp(T.LJ[:], T.Li[:], ["Li"], ["LJ"])
+        vts(T.Li[:], found, -2047.5, ALU.add, 1.0 / 4096, ALU.mult, FF, ["Li"])
+        vts(T.Fi[:], found, BIG / 2, ALU.min, None, None, FF, ["Fi"])
+        vts(T.LJ[:], T.Li[:], 2048.0, ALU.add, 4096.0, ALU.min, ["Li"], ["LJ"])
         sact(qs[:, 0:64], T.Qb[:].indirect(T.LJ[:, 0:4]), ACT.Abs, ["LJ", "Qx"] + ["Q%s%d" % (x, i) for x in "eo" for i in range(4)],
              ["qs%d" % t], c=gat(64))
-        vts(T.inv[:], found, BIG, ALU.is_ge, float(SP), ALU.mult, FF, ["inv"])
+        vts(T.inv[:], found, BIG / 2, ALU.is_ge, float(SP), ALU.mult, FF, ["inv"])
         vts(T.um[:], T.Fi[:], 63, ALU.bitwise_and, None, None, ["Fi"], ["um"])
         vtt(T.cb[:], T.inv[:], T.c64[:], ALU.add, ["inv", "c64"], ["cb"])
         vtt(qs[:, 64:68], T.um[:], T.cb[:], ALU.add, ["um", "cb"], ["qi%d" % t])
@@ -406,7 +435,7 @@ def rank_program(g, core, T, topo):
         vtt(T.E[:, c], T.E[:, c], T.wE[:, c], ALU.add, ["E" + s, "wE" + s], ["E" + s], c=256)
 
     def kappa():
-        group([(T.pU0[:, 256:257], T.ones[:], T.cum[:, 255:256], True, True)], ["ones", "cum%d" % (len(BLOCKS) - 1)], ["pU0", "kp"], ["pU0"])
+        group([(T.pU0[:, 256:257], T.ones[:, 0:128], T.cum[:, 255:256], True, True)], ["ones", "cum%d" % (len(BLOCKS) - 1)], ["pU0", "kp"], ["pU0"])
         vcp(T.kri[:], T.pU0[:, 256:257], ["kp"], ["kri"], ["pU0"])
         vts(T.krm[:], T.kri[:], 31, ALU.bitwise_and, None, None, ["kri"], ["krm"])
         vcp(T.kap[:], T.krm[:], ["krm"], ["kap"])
@@ -427,18 +456,21 @@ def rank_program(g, core, T, topo):
         last = t == rounds - 1
         for i in range(4):
             amounts(i)
-            hashes(i, t)
-            scores(i)
+            for b, chunks in enumerate(HASHED):
+                if chunks[-1] == i:
+                    hashes(b, t)
             if i % 2:
                 counts(i // 2)
+        for i in range(4):
+            scores(i)
         for b in range(len(BLOCKS)):
             decide(b)
         for b in range(2):
             update(b)
         send(t)
         if last:
-            dma("Y", T.ym[:], T.mB[:], MM, ["ym"], LOAD)
-            dma("S", T.yl[:], T.E[:], EE, ["yl"], LOAD)
+            dma("S", T.yl[:], T.E[:], EE + ["land%d" % t], ["yl"], LOAD)
+            dma("S", T.ym[:], T.mB[:], MM + ["land%d" % t], ["ym"], LOAD)
         else:
             lists()
             kappa()
@@ -459,6 +491,8 @@ def rank_program(g, core, T, topo):
         toks = [lastw[x] for x in list(R) + list(W) if x in lastw]
         toks += [y for x in W for y in readers.get(x, [])]
         toks += [y for b in B for qq, y in banks.get(b, {}).items() if qq != q]
+        if q == "P":
+            toks = [y for y in toks if y[2] != q]
         k = known[q]
         for sem, val, _, snap, _ in sorted(toks, key=lambda y: -y[4]):
             if k.get(sem, 0) < val:

import math
from concourse.mybir import AluOpType as ALU, ActivationFunctionType as ACT

ZC, C15, SP, NOFF = 4096, 4097, 4160, 16384
GW = NOFF + 4096
AW = SP + 4096
WEND = NOFF + AW
NENG = 8
LAM, LOW, PART = 0.6, -78.0, 0.4
BIG = float(2 ** 24)

OPT = dict(cc="SSVV", gE="VSSS", gB="SSSS", relu="VVVV", over="SSSV")
PIECES = [[(32, "S", "S")] * 2, [(32, "S", "S"), (32, "V", "V")], [(32, "S", "S"), (32, "V", "S")], [(32, "V", "S"), (32, "V", "V")]]
HASHED = [(0,), (1,), (2,), (3,)]
BLOCKS = [(0, 1), (2, 3)]
SHORT = (1,)
PLACES = ["SSSS", "VVSS"]
SPLIT = 1
GATHER, SCATTER, MATMUL, WAKE, LOAD, FLIGHT, SLACK = 1.4, 3.8, 0.6, 195, 1800, 3000, 50
START = {"V": 25, "S": 65}
SWEEPS, JITTER = 120, 600
ORDER = []


def _sb(cols, dt):
    return ("sbuf", [128, cols], dt)


SCRATCH = {"XT": _sb(WEND, "bfloat16"), "Qb": _sb(4096 + 16, "bfloat16"), "F": _sb(1024, "float32"), "LL": _sb(384, "uint16"),
           "ND": _sb(128, "int32"), "tx": _sb(64, "float32"), "LI": _sb(4, "uint16"), "LJ": _sb(4, "uint16"),
           "zero": _sb(1024, "bfloat16"), "iS": _sb(144, "int32"), "LY": _sb(256, "uint16"),
           "prm": _sb(512, "float16"), "Pn": _sb(1024, "float32")}
SCRATCH.update({n: _sb(4096, "bfloat16") for n in ("Bb", "bb", "zb", "sb")})
SCRATCH.update({n: _sb(2048, "bfloat16") for n in ("pe", "po")})
SCRATCH.update({n: _sb(256, "int32") for n in ("ledI", "eu", "wv", "hs", "hm")})
SCRATCH.update({n: _sb(256, "float32") for n in ("E", "wE", "Ls", "wu")})
SCRATCH.update({n: _sb(256, "float16") for n in ("E16", "mA", "mE")})
SCRATCH.update({n: _sb(256, "bfloat16") for n in ("mB", "sg", "cc", "ts", "comp", "val", "win", "cum", "fA", "arow", "ovT", "sT", "su")})
SCRATCH.update({n: _sb(68, "bfloat16") for n in ("qs0", "qs1", "qs2", "land0", "land1", "land2")})
SCRATCH.update({n: _sb(144, "bfloat16") for n in ("Wp", "Wn", "W2", "On")})
SCRATCH.update({n: _sb(128, "bfloat16") for n in ("identB", "I4k", "cU", "cPh", "blkT", "blkB", "kmat")})
SCRATCH.update({"ones": _sb(192, "bfloat16"), "kmat2": _sb(128, "bfloat16"), "blkH": _sb(128, "float16"), "wh": _sb(256, "float16"),
                "k4h": _sb(1, "float32"), "jn": _sb(512, "bfloat16"), "IB": _sb(128, "bfloat16")})
SCRATCH.update({"identH": _sb(128, "float16"), "blkF": _sb(128, "float32")})
SCRATCH.update({n: _sb(128, "int32") for n in ("iD", "iG", "iP")})
SCRATCH.update({n: _sb(4, "int32") for n in ("Fi", "Li", "um")})
SCRATCH.update({n: _sb(4, "float32") for n in ("c64", "inv", "cb", "fJ", "jB")})
SCRATCH.update({n: _sb(1, "int32") for n in ("pI", "kI", "parI", "i7", "kri", "krm")})
SCRATCH.update({n: _sb(1, "float32") for n in ("kcol", "negk", "wcol", "par", "k256", "k4k", "k4", "ua", "uc", "kap", "sa", "sc0", "ma",
                                                "mc", "lo7", "hi7", "bk")})
SCRATCH.update({n: ("psum", [128, 512], "float32") for n in ("pU0", "pU1", "pE", "pA", "pB", "pZ", "pY0", "pY1")})
SEMAPHORES = (["cV", "cS", "cP", "cG", "sent"] + ["arr%d" % t for t in range(3)] + ["d%d" % i for i in range(24)])


def in_order(calls):
    n = len(calls)
    lastw, readers, pre, post = {}, {}, [], [[] for _ in calls]
    for i, (q, _, _, R, W, _, _) in enumerate(calls):
        p = {lastw[t] for t in list(R) + list(W) if t in lastw} | {j for t in W for j in readers.get(t, [])}
        pre.append(sorted(p))
        for j in p:
            post[j].append(i)
        for t in R:
            readers.setdefault(t, []).append(i)
        for t in W:
            lastw[t], readers[t] = i, []

    def sweep(pre, post, rank):
        left = [len(p) for p in pre]
        ready = {i: 0 for i in range(n) if not left[i]}
        done, free, bank, order = [0] * n, {}, {}, []
        while ready:
            st = {i: max([r, free.get(calls[i][0], 0)] + [bank[b][1] + WAKE for b in calls[i][5] if b in bank and bank[b][0] != calls[i][0]])
                  for i, r in ready.items()}
            first = min(ready, key=lambda i: (st[i], -rank[i]))
            i = max((i for i in ready if calls[i][0] == calls[first][0] and st[i] <= st[first] + SLACK), key=lambda i: rank[i])
            free[calls[i][0]], done[i] = st[i] + calls[i][1], st[i] + calls[i][2]
            for b in calls[i][5]:
                bank[b] = (calls[i][0], done[i])
            del ready[i]
            order.append(i)
            for j in post[i]:
                left[j] -= 1
                if not left[j]:
                    ready[j] = max(done[x] for x in pre[j]) + WAKE
        return done, order

    def pack(pre, order):
        start, done, busy = [0] * n, [0] * n, {}
        for i in order:
            q, hold, length, _, _, banks, _ = calls[i]
            s = max([done[j] + WAKE for j in pre[i]], default=0)
            for a, b in sorted(busy.get(q, []) + [(a - WAKE, b + WAKE) for x in banks for a, b, o in busy.get(x, []) if o != q]):
                if b > s:
                    if s + hold <= a:
                        break
                    s = b
            start[i], done[i] = s, s + length
            busy.setdefault(q, []).append((s, s + hold))
            for x in banks:
                busy.setdefault(x, []).append((s, s + hold, q))
        return start, done

    rank, best, seed = [-i for i in range(n)], None, 1
    for _ in range(SWEEPS):
        _, order = sweep(pre, post, rank)
        for _ in range(3):
            start, done = pack(pre, order)
            if best is None or max(done) < max(best[1]):
                best = (start, done)
            _, back = pack(post, sorted(range(n), key=lambda i: (-done[i], -i)))
            order = sorted(range(n), key=lambda i: (-back[i], i))
        seed = (seed * 1103515245 + 12345) % 2 ** 31
        rank, _ = sweep(post, pre, [d + JITTER * ((seed * (i + 1) * 2654435761 >> 16) % 1024) / 1024 for i, d in enumerate(best[1])])
    loads = [i for i in range(n) if not calls[i][3] and calls[i][1] < calls[i][2]]
    return loads + sorted(set(range(n)) - set(loads), key=lambda i: (best[0][i], i))


def rank_program(g, core, T, topo):
    rank = T.rank_of(core)
    if rank is None:
        return
    n_ranks = len(T.cores)
    rounds = 3
    V, S, P = g.vector, g.scalar, g.tensor
    Q = {"V": V, "S": S, "P": P, "G": g, "Y": g.sync}
    calls, turn, ends, signs = [], [0], [], {}

    def op(q, c, f, R, W, B=()):
        c += START.get(q, 0)
        calls.append((q, c, c, R, W, B, f))

    def dma(q, out, in_, R, W, c):
        calls.append((q, 100, c, R, W, (), ("dma", out, in_)))

    def vts(out, in0, s1, o0, s2, o1, R, W, B=(), c=64):
        if o1 is None:
            op("V", c, lambda: V.tensor_scalar(out, in0, s1, None, o0), R, W, B)
        else:
            op("V", c, lambda: V.tensor_scalar(out, in0, s1, s2, o0, o1), R, W, B)

    def vtt(out, a, b, o, R, W, B=(), c=64):
        op("V", c, lambda: V.tensor_tensor(out, a, b, o), R, W, B)

    def vcp(out, in_, R, W, B=(), c=64):
        op("V", c, lambda: V.tensor_copy(out, in_), R, W, B)

    def vms(ap, x, W, c=64):
        op("V", c, lambda: V.memset(ap, x), [], W)

    def vscan(out, a, b, init, o0, o1, R, W, c=64, B=()):
        op("V", c, lambda: V.tensor_tensor_scan(out, a, b, init, o0, o1), R, W, B)

    def sact(out, in_, f, R, W, B=(), bias=0.0, scale=1.0, c=64):
        op("S", c, lambda: S.activation(out, in_, f, bias=bias, scale=scale), R, W, B)

    def iota(out, pat, base, cm, W, small=False):
        c = 160 + 2 * math.prod(n for _, n in pat)
        if small:
            op("G", c, lambda: g.iota(out, pat, base, cm, allow_small_or_imprecise_dtypes=True), [], W)
        else:
            op("G", c, lambda: g.iota(out, pat, base, cm), [], W)

    def group(mms, R, W, B, n=64, wide=0):
        def f():
            r = None
            for m in mms:
                r = P.matmul(*m)
            return r
        op("P", (len(mms) + 3 * wide) * max(n, 64) * MATMUL, f, R, W, B)

    def col(name):
        return T[name][:, 0:1]

    def gat(n):
        return 70 + GATHER * n

    EE, MM = ["E0", "E1"], ["mB0", "mB1"]
    dma("S", T.ledI[:], T.led[:], [], ["ledI"], LOAD)
    dma("S", T.mB[:], T.mk[:], [], MM, LOAD + 300)
    dma("Y", T.XT[:, 0:3072], T.xt[:, 0:3072], [], ["X0", "X1", "X2"], LOAD + 2900)
    dma("Y", T.XT[:, 3072:4096], T.xt[:, 3072:4096], [], ["X3"], LOAD + 3700)
    XP = ["X0", "X1", "X2", "X3", "C", "T1"]
    NP = ["N0", "N1", "N2", "N3"]
    XALL = XP + NP

    wide = 64 * max(len(b) for b in BLOCKS)
    iota(T.pI[:], [[0, 1]], 0, 1, ["pI"])
    iota(T.iP[:], [[16, 8], [1000, 2], [2, 8]], 0, -1, ["iP"])
    iota(T.iD[:], [[1, 128]], 0, -1, ["iD"])
    iota(T.iS[:], [[1, 144]], -15, -1, ["iS"])
    iota(T.iG[:], [[-16, 8], [0, 16]], 0, 1, ["iG"])
    iota(T.arow[:], [[512, 256]], -128 * 512, 0, ["arow"], True)
    iota(T.fJ[:], [[1, 4]], 0, 0, ["fJ"], True)
    iota(T.c64[:], [[64, 4]], 0, 0, ["c64"], True)
    iota(T.Qb[:, 4096:4112], [[0, 16]], 0, 0, ["Qx"], True)
    vms(T.XT[:, ZC:ZC + 16], 0.0, ["C"])
    vms(T.XT[:, C15:C15 + 1], 2048.0, ["C"])
    vms(T.XT[:, SP:AW:64], 0.0, ["T1"])
    vms(T.zero[:], 0.0, ["zero"], 512)
    vms(T.ones[:], 1.0, ["ones"], 96)
    vms(T.cU[:], 6144.0, ["cU"])
    for name, bits in (("kI", 15), ("parI", 1), ("i7", 7)):
        vts(T[name][:], T.pI[:], bits, ALU.bitwise_and, None, None, ["pI"], [name])
    for name, src, a, b in (("ma", "parI", NOFF, -NOFF), ("mc", "parI", -NOFF, NOFF + 2048), ("negk", "kI", -1, 0), ("kcol", "kI", 1, 0),
                            ("par", "parI", 1, 0)):
        vts(T[name][:], T[src][:], float(a), ALU.mult, float(b), ALU.add, [src], [name])
    for name, src, a, b in (("wcol", "kcol", 2, 1), ("sa", "par", -0.0625, 0),
                            ("sc0", "par", 0.0625, -0.03125), ("k256", "kcol", 256, 0), ("k4k", "kcol", 4096, 0), ("k4h", "kcol", 4096, 2048), ("k4", "kcol", 4, 0.5),
                            ("bk", "kcol", -LAM, LOW)):
        sact(T[name][:], T[src][:], ACT.Copy, [src], [name], bias=float(b), scale=float(a))
    vts(T.lo7[:], T.i7[:], 7, ALU.is_equal, float(C15), ALU.mult, ["i7"], ["lo7"])
    vts(T.hi7[:], T.i7[:], 7, ALU.is_equal, float(ZC), ALU.add, ["i7"], ["hi7"])
    for par in range(2):
        for b in range(2):
            j = 2 * par + b
            vts(T.prm[:, 128 * j:128 * j + 128], T.iP[:], 1000 * b - par, ALU.is_equal, None, None, ["iP"], ["perm%d" % j], c=128)
    for name in ("identH", "identB"):
        vts(T[name][:], T.iD[:], 0, ALU.is_equal, None, None, ["iD"], [name], c=128)
    vts(T.On[:], T.iS[:], col("negk"), ALU.is_equal, None, None, ["iS", "negk"], ["On"], c=144)
    for name in ("blkF", "blkH"):
        vts(T[name][:], T.iG[:], col("kcol"), ALU.is_equal, None, None, ["iG", "kcol"], [name], c=128)
    for name, src, w in (("Wp", "On", "wcol"), ("Wn", "Wp", -1.0), ("W2", "Wp", 2.0), ("blkT", "blkF", PART), ("blkB", "blkF", -BIG),
                         ("kmat", "blkF", "k4k"), ("kmat2", "blkF", "k4h")):
        sact(T[name][:], T[src][:], ACT.Copy, [src, w], [name], scale=col(w) if w in SCRATCH else w, c=144)
    vts(T.jB[:], T.fJ[:], col("k4"), ALU.add, BIG, ALU.mult, ["fJ", "k4"], ["jB"])
    sact(T.cPh[:], T.ones[:, 0:128], ACT.Exp, ["ones"], ["cPh"], scale=LAM + LOW + math.log(PART / 128), c=1700)

    def sel(name, k):
        return T[name][:, 15 - k:143 - k]

    E8 = ["E8_%d" % i for i in range(4)]

    def lists(src="E"):
        vts(T.E16[:], T[src][:], -2048.0, ALU.add, None, None, EE if src == "E" else [src], ["E16"], c=256)
        vts(T.mA[:], T.mB[:], -float(NOFF), ALU.mult, NOFF + 2048.0, ALU.add, MM, ["mA"], c=128)
        vts(T.mE[:], T.mB[:], col("ma"), ALU.mult, col("mc"), ALU.add, MM + ["ma", "mc"], ["mE"], c=128)
        for bank, par, srcs in (("pY0", 0, ("E16", "mA")), ("pY1", 1, ("E16", "mA")), ("pB", 1, ("E16",))):
            terms = [(s, b) for s in srcs for b in range(2)]
            group([(T[bank][:, 0:128], T.prm[:, 128 * (2 * par + b):128 * (2 * par + b + 1)], T[s][:, b:256:2], i == 0,
                    i == len(terms) - 1) for i, (s, b) in enumerate(terms)],
                  list(srcs) + ["perm%d" % (2 * par), "perm%d" % (2 * par + 1)], [bank + x for x in ("", "_0", "_1")], [bank], 128)
        group([(T.pE[:, 0:256], T.identH[:], T[s][:], s == "E16", s == "mE") for s in ("E16", "mE")], ["identH", "E16", "mE"],
              E8, ["pE"], 256)
        vts(T.LL[:, 256:384], T.pY1[:, 0:128], col("lo7"), ALU.max, col("hi7"), ALU.min, ["pY1", "lo7", "hi7"], ["LB"], ["pY1"], 128)
        vcp(T.LL[:, 0:128], T.pY0[:, 0:128], ["pY0"], ["LE"], ["pY0"], 128)
        vts(T.LL[:, 128:256], T.pB[:, 0:128], 2048.0, ALU.add, None, None, ["pB_0", "pB_1"], ["LX"], ["pB"], 128)
        sact(T.sg[:], T.mB[:], ACT.Identity, MM + ["sa", "sc0"], ["sg"], bias=col("sc0"), scale=col("sa"), c=256)

    lists("ledI")
    vcp(T.E[:], T.ledI[:], ["ledI"], EE, c=256)
    for b in range(4):
        x, neg = T.XT[:, b * 1024:(b + 1) * 1024], T.XT[:, NOFF + b * 1024:NOFF + (b + 1) * 1024]
        q = "S" if b == 1 else "V"
        made = [w for c in calls if c[0] == q and c[1] == c[2] for w in c[4]] if b < 2 else []
        if b == 1:
            sact(neg, x, ACT.Copy, ["X1"] + made, ["N1"], scale=-1.0, c=1024)
        else:
            vts(neg, x, -1.0, ALU.mult, None, None, ["X%d" % b] + made, ["N%d" % b], c=512)

    def ca(i):
        return slice(i * 64, (i + 1) * 64)

    def ce(i, par):
        return slice(i * 1024 + par, (i + 1) * 1024, 2)

    def lst(n, i):
        return T.LL[:, 128 * n + 32 * i:128 * n + 32 * i + 32]

    def line(buf, i, k):
        return buf[:, i * 1024 + k:(i + 1) * 1024:16]

    def parts(name, i):
        return ["%s%d_%d" % (name, i, h) for h in range(SPLIT)]

    def amounts(i):
        s, m = str(i), 1024 // SPLIT
        src = T.XT[:, 0:GW].indirect(lst(0, i))
        if OPT["gE"][i] == "V":
            vcp(T.Qb[:, ce(i, 0)], src, ["LE"] + XALL, ["Qe" + s], c=gat(512))
        else:
            sact(T.Qb[:, ce(i, 0)], src, ACT.Copy, ["LE"] + XALL, ["Qe" + s], c=gat(512))
        src = T.XT[:, 0:ZC + 16].indirect(lst(2, i))
        if OPT["gB"][i] == "V":
            vts(T.Bb[:, ce(i, 1)], src, -1.0, ALU.mult, None, None, ["LB"] + XP, ["Bo" + s], c=gat(512))
        else:
            sact(T.Bb[:, ce(i, 1)], src, ACT.Copy, ["LB"] + XP, ["Bo" + s], scale=-1.0, c=gat(512))
        cuts = [(h, i * 1024 + h * m) for h in range(SPLIT)]
        for h, lo in cuts:
            j, ev = "%d_%d" % (i, h), slice(lo, lo + m, 2)
            if OPT["relu"][i] == "V":
                vts(T.Bb[:, ev], T.Qb[:, ev], 0.0, ALU.max, None, None, ["Qe" + s], ["Be" + j], c=m // 4)
            else:
                sact(T.Bb[:, ev], T.Qb[:, ev], ACT.Relu, ["Qe" + s], ["Be" + j], c=m // 2)
            vscan(T.bb[:, lo:lo + m], T.Bb[:, lo:lo + m], T.zero[:, 0:m], 0.0, ALU.add, ALU.max, ["Be" + j, "Bo" + s, "zero"],
                  ["bb" + j], m // 2)
            vts(T.pe[:, lo // 2:(lo + m) // 2], T.Qb[:, ev], 0.0, ALU.not_equal, None, None, ["Qe" + s], ["pe" + j], c=m // 4)
        vtt(T.Qb[:, ce(i, 1)], T.XT[:, 0:4096].indirect(lst(1, i)), T.bb[:, ce(i, 0)], ALU.min, ["LX"] + parts("bb", i) + XP,
            ["Qo" + s], c=gat(512))
        for h, lo in cuts:
            out, od = T.po[:, lo // 2:(lo + m) // 2], T.Qb[:, lo + 1:lo + m:2]
            if OPT["over"][i] == "V":
                vts(out, od, 1.0, ALU.min, None, None, ["Qo" + s], ["po%d_%d" % (i, h)], c=m // 4)
            else:
                sact(out, od, ACT.Sign, ["Qo" + s], ["po%d_%d" % (i, h)], c=m // 2)

    def upl(b):
        n, lo, w = "pU%d" % (b % 2), 64 * sum(len(x) for x in HASHED[b % 2:b:2]), 64 * len(HASHED[b])
        return n, T[n][:, lo:lo + w], slice(64 * HASHED[b][0], 64 * HASHED[b][0] + w)

    def hashes(b, t):
        (n, o, a), s, cs = upl(b), str(b), HASHED[b]
        w = 64 * len(cs)

        def rows(buf, k):
            return buf[:, 16 * a.start + k:16 * a.stop:16]

        def of(name):
            return ["%s%d" % (name, i) for i in cs]

        mms = [(o, T.cU[:], T.ones[:, 0:w], True, False)]
        for k in range(0, 16, 2):
            mms += [(o, sel("Wn", k), rows(T.Qb, k), False, False), (o, sel("W2", k), rows(T.Bb, k), False, False)]
        group(mms, ["cU", "ones", "Wn", "W2"] + of("Qe") + [x for i in cs for x in parts("Be", i)], [n, "u" + s], [n], w)
        group([(o, sel("Wp", k), rows(T.Qb, k), False, k == 15) for k in range(1, 16, 2)], ["Wp"] + of("Qo"), [n, "u" + s], [n], w)
        if OPT["cc"][cs[0]] == "V":
            vts(T.cc[:, a], o, -2047.5, ALU.add, None, None, ["u" + s], ["cc" + s], [n], w)
        else:
            sact(T.cc[:, a], o, ACT.Copy, ["u" + s], ["cc" + s], [n], bias=-2047.5, c=w)
        vtt(o, o, T.cc[:, a], ALU.subtract, ["u" + s, "cc" + s], ["u" + s], [n], w)
        ek = T.pE[:, a] if t == 0 else T.pE[:, 256 + a.start:256 + a.stop]
        vtt(T.eu[:, a], o, T.E[:, a], ALU.mult, ["u" + s, "E%d" % (cs[0] // 2)], ["eu" + s], [n], w)
        vts(T.wv[:, a], T.eu[:, a], 5, ALU.arith_shift_right, 4095, ALU.bitwise_and, ["eu" + s], ["wv" + s], c=w)
        vtt(T.hs[:, a], ek, T.wv[:, a], ALU.add, ["wv" + s, "Ek"] + of("E8_"), ["hs" + s], ["pE"], w)
        vts(T.hm[:, a], T.hs[:, a], 4095 + NOFF, ALU.bitwise_and, None, None, ["hs" + s], of("hm"), c=w)
        vcp(T.LY[:, a], T.hm[:, a], of("hm"), of("LY"), c=w)

    def region(i, j, whole=False):
        b = [i in x for x in BLOCKS].index(True)
        n, w = "pA" if b % 2 == 0 else "pB", len(BLOCKS[b])
        lo = j * w + (0 if whole else i - BLOCKS[b][0]) + (4 if b >= 2 else 0)
        hi = lo + (w if whole else 1)
        return n, T[n][:, 64 * lo:64 * hi], ["%s_%d" % (n, x) for x in range(lo, hi)]

    def scores(i):
        s, lo, names = str(i), 64 * i, []
        for n_acc, who, sign in PIECES[i]:
            c, m = slice(16 * lo, 16 * (lo + n_acc)), 16 * n_acc
            z, sg = "z%d" % lo, "s%d" % lo
            names.append(sg)
            src = T.XT[:, 0:GW].indirect(T.LY[:, lo:lo + n_acc])
            if who == "V":
                vtt(T.zb[:, c], src, T.Qb[:, c], ALU.subtract, ["LY" + s, "Qe" + s, "Qo" + s] + XALL, [z], c=gat(m))
                if sign == "V":
                    vts(T.sb[:, c], T.zb[:, c], -1.0, ALU.max, 1.0, ALU.min, [z], [sg], c=m // 2)
                else:
                    sact(T.sb[:, c], T.zb[:, c], ACT.Sign, [z], [sg], c=m)
            else:
                sact(T.zb[:, c], src, ACT.Copy, ["LY" + s] + XALL, [z], scale=-1.0, c=gat(m))
                n = "pY%d" % (turn[0] % 2)
                turn[0] += 1
                o = T[n][:, 0:m]
                group([(o, T.identB[:], T.Qb[:, c], True, False)], ["identB", "Qe" + s, "Qo" + s], [n], [n], m)
                group([(o, T.identB[:], T.zb[:, c], False, True)], ["identB", z], [n], [n], m)
                sact(T.sb[:, c], o, ACT.Sign, [n], [sg], [n], scale=-1.0, c=m)
            lo += n_acc
        n, o, w = region(i, 0)
        group([(o, sel("On", k), line(T.sb, i, k), k == 0, k == 15) for k in range(16)], ["On"] + names, w, [n])

    def counts(b):
        n, s, c = "pZ", str(b), slice(128 * b, 128 * b + 128)
        group([(T[n][:, 256 + k:384:16], (T.po if k % 2 else T.pe)[:, b * 1024 + k // 2:(b + 1) * 1024:8], T.On[:, 15:143:16], True, True)
               for k in range(16)], ["On"] + [x for i in (2 * b, 2 * b + 1) for x in parts("pe", i) + parts("po", i)], ["cnt"], [n])
        sact(T.ovT[:, c], T[n][:, 256:384], ACT.Sign, ["cnt"], ["ovT" + s], [n], bias=-8.5, c=128)
        group([(T[n][:, 384:512], T.ones[:, 0:128], T.identB[:], True, False), (T[n][:, 384:512], T.ovT[:, c], T.identB[:], False, True)],
              ["ones", "identB", "ovT" + s], ["ov"], [n], 128)
        vtt(T.ts[:, c], T[n][:, 384:512], T.sg[:, c], ALU.mult, ["ov", "sg"], ["gov" + s], [n], 128)

    def decide(b):
        i, w = BLOCKS[b][0], 64 * len(BLOCKS[b])
        a, s, ones = slice(64 * i, 64 * i + w), str(b), T.ones[:, 0:w]
        (n, score, nS), (_, total, nT), (_, ln, nL) = [region(i, j, True) for j in (0, 0, 1)]
        won, short = ["win%d" % x for x in BLOCKS[b]], b in SHORT
        vtt(T.comp[:, a], score, T.ts[:, a], ALU.mult, nS + ["gov%d" % (x // 2) for x in BLOCKS[b]], ["comp" + s], [n], w)
        sact(T.val[:, a], T.comp[:, a], ACT.Exp, ["comp" + s, "bk"], ["val" + s], bias=col("bk"), scale=16 * 17 * LAM, c=w)
        group([(total, T.cPh[:], ones, True, False)], ["cPh", "ones"], nT, [n], w)
        group([(total, T.blkT[:], T.val[:, a], False, True)], ["blkT", "val" + s], nT, [n], w)
        vtt(T.win[:, a], total, T.val[:, a], ALU.is_lt, nT + ["val" + s], won, [n], w)
        for x, cs in enumerate(HASHED):
            if cs[0] in BLOCKS[b]:
                m, u, c = upl(x)
                if short:
                    sact(u, u, ACT.Copy, ["u%d" % x], ["u%d" % x], [m], bias=-2048.0, c=64 * len(cs))
                vtt((T.wh if short else T.wu)[:, c], u, T.win[:, c], ALU.mult, ["u%d" % x] + won, ["wu%d" % y for y in cs], [m],
                    64 * len(cs))
        vscan(T.cum[:, a], T.win[:, a], T.zero[:, 0:w], T.cum[:, 64 * i - 1:64 * i] if b else 0.0, ALU.add, ALU.add,
              won + ["zero"] + (["cum%d" % (b - 1)] if b else []), ["cum" + s])
        group([(ln, T.ones[:, 0:128], T.arow[:, a], True, False), (ln, (T.kmat2 if short else T.kmat)[:], T.win[:, a], False, False)],
              ["ones", "arow", "kmat", "kmat2"] + won, nL, [n], w)
        group([(ln, T.blkH[:], T.wh[:, a], False, True) if short else (ln, T.blkF[:], T.wu[:, a], False, True)],
              ["blkF", "blkH"] + ["wu%d" % x for x in BLOCKS[b]], nL, [n], w, 0 if short else 1)
        who = PLACES[b]
        if "V" in who:
            group([(T.pY0[:, a], T.blkB[:], T.cum[:, a], True, True)], ["blkB", "cum" + s], ["pY0"], ["pY0"], w)
        if "S" in who:
            group([(T.pZ[:, a], T.blkB[:], T.cum[:, a], True, True)], ["blkB", "cum" + s], ["pZ" + s], ["pZ"], w)
        for j in range(4):
            o = 256 * j + 64 * i
            if who[j] == "V":
                vts(T.Pn[:, o:o + w], T.pY0[:, a], T.jB[:, j:j + 1], ALU.add, None, None, ["pY0", "jB"], ["Pn%d%s" % (j, s)], ["pY0"], w)
            else:
                sact(T.Pn[:, o:o + w], T.pZ[:, a], ACT.Identity, ["pZ" + s, "jB"], ["Pn%d%s" % (j, s)], ["pZ"], bias=T.jB[:, j:j + 1], c=w)
            vscan(T.F[:, o:o + w], ln, T.Pn[:, o:o + w], T.F[:, o - 1:o] if b else BIG, ALU.min, ALU.max,
                  nL + ["Pn%d%s" % (j, s), "F%d" % j], ["F%d" % j], w, [n])

    def send(t):
        FF, qs, found = ["F%d" % j for j in range(4)], T["qs%d" % t], T.F[:, 255:1024:256]
        vts(T.Li[:], found, -2047.5, ALU.add, 1.0 / 4096, ALU.mult, FF, ["Li"])
        vts(T.Fi[:], found, BIG / 2, ALU.min, None, None, FF, ["Fi"])
        vts(T.LJ[:], T.Li[:], 2048.0, ALU.add, 4096.0, ALU.min, ["Li"], ["LJ"])
        sact(qs[:, 0:64], T.Qb[:].indirect(T.LJ[:, 0:4]), ACT.Abs, ["LJ", "Qx"] + ["Q%s%d" % (x, i) for x in "eo" for i in range(4)],
             ["qs%d" % t], c=gat(64))
        vts(T.inv[:], found, BIG / 2, ALU.is_ge, float(SP), ALU.mult, FF, ["inv"])
        vts(T.um[:], T.Fi[:], 63, ALU.bitwise_and, None, None, ["Fi"], ["um"])
        vtt(T.cb[:], T.inv[:], T.c64[:], ALU.add, ["inv", "c64"], ["cb"])
        vtt(qs[:, 64:68], T.um[:], T.cb[:], ALU.add, ["um", "cb"], ["qi%d" % t])
        calls.append(("G", 300, FLIGHT, ["qs%d" % t, "qi%d" % t], ["land%d" % t], (), ("send", t)))

    def update(b):
        c, s = slice(128 * b, 128 * b + 128), str(b)
        e8, won = E8[2 * b:2 * b + 2], ["win%d" % i for i in (2 * b, 2 * b + 1)]
        vtt(T.pE[:, c], T.hm[:, c], T.pE[:, c], ALU.subtract, e8 + ["hm%d" % i for i in (2 * b, 2 * b + 1)], e8, ["pE"], 128)
        vtt(T.wE[:, c], T.pE[:, c], T.win[:, c], ALU.mult, e8 + won, ["wE" + s], ["pE"], 128)
        vtt(T.mB[:, c], T.mB[:, c], T.win[:, c], ALU.not_equal, ["mB" + s] + won, ["mB" + s], c=256)
        vtt(T.E[:, c], T.E[:, c], T.wE[:, c], ALU.add, ["E" + s, "wE" + s], ["E" + s], c=256)

    def kappa():
        group([(T.pU0[:, 256:257], T.ones[:, 0:128], T.cum[:, 255:256], True, True)], ["ones", "cum%d" % (len(BLOCKS) - 1)], ["pU0", "kp"], ["pU0"])
        vcp(T.kri[:], T.pU0[:, 256:257], ["kp"], ["kri"], ["pU0"])
        vts(T.krm[:], T.kri[:], 31, ALU.bitwise_and, None, None, ["kri"], ["krm"])
        vcp(T.kap[:], T.krm[:], ["krm"], ["kap"])
        sact(T.pE[:, 256:512], T.pE[:, 0:256], ACT.Identity, ["kap"] + E8, ["Ek"], ["pE"], bias=col("kap"), c=256)

    def arrive(t, last):
        ln = "land%d" % t
        vts(T.LI[:], T[ln][:, 64:68], col("k256"), ALU.add, None, None, [ln, "k256"], ["LI"])
        vtt(T.tx[:], T.XT[:, 0:AW].indirect(T.LI[:, 0:4]), T[ln][:, 0:64], ALU.add, ["LI", ln] + XP, ["tx"], c=gat(64))
        vts(T.ND[:, 0:64], T.tx[:], 0.5, ALU.mult, -0.25, ALU.add, ["tx"], ["ND0"])
        vcp(T.XT[:, 0:AW].indirect(T.LI[:, 0:4]), T.ND[:, 0:64], ["LI", "ND0"], XP, c=60 + 64 * SCATTER)
        if not last:
            calls[-1] = calls[-1][:2] + (calls[-1][2] + WAKE,) + calls[-1][3:]
            vts(T.ND[:, 64:128], T.tx[:], -0.5, ALU.mult, 0.25, ALU.add, ["tx"], ["ND1"])
            vcp(T.XT[:, NOFF:WEND].indirect(T.LI[:, 0:4]), T.ND[:, 64:128], ["LI", "ND1"], NP, c=60 + 64 * SCATTER)

    for t in range(rounds):
        last = t == rounds - 1
        for i in range(4):
            amounts(i)
            for b, chunks in enumerate(HASHED):
                if chunks[-1] == i:
                    hashes(b, t)
            if i % 2:
                counts(i // 2)
        for i in range(4):
            scores(i)
        for b in range(len(BLOCKS)):
            decide(b)
        for b in range(2):
            update(b)
        send(t)
        if last:
            dma("S", T.yl[:], T.E[:], EE + ["land%d" % t], ["yl"], LOAD)
            dma("S", T.ym[:], T.mB[:], MM + ["land%d" % t], ["ym"], LOAD)
        else:
            lists()
            kappa()
        arrive(t, last)
        if not last:
            ends.append(len(calls))
    dma("Y", T.yx[:], T.XT[:, 0:4096], XP, ["yx"], LOAD + 4000)

    count = {}
    known = {q: {} for q in Q}
    lastw, readers, banks = {}, {}, {}
    n_dma = 0
    if not ORDER:
        for lo, hi in zip([0] + ends, ends + [len(calls)]):
            ORDER.extend(lo + i for i in in_order(calls[lo:hi]))
    for seq, i in enumerate(ORDER):
        q, _, _, R, W, B, f = calls[i]
        toks = [lastw[x] for x in list(R) + list(W) if x in lastw]
        toks += [y for x in W for y in readers.get(x, [])]
        toks += [y for b in B for qq, y in banks.get(b, {}).items() if qq != q]
        if q == "P":
            toks = [y for y in toks if y[2] != q]
        k = known[q]
        for sem, val, _, snap, _ in sorted(toks, key=lambda y: -y[4]):
            if k.get(sem, 0) < val:
                Q[q].wait_ge(T.sem[sem], val)
                for s, v in list(snap.items()) + [(sem, val)]:
                    k[s] = max(k.get(s, 0), v)
        snap = dict(k)
        if isinstance(f, tuple) and f[0] == "send":
            t = f[1]
            step = 1 + t % (n_ranks - 1)
            dst, src = T.cores[(rank + step) % n_ranks], T.cores[(rank - step) % n_ranks]
            rid, pid, _ = topo.addr(dst)
            eng = topo.engines(core, dst)[:NENG]
            g.remote_dma(T["land%d" % t][:], T["qs%d" % t][:], T.sem["arr%d" % t], T.sem.sent, pid, rid, sum(1 << e for e in eng))
            count["sent"] = count.get("sent", 0) + len(eng)
            q, sem, n, R, snap = "R", "arr%d" % t, len(topo.engines(src, core)[:NENG]), [], {}
        elif isinstance(f, tuple):
            sem, n = "d%d" % n_dma, 16
            n_dma += 1
            Q[q].dma_start(f[1], f[2]).then_inc(T.sem[sem], n)
        else:
            sem, n = "c" + q, 1
            f().then_inc(T.sem[sem], n)
        count[sem] = count.get(sem, 0) + n
        tok = (sem, count[sem], q, snap, seq)
        for x in R:
            readers.setdefault(x, []).append(tok)
        for x in W:
            lastw[x], readers[x] = tok, []
        for b in B:
            banks.setdefault(b, {})[q] = tok
    for sem, n in count.items():
        if known["G"].get(sem, 0) < n:
            g.wait_ge(T.sem[sem], n)
